import numpy as np, ml_dtypes
CORES = [35,38,43,46]
N = 4
BF = ml_dtypes.bfloat16
def gentries(a):
    return np.ascontiguousarray(a.reshape(8, 16, -1).transpose(0, 2, 1)).reshape(8, -1)
def gtable(e):
    e = np.asarray(e); return np.ascontiguousarray(e.reshape(8, -1, 16).transpose(0, 2, 1)).reshape(128, -1).astype(np.int32)
W, L, T, TH, A, B, FO = 4096, 256, 8, 60, 4, 10, 8
def parts(rng):
    return (rng.integers(0, 16, (N, 8, 16, W)), rng.integers(0, W, (N, 8, 16, W)), rng.integers(0, 64, (N, 8, 16, L)), rng.integers(0, W, (N, 8, 16, L)),
            rng.integers(0, W, (N, 8, 16, L)), rng.integers(0, 16, (N, 8, 16, L)), rng.integers(0, W, (N, 8, L)), rng.integers(0, 64, (N, 8, 16)))
def keys(x, w, p):
    z = np.take_along_axis(x, p[:, :, None, :], 3)
    return np.add.reduce(z * w[..., None], axis=2) & 63
def pack(x, d, m, u, n, q, o, w):
    return {"feat": np.ascontiguousarray(x.reshape(N, 128, W)).astype(np.float32).astype(BF), "kids": np.ascontiguousarray(d.reshape(N, 128, W)).astype(np.int32),
            "mkey": np.ascontiguousarray(m.reshape(N, 128, L)).astype(np.float32).astype(BF), "mobj": np.ascontiguousarray(u.reshape(N, 128, L)).astype(np.int32),
            "cand": np.stack([gtable(a.transpose(0, 2, 1).reshape(8, -1)) for a in n]), "want": np.ascontiguousarray(q.reshape(N, 128, L)).astype(np.float32).astype(BF),
            "last": np.ascontiguousarray(o).astype(np.int32), "wts": np.ascontiguousarray(w.reshape(N, 128, 1)).astype(np.int32)}
def setup_inputs(rng):
    return pack(*parts(rng))
def setup_inputs_corners(rng):
    x, d, m, u, n, q, o, w = parts(rng); own = np.arange(W)[None, None, None, :]
    kind = rng.integers(0, 7, (N, 8, 1, W))
    d = np.where(kind == 0, own, d); d = np.where(kind == 1, (own + 1) % W, d)
    d = np.where(kind == 2, (W - 1) * rng.integers(0, 2, d.shape), d); d = np.where(kind == 3, d[:, :, :1, :], d)
    d[2] = d[2] & -2
    x[3, :, 0] = (x[3, :, 0] & 14) | (own[0, 0] & 1); w[3] = w[3] & 62; w[3, :, 0] = w[3, :, 0] | 1
    p = rng.integers(0, W, (N, 8, L)); p[1] = 1 + np.argsort(rng.random((8, W - 2)), axis=1)[:, :L]
    p[:, :, 0] = 0; p[:, :, L - 1] = W - 1; p[3] = p[3] | 1
    n0 = n[0]; n = np.repeat(p[:, :, None, :], 16, axis=2); n[0] = np.where(rng.random((8, 1, L)) < 0.5, n0, n[0])
    j = rng.choice(np.array([0, A - 1, A, B - 1, B, 15, 16]), (N, 8, L))
    j[1] = np.where(j[1] == 16, 15, j[1]); j[2] = 16; j[3] = np.where(j[3] == 16, 0, j[3]); j[3, 7, L - 1] = 16
    c = keys(x, w, p)[:, :, None, :]; rows = np.arange(16)[None, None, :, None]; jj = j[:, :, None, :]
    off = rng.integers(1, 64, m.shape); off[3] = 2 * rng.integers(1, 32, off[3].shape)
    m = np.where((rows == jj) | ((rows > jj) & (rng.random(m.shape) < 0.2)), c, (c + off) & 63)
    m[1, :, :, 1] = c[1, :, :, 1]
    s = rng.integers(0, 5, u.shape); u = np.where(s == 0, 0, np.where(s == 1, W - 1, np.where(s == 2, p[:, :, None, :], u)))
    s = rng.integers(0, 4, o.shape); o = np.where(s == 0, 0, np.where(s == 1, W - 1, np.where(s == 2, p, o)))
    u[1, :, :, 1] = rng.integers(1, W - 1, (8, 16)); u[1, :, :, L - 1] = rng.integers(1, W - 1, (8, 16))
    z = np.take_along_axis(x[1], p[1][:, None, :], 2)
    q[1, 6] = z[6]; q[1, 7] = np.where(z[7] >= 8, 0, 15); u[1, 6, 0, 0] = W - 1; o[1, 6, 0] = 0
    return pack(x, d, m, u, n, q, o, w)
def setup_inputs_ends(rng):
    x, d, m, u, n, q, o, w = parts(rng)
    x = 15 * (rng.random((N, 8, 16, W)) < rng.choice(np.array([0.0, 0.3, 0.5, 0.5, 0.7, 1.0]), (N, 8, 1, W))).astype(np.int64)
    for g in range(8):
        x[:, g, :, 0] = 15 * (g & 1); x[:, g, :, W - 1] = 15 * (g & 1)
        x[:, g, :, W - 2] = 15 * (g & 1); x[:, g, 15, W - 2] = 15 - 15 * (g & 1)
    w = 63 * rng.integers(0, 2, w.shape); w[:, 6:] = 63; w[:, 0] = 0
    q = 15 * rng.integers(0, 2, q.shape)
    d = np.where(rng.random(d.shape) < 0.7, (W - 1) * rng.integers(0, 2, d.shape), d)
    n = np.where(rng.random(n.shape) < 0.7, (W - 1) * rng.integers(0, 2, n.shape), n)
    u = np.where(rng.random(u.shape) < 0.7, (W - 1) * rng.integers(0, 2, u.shape), u)
    o = np.where(rng.random(o.shape) < 0.75, (W - 1) * rng.integers(0, 2, o.shape), o)
    m = np.where(rng.random(m.shape) < 0.7, 63 * rng.integers(0, 2, m.shape), (49 * rng.integers(0, 17, m.shape)) & 63)
    for l in (0, 1, 2, 3, L - 4, L - 3, L - 2, L - 1): n[:, :, 0::2, l] = W - 1; n[:, :, 1::2, l] = 0
    for l, k in ((2, 1), (3, 13), (L - 4, 1), (L - 3, 13)): n[:, :, k, l] = W - 2; n[:, :, 14, l] = W - 2
    for g in range(8):
        for l in (1, 2, 3, L - 4, L - 3, L - 1): q[:, g, :, l] = 15 - 15 * (g & 1)
        for l in (0, L - 2): q[:, g, :, l] = 15 * (g & 1)
    kk = keys(x, w, np.full((N, 8, 1), W - 1))
    m[:, :, 12:, L - 1] = 63; u[:, :, 12:, L - 1] = W - 1
    m[:, :, 11, 1] = kk[:, :, 0]; m[:, :, 11, L - 1] = kk[:, :, 0]
    h = W // FO
    d[:, 7, 15, h - 1::h] = W - 1; d[:, 7, 15, h - 2::h] = W - 1; d[:, :, 0, 0::h] = 0
    return pack(x, d, m, u, n, q, o, w)
def setup_inputs_shared(rng):
    x, d, m, u, n, q, o, w = parts(rng)
    hot = np.stack([np.concatenate([np.array([0, W - 1]), 1 + rng.permutation(W - 2)[:22]]) for g in range(8)])
    gg = np.arange(8)[None, :, None, None]
    d = hot[gg, rng.integers(0, 24, d.shape)]; n = hot[gg, rng.integers(0, 24, n.shape)]
    u = np.where(rng.random(u.shape) < 0.5, hot[gg, rng.integers(0, 24, u.shape)], u)
    kh = keys(x, w, np.repeat(hot[None], N, axis=0))
    m = np.where(rng.random(m.shape) < 0.6, kh[np.arange(N)[:, None, None, None], gg, rng.integers(0, 24, m.shape)], m)
    for r, g, i in ((0, 0, 2), (N - 1, 7, 1)):
        n[r, g] = hot[g, i]; m[r, g, 0] = kh[r, g, i]; u[r, g, 0, 0] = hot[g, 3]
    return pack(x, d, m, u, n, q, o, w)
def setup_inputs_spread(rng):
    x, d, m, u, n, q, o, w = parts(rng)
    def uneven(top, shape, kshape):
        return np.minimum((top * rng.random(shape) ** np.exp2(rng.integers(-2, 3, kshape))).astype(np.int64), top - 1)
    x = uneven(16, x.shape, (N, 8, 1, W)); q = uneven(16, q.shape, (N, 8, 1, L)); d = uneven(W, d.shape, (N, 8, 16, 1))
    u = uneven(W, u.shape, (N, 8, 1, L)); n = uneven(W, n.shape, (N, 8, 16, 1)); o = uneven(W, o.shape, (N, 8, 1)); w = uneven(64, w.shape, (N, 8, 1))
    m = m & rng.choice(np.array([63, 63, 7, 56, 1]), (N, 8, 1, L))
    return pack(x, d, m, u, n, q, o, w)
def setup_inputs_ties(rng):
    x, d, m, u, n, q, o, w = parts(rng); h = W // 2
    x[..., h:] = x[..., :h][..., ::-1]
    p = rng.integers(0, W, (N, 8, L)); p[:, :, L - 1] = W - 1
    z = np.take_along_axis(x, p[:, :, None, :], 3); tot = TH + rng.integers(-1, 2, (N, 8, 1, L))
    dl = (tot >> 4) + (np.arange(16)[None, None, :, None] < (tot & 15))
    q = np.where(z >= 8, z - dl, z + dl)
    twin = np.where(rng.random(n.shape) < 0.5, p[:, :, None, :], W - 1 - p[:, :, None, :])
    n = np.where(rng.random(n.shape) < 0.6, twin, n)
    c = keys(x, w, p)[:, :, None, :]
    m = np.where(rng.random((N, 8, 1, L)) < 0.4, (c + (m & 3)) & 63, m)
    return pack(x, d, m, u, n, q, o, w)
def check_inputs(d):
    bad = []
    for k, lo, hi in (("feat", 0, 15), ("kids", 0, W - 1), ("mkey", 0, 63), ("mobj", 0, W - 1), ("cand", 0, W - 1), ("want", 0, 15), ("last", 0, W - 1), ("wts", 0, 63)):
        v = np.asarray(d[k]).astype(np.float64)
        if not (np.min(v) >= lo and np.max(v) <= hi and np.all(v == np.rint(v))): bad.append("range of " + k)
    return bad
def reference(feat, kids, mkey, mobj, cand, want, last, wts):
    x = np.ascontiguousarray(feat.astype(np.int32).reshape(N, 8, 16, W).transpose(0, 1, 3, 2))
    d = np.array(kids.astype(np.int64).reshape(N, 8, 16, W).transpose(0, 1, 3, 2))
    m = np.array(mkey.astype(np.int64).reshape(N, 8, 16, L).transpose(0, 1, 3, 2))
    u = np.array(mobj.astype(np.int64).reshape(N, 8, 16, L).transpose(0, 1, 3, 2))
    n = np.stack([gentries(a) for a in cand]).astype(np.int64).reshape(N, 8, L, 16)
    q = np.array(want.astype(np.int32).reshape(N, 8, 16, L).transpose(0, 1, 3, 2))
    prev = np.array(last.astype(np.int64)); w = wts.astype(np.int64).reshape(N, 8, 1, 16)
    count = np.zeros(N, np.int64); gi = np.arange(8)[:, None]
    for t in range(T):
        seen = np.zeros(N, np.int64)
        for r in range(N):
            s = (r + t) % N
            dist = np.add.reduce(np.abs(x[s][gi[:, :, None], n[r]] - q[r][:, :, None, :]), axis=3)
            like = dist < TH + (count[s] & 15); alike = np.any(like, axis=2)
            k = np.where(alike, np.argmax(like, axis=2), np.argmin(dist, axis=2))
            o = np.take_along_axis(n[r], k[:, :, None], 2)[:, :, 0]
            xo = x[s][gi, o]; c = np.add.reduce(xo * w[s], axis=2) & 63
            hit = m[s] == c[:, :, None]; covered = np.any(hit, axis=2); j = np.argmax(hit, axis=2)
            own = d[s][gi, o]; e = d[s][gi, np.take_along_axis(u[s], j[:, :, None], 2)[:, :, 0]]
            top = covered & (j < B); low = covered & ((j < A) | (j >= B))
            new = np.concatenate([np.where(top[:, :, None], e[:, :, :8], own[:, :, :8]), np.where(low[:, :, None], e[:, :, 8:], own[:, :, 8:])], axis=2)
            g, l = np.nonzero(covered); first = np.unique(g * W + o[g, l], return_index=True)[1]
            g, l = g[first], l[first]; d[s, g, o[g, l]] = new[g, l]
            g, l = np.nonzero(~alike); row = (l + 5 * t) & 15
            m[s, g, l, row] = c[g, l]; u[s, g, l, row] = prev[r, g, l]
            seen[s] = np.count_nonzero(covered); prev[r] = o; n[r] = new; q[r] = np.abs(q[r] - xo)
        count = seen
    dd = d.transpose(0, 1, 3, 2).reshape(N, 128, FO, W // FO)
    return {"yn": n.transpose(0, 1, 3, 2).reshape(N, 128, L).astype(np.float32), "ymu": (64 * u + m).transpose(0, 1, 3, 2).reshape(N, 128, L).astype(np.float32),
            "yd": np.add.reduce(dd * np.arange(1, FO + 1)[:, None], axis=2).astype(np.float32)}

@@ -1,0 +1,489 @@
+from concourse.mybir import AluOpType as ALU, AxisListType, ActivationFunctionType as AF
+
+STEPS, W, L, LIM = 8, 4096, 256, 60
+CH = [(0, 2), (2, 6), (6, 10), (10, 14)]
+OWN = 14
+XF = 1
+KD, KG = 6, 3
+NT = 6
+BIG = float(2 ** 26)
+
+_f, _b, _h, _i, _u = "float32", "bfloat16", "float16", "int32", "uint16"
+SCRATCH = {
+    "featW": ("sbuf", [128, 2 * W], _b), "kidi": ("sbuf", [128, W], _i), "kid": ("sbuf", [128, W + 16], _f),
+    "keyW": ("sbuf", [128, W], _f), "idW": ("sbuf", [128, W + 16], _f),
+    "Wx": ("sbuf", [128, W], _b), "D": ("sbuf", [128, W], _b), "A": ("sbuf", [128, 16, 256], _b), "raw": ("sbuf", [128, 512], _b),
+    "LH": ("sbuf", [128, 2048], _b), "SH": ("sbuf", [128, 2048], _h), "R16": ("sbuf", [128, 8, 32], _h),
+    "i1": ("sbuf", [128, 128], _i), "i1b": ("sbuf", [128, 128], _i), "i2": ("sbuf", [128, 16], _i), "i2b": ("sbuf", [128, 16], _i),
+    "i3": ("sbuf", [128, 16], _i), "i3b": ("sbuf", [128, 16], _i), "i4": ("sbuf", [128, 16], _i), "i5": ("sbuf", [128, 16], _i), "i6": ("sbuf", [128, 16], _i),
+    "bi": ("sbuf", [128, 16], _i), "exb": ("sbuf", [128, 16], _u), "dg": ("sbuf", [128, 16], _f), "ib": ("sbuf", [128, 8], _i),
+    "a1": ("sbuf", [128, 16], _f), "a2": ("sbuf", [128, 16], _f), "a3": ("sbuf", [128, 16], _f), "a4": ("sbuf", [128, 16], _f),
+    "blk": ("sbuf", [128, 128], _f), "diag": ("sbuf", [128, 256], _f), "I16": ("sbuf", [128, 128], _h), "IB": ("sbuf", [128, 128], _b),
+    "IN": ("sbuf", [128, 128], _b), "If": ("sbuf", [128, 128], _f), "ones": ("sbuf", [128, 128], _b), "wblk": ("sbuf", [128, 128], _b),
+    "b8": ("sbuf", [128, 8], _b), "Kc": ("sbuf", [128, 256], _b), "expl": ("sbuf", [128, 16], _u),
+    "RST": ("sbuf", [128, 256], _f), "RZ": ("sbuf", [128, 256], _f), "R1": ("sbuf", [128, 256], _f), "R2": ("sbuf", [128, 256], _f),
+    "CJ": ("sbuf", [128, 16], _f), "CJ2": ("sbuf", [128, 256], _f),
+    "col": ("sbuf", [128, 16], _f), "offc": ("sbuf", [128, 16], _f), "wti": ("sbuf", [128, 1], _i), "wtf": ("sbuf", [128, 1], _f),
+    "ci": ("sbuf", [128, 256], _i), "mkb": ("sbuf", [128, 256], _b), "moi": ("sbuf", [128, 256], _i), "mk16": ("sbuf", [128, 256], _h), "mo16": ("sbuf", [128, 256], _h),
+    "lai": ("sbuf", [128, 16], _i), "LX": ("sbuf", [128, 32], _f), "LT": ("sbuf", [128, 32], _f), "prev0": ("sbuf", [128, 16], _f),
+    "X": ("sbuf", [128, 16, 32], _h), "XT": ("sbuf", [128, 16, 32], _h), "Y": ("sbuf", [128, 16, 32], _h), "YT": ("sbuf", [128, 16, 32], _h),
+    "G": ("sbuf", [128, 8, 32], _h), "GT": ("sbuf", [128, 8, 32], _h), "PM": ("sbuf", [128, 512], _h), "S4": ("sbuf", [128, 4, 2, 16], _h),
+    "MK": ("sbuf", [128, 256], _f), "Lp": ("sbuf", [128, 256], _f), "vm": ("sbuf", [128, 256], _f), "vI": ("sbuf", [128, 256], _i),
+    "oa": ("sbuf", [128, 16], _i), "kk": ("sbuf", [128, 16], _i), "po": ("sbuf", [128, 16], _i), "pb": ("sbuf", [128, 16], _i), "pbb": ("sbuf", [128, 16], _i), "pu": ("sbuf", [128, 16], _u),
+    "ky": ("sbuf", [128, 256], _f), "ks": ("sbuf", [128, 256], _i), "key": ("sbuf", [128, 16], _i),
+    "eq": ("sbuf", [128, 256], _f), "em": ("sbuf", [128, 256], _f), "es": ("sbuf", [128, 256], _i),
+    "eo": ("sbuf", [128, 16], _i), "sT": ("sbuf", [128, 16], _i), "sL": ("sbuf", [128, 16], _i), "de": ("sbuf", [128, 16], _i),
+    "tT": ("sbuf", [128, 16], _i), "tL": ("sbuf", [128, 16], _i), "l2": ("sbuf", [128, 32], _i), "u2": ("sbuf", [128, 32], _u),
+    "top": ("sbuf", [128, 256], _f), "cf": ("sbuf", [128, 256], _f),
+    "na": ("sbuf", [128, 16], _f), "cov": ("sbuf", [128, 16], _b), "ncd": ("sbuf", [128, 16], _f), "s1": ("sbuf", [128, 16], _f), "s1u": ("sbuf", [128, 16], _u),
+    "gl": ("sbuf", [128, 256], _f), "eq2": ("sbuf", [128, 256], _f), "dsum": ("sbuf", [128, 256], _f), "dd": ("sbuf", [128, 16], _f), "s2": ("sbuf", [128, 16], _f), "s2u": ("sbuf", [128, 32], _u),
+    "dk": ("sbuf", [128, 16], _f), "dk2": ("sbuf", [128, 16], _f), "pn": ("sbuf", [128, 16], _f), "dn": ("sbuf", [128, 16], _f), "dn2": ("sbuf", [128, 16], _f),
+    "cs": ("sbuf", [128, 1], _f), "csi": ("sbuf", [128, 1], _i), "csa": ("sbuf", [128, 1], _i), "limA": ("sbuf", [128, 1], _f),
+    "yno": ("sbuf", [128, 256], _f), "ymo": ("sbuf", [128, 256], _f), "acc": ("sbuf", [128, 512], _f),
+    "outC": ("sbuf", [128, STEPS * 272], _u), "inC": ("sbuf", [128, (STEPS + 1) * 272], _u),
+    "outW": ("sbuf", [128, STEPS * 256], _b), "inW": ("sbuf", [128, STEPS * 256], _b),
+    "pv": ("psum", [128, 8, 32], _f), "pL": ("psum", [128, 8, 32], _f), "pM": ("psum", [128, 512], _f), "pC": ("psum", [128, 512], _f),
+    "pW": ("psum", [128, 512], _f), "pA": ("psum", [128, 512], _f), "pB": ("psum", [128, 512], _f), "pX": ("psum", [128, 512], _f),
+}
+DMAS = ["cand", "want", "wts", "last", "mkey", "mobj", "f0", "fd", "k0", "k1", "k2", "k3", "yn", "ymu", "yd"]
+SEMAPHORES = ["sv", "st", "ss", "sg", "ls"] + ["d_" + n for n in DMAS] + ["w%d" % t for t in range(1, STEPS)] + [x + "%d" % t for t in range(1, STEPS + 1) for x in "ab"]
+
+
+def make(g, T):
+    Q = {"v": g.vector, "t": g.tensor, "s": g.scalar, "g": g, "y": g.sync}
+    own = {"v": "sv", "t": "st", "s": "ss", "g": "sg"}
+    cnt, known, hist, tags = {}, {q: {} for q in Q}, {}, {}
+
+    def tag(n):
+        if n not in tags:
+            tags[n] = {"w": {}, "r": {}, "base": {}, "full": False}
+        return tags[n]
+
+    def merge(a, b):
+        for s, c in b.items():
+            if a.get(s, 0) < c:
+                a[s] = c
+
+    def wait(q, needs):
+        for s in sorted(needs, key=lambda s: -len(hist.get((s, needs[s]), {}))):
+            c = needs[s]
+            if known[q].get(s, 0) < c:
+                Q[q].wait_ge(T.sem[s], c)
+                merge(known[q], hist.get((s, c), {}))
+                merge(known[q], {s: c})
+
+    def deps(q, r, w, p, acc):
+        need = {}
+        for n in r:
+            merge(need, tag(n)["w"])
+        for n in w:
+            d = tag(n)
+            for m in (d["w"], d["r"], d["base"]):
+                merge(need, {s: c for s, c in m.items() if not (acc and s == own.get(q))})
+        for n in p:
+            d = tag(n)
+            if d["full"] or d["r"]:
+                merge(d["base"], d["w"])
+                merge(d["base"], d["r"])
+                d["w"], d["r"], d["full"] = {}, {}, False
+            merge(need, d["base"])
+        return need
+
+    def mark(s, c, r, w, p, acc):
+        for n in r:
+            merge(tag(n)["r"], {s: c})
+        for n in w:
+            if acc:
+                merge(tag(n)["w"], {s: c})
+                tag(n)["r"] = {}
+            else:
+                tags[n] = {"w": {s: c}, "r": {}, "base": {}, "full": True}
+        for n in p:
+            merge(tag(n)["w"], {s: c})
+
+    def op(q, fn, args, r=(), w=(), p=(), acc=False, kw=None):
+        wait(q, deps(q, r, w, p, acc))
+        s = own[q]
+        cnt[s] = c = cnt.get(s, 0) + 1
+        fn(*args, **(kw or {})).then_inc(T.sem[s], 1)
+        hist[(s, c)] = dict(known[q])
+        mark(s, c, r, w, p, acc)
+
+    def dma(q, out, in_, name, r=(), w=(), p=()):
+        wait(q, deps(q, r, w, p, False))
+        s = "d_" + name
+        cnt[s] = 16
+        Q[q].dma_start(out, in_).then_inc(T.sem[s], 16)
+        hist[(s, 16)] = dict(known[q])
+        mark(s, 16, r, w, p, False)
+
+    def arrive(s, c, w):
+        cnt[s] = c
+        mark(s, c, (), w, (), False)
+
+    def need(q, r):
+        wait(q, deps(q, r, (), (), False))
+
+    def finish(q):
+        for s in sorted(cnt):
+            if known[q].get(s, 0) < cnt[s]:
+                Q[q].wait_ge(T.sem[s], cnt[s])
+    return op, dma, arrive, need, finish, cnt
+
+
+def rank_program(g, core, T, topo):
+    rank = T.rank_of(core)
+    if rank is None:
+        return
+    op, dma, arrive, need, finish, cnt = make(g, T)
+    v, te, sc = g.vector, g.tensor, g.scalar
+    n = len(T.cores)
+    nxt, prv = T.cores[(rank + 1) % n], T.cores[(rank - 1) % n]
+    rid, pid, _se = topo.addr(nxt)
+    mask, nout, nin = topo.mask(core, nxt), len(topo.engines(core, nxt)), len(topo.engines(prv, core))
+
+    def ts(out, in0, s1, s2, o0, o1, r, w=(), p=()):
+        args = (out, in0, s1, s2, o0) if o1 is None else (out, in0, s1, s2, o0, o1)
+        op("v", v.tensor_scalar, args, r, w, p)
+
+    def tt(out, a, b, o, r, w=(), p=()):
+        op("v", v.tensor_tensor, (out, a, b, o), r, w, p)
+
+    def cp(out, a, r, w=(), p=()):
+        op("v", v.tensor_copy, (out, a), r, w, p)
+
+    def scan(out, d0, d1, o0, o1, r, w):
+        op("v", v.tensor_tensor_scan, (out, d0, d1, 0.0, o0, o1), r, (w,))
+
+    def act(out, a, f, r, w=(), p=(), **kw):
+        op("s", sc.activation, (out, a, f), r, w, p, kw=kw)
+
+    def mm(out, l, rh, st, sp, r, w):
+        op("t", te.matmul, (out, l, rh, st, sp), r, (w,), acc=not st)
+
+    def send(out, in_, sem, r):
+        need("g", r)
+        g.remote_dma(out, in_, T.sem[sem], T.sem.ls, pid, rid, mask)
+        cnt["ls"] = cnt.get("ls", 0) + nout
+
+    def fill(ap, x, w=(), p=()):
+        op("v", v.memset, (ap, x), (), w, p)
+
+    def iota(out, pat, base, ch, w, **kw):
+        op("g", g.iota, (out, pat, base, ch), (), (w,), kw=kw)
+    C = lambda j: T.col[:, j:j + 1]
+    M1, M0, SCT, BIT, CEN, DUMP, THR, OFF, CEN0 = range(9)
+    inC = lambda t: T.inC[:, 272 * t:272 * t + 256]
+    inP = lambda t: T.inC[:, 272 * t + 256:272 * t + 272]
+    outO = lambda t: T.outC[:, 272 * t + 256:272 * t + 272]
+    inW = lambda t: T.inW[:, 256 * t:256 * t + 256]
+    outW = lambda t: T.outW[:, 256 * t:256 * t + 256]
+    last16 = lambda b: b[:, 15::16]
+
+    dma("s", T.ci[:], T.cand[:], "cand", w=("ci",))
+    dma("y", inW(0), T.want[:], "want", w=("inW0",))
+    dma("y", T.featW[:, 0:W], T.feat[:], "f0", w=("feat",))
+    dma("s", T.mkb[:], T.mkey[:], "mkey", w=("mkb",))
+    dma("s", T.moi[:], T.mobj[:], "mobj", w=("moi",))
+    dma("s", T.wti[:], T.wts[:], "wts", w=("wti",))
+    dma("s", T.lai[:], T.last[:], "last", w=("lai",))
+    for q in range(4):
+        dma("y", T.kidi[:, 1024 * q:1024 * q + 1024], T.kids[:, 1024 * q:1024 * q + 1024], "k%d" % q, w=("kidi%d" % q,))
+    dma("y", T.featW[:, W:2 * W], T.feat[:], "fd", w=("featd",))
+
+    iota(T.i5[:], [[0, 16]], 0, 1, "i5")
+    iota(T.i2[:], [[1, 16]], 128, -1, "i2")
+    iota(T.i1[:], [[16, 8], [0, 16]], 15, -1, "i1")
+    iota(T.i4[:], [[1, 16]], 0, 0, "i4")
+    iota(T.i3[:], [[1, 16]], 0, 1, "i3")
+    iota(T.i6[:], [[256, 16]], 0, 0, "i6")
+    iota(T.Kc[:], [[0, 16], [4096, 16]], 2048, 0, "Kc", allow_small_or_imprecise_dtypes=True)
+    iota(T.idW[:], [[1, W + 16]], 0, 0, "idW", allow_small_or_imprecise_dtypes=True)
+    fill(T.LH[:], 0.0, w=("LH",))
+    ts(T.i2b[:], T.i2[:], 15, None, ALU.bitwise_and, None, ("i2",), ("i2b",))
+    ts(T.bi[:], T.i5[:], 15, None, ALU.bitwise_and, None, ("i5",), ("bi",))
+    ts(T.i1b[:], T.i1[:], 4, None, ALU.arith_shift_right, None, ("i1",), ("i1b",))
+    ts(T.ib[:, 0:1], T.i5[:, 0:1], 4, 1, ALU.logical_shift_right, ALU.bitwise_and, ("i5",), ("ib0",))
+    ts(T.ib[:, 1:2], T.i5[:, 0:1], 3, 1, ALU.logical_shift_right, ALU.bitwise_and, ("i5",), ("ib1",))
+    ts(T.dg[:], T.i2b[:], 0.0, None, ALU.is_equal, None, ("i2b",), ("dg",))
+    cp(T.exb[:], T.bi[:], ("bi",), ("exb",))
+    ts(T.blk[:], T.i1b[:], 0.0, None, ALU.is_equal, None, ("i1b",), ("blk",))
+    act(T.diag[:], T.dg[:].indirect(T.exb[:]), AF.Copy, ("dg", "exb"), ("diag",))
+    ts(T.b8[:], T.blk[:, 0::16], 65536.0, None, ALU.mult, None, ("blk",), ("b8",))
+    cp(C(M1), T.ib[:, 0:1], ("ib0",), ("m1",))
+    ts(C(M0), T.ib[:, 0:1], -1.0, 1.0, ALU.mult, ALU.add, ("ib0",), ("m0",))
+    ts(C(SCT), T.ib[:, 1:2], -1.0, 1.0, ALU.mult, ALU.add, ("ib1",), ("sct",))
+    ts(C(DUMP), T.bi[:, 0:1], float(W), None, ALU.add, None, ("bi",), ("dump",))
+    fill(C(CEN0), 2048.0, w=("cen0",))
+    for b in range(16):
+        act(T.LH[:, 129 * b:129 * b + 113:16], T.b8[:], AF.Copy, ("b8",), p=("LH",))
+    tt(T.If[:], T.blk[:], T.diag[:, 0:128], ALU.mult, ("blk", "diag"), ("If",))
+    cp(T.inC[:, 0:256], T.ci[:], ("ci",), ("inCa0", "inCb0"))
+    cp(T.I16[:], T.If[:], ("If",), ("I16",))
+    cp(T.IB[:], T.If[:], ("If",), ("IB",))
+    ts(T.IN[:], T.If[:], -1.0, None, ALU.mult, None, ("If",), ("IN",))
+
+    def expand(t, q, k):
+        out, nm = T.Wx[:, k::16], "inW%d" % t
+        if q == "v":
+            cp(out, inW(t), (nm,), p=("Wx",))
+        elif q == "s":
+            act(out, inW(t), AF.Copy, (nm,), p=("Wx",))
+        else:
+            op("g", g.affine_select, (out, inW(t), [[0, 256]], ALU.is_equal, 0.0, 0, 0), (nm,), p=("Wx",))
+    for k in range(16):
+        expand(0, "v" if k < KD else "s", k)
+    cp(T.wtf[:], T.wti[:], ("wti",), ("wtf",))
+    ts(T.wblk[:], T.blk[:], T.wtf[:], None, ALU.mult, None, ("blk", "wtf"), ("wblk",))
+    fill(T.R1[:], 1.0, w=("R1",))
+    fill(T.R1[:, 0::16], 0.0, p=("R1",))
+    act(T.R2[:], T.R1[:], AF.Copy, ("R1",), ("R2",), scale=2.0)
+    act(T.RZ[:], T.R1[:], AF.Copy, ("R1",), ("RZ",), scale=BIG)
+    act(T.RST[:], T.R1[:], AF.Copy, ("R1",), ("RST",), scale=-BIG, bias=BIG)
+    ts(C(BIT), C(SCT), 4097.0, -1.0, ALU.mult, ALU.add, ("sct",), ("bit",))
+    ts(C(CEN), C(SCT), 4096.0, 2048.0, ALU.mult, ALU.add, ("sct",), ("cen",))
+    ts(C(OFF), C(SCT), 4096.0, None, ALU.mult, None, ("sct",), ("off",))
+    cp(T.expl[:], T.i4[:], ("i4",), ("expl",))
+    fill(T.limA[:], 65536.0 * (LIM - 1), w=("limA",))
+    ts(T.pbb[:], T.bi[:], 16.0, None, ALU.mult, None, ("bi",), ("pbb",))
+    ts(T.i3b[:], T.i3[:], 15, None, ALU.bitwise_and, None, ("i3",), ("i3b",))
+    tt(T.pb[:], T.pbb[:], T.i6[:], ALU.add, ("pbb", "i6"), ("pb",))
+    ts(T.a1[:], T.i3b[:], -16384.0, 262144.0 + 4096.0, ALU.mult, ALU.add, ("i3b",), ("a1",))
+    ts(T.a2[:], T.i3b[:], 10.0, 4096.0, ALU.is_lt, ALU.mult, ("i3b",), ("a2",))
+    ts(T.a3[:], T.i3b[:], 4.0, 4096.0, ALU.is_lt, ALU.mult, ("i3b",), ("a3",))
+    tt(T.a4[:], T.a1[:], T.a2[:], ALU.add, ("a1", "a2"), ("a4",))
+    tt(T.CJ[:], T.a4[:], T.a3[:], ALU.add, ("a4", "a3"), ("CJ",))
+    act(T.CJ2[:], T.CJ[:].indirect(T.exb[:]), AF.Copy, ("CJ", "exb"), ("CJ2",), bias=2048.0)
+    cp(T.R16[:, :, 0:16], T.I16[:], ("I16",), p=("R16",))
+    cp(T.R16[:, :, 16:32], T.I16[:], ("I16",), p=("R16",))
+    for s in range(2):
+        cp(T.S4[:, :, s, :], T.R16[:, 1 - s::2, 0:16], ("R16",), p=("S4",))
+    for e, m, nm in ((0, M0, "m0"), (1, M1, "m1")):
+        ts(T.PM[:, 384 * e:384 * e + 128], T.I16[:], C(m), None, ALU.mult, None, ("I16", nm), p=("PM",))
+        ts(T.PM[:, 128 + 128 * e:256 + 128 * e], T.S4[:], C(m), None, ALU.mult, None, ("S4", nm), p=("PM",))
+    for b in range(16):
+        cp(T.SH[:, 128 * b:128 * b + 128], T.R16[:, :, b:b + 16], ("R16",), p=("SH",))
+
+    def flip_calls(src, ns, X, XT, nx):
+        return [lambda: ts(X[:, :, 0:16], src, C(M0), None, ALU.mult, None, (ns, "m0"), p=(nx,)),
+                lambda: ts(X[:, :, 16:32], src, C(M1), None, ALU.mult, None, (ns, "m1"), p=(nx,)),
+                lambda: op("v", v.transpose, (XT[:], X[:]), (nx,), (nx + "T",))]
+
+    def halves(out, XT, nx, w):
+        mm(out, T.I16[:], XT[:, :, 0:16], True, False, ("I16", nx + "T"), w)
+        mm(out, T.I16[:], XT[:, :, 16:32], False, True, ("I16", nx + "T"), w)
+    cp(T.mk16[:], T.mkb[:], ("mkb",), ("mk16",))
+    ts(T.mo16[:], T.moi[:], 2048.0, None, ALU.subtract, None, ("moi",), ("mo16",))
+    for ps, src in (("pA", "mk16"), ("pB", "mo16")):
+        for b in range(16):
+            op("t", te.matmul, (T[ps][:, b:256:16], T.SH[:, 128 * b:128 * b + 128], T[src][:, b::16], True, True), ("SH", src), p=(ps,))
+    for f in flip_calls(T.pA[:, 0:256], "pA", T.X, T.XT, "X") + flip_calls(T.pB[:, 0:256], "pB", T.Y, T.YT, "Y"):
+        f()
+    halves(T.pA[:, 0:256], T.XT, "X", "pA")
+    halves(T.pB[:, 0:256], T.YT, "Y", "pB")
+    ts(T.LX[:, 0:16], T.lai[:], C(M0), None, ALU.mult, None, ("lai", "m0"), p=("LX",))
+    ts(T.LX[:, 16:32], T.lai[:], C(M1), None, ALU.mult, None, ("lai", "m1"), p=("LX",))
+    op("v", v.transpose, (T.LT[:], T.LX[:]), ("LX",), ("LT",))
+    tt(T.prev0[:], T.LT[:, 0:16], T.LT[:, 16:32], ALU.add, ("LT",), ("prev0",))
+    scan(T.dsum[:], T.R2[:], T.diag[:], ALU.mult, ALU.add, ("R2", "diag"), "dsum")
+    ts(C(THR), T.dsum[:, 15:16], 2.0, None, ALU.mult, None, ("dsum",), ("thr",))
+    ts(T.offc[:], T.dg[:], 0.0, C(OFF), ALU.mult, ALU.add, ("dg", "off"), ("offc",))
+    act(T.MK[:], T.pA[:, 0:256], AF.Copy, ("pA",), ("MK",))
+    tt(T.pM[:, 0:256], T.pB[:, 0:256], T.CJ2[:], ALU.add, ("pB", "CJ2"), ("pM",))
+    fill(T.ones[:], 1.0, w=("ones",))
+
+    kbank = ["pC", "pW", "pA", "pB"]
+
+    def keys(i0):
+        for i in range(i0, i0 + 4):
+            p = kbank[i % 4]
+            mm(T[p][:], T.wblk[:], T.featW[:, 512 * i:512 * i + 512], True, True, ("wblk", "feat"), p)
+        for i in range(i0, i0 + 4):
+            p = kbank[i % 4]
+            act(T.keyW[:, 512 * i:512 * i + 512], T[p][:], AF.Copy, (p,), p=("keyW",))
+
+    scq = []
+
+    def scatters():
+        scq.extend(range(15, -1, -1))
+
+    def scatter(k=1):
+        for i in range(min(k, len(scq))):
+            c = scq.pop(0)
+            tt(T.kid[:].indirect(T.s2u[:, 2 * c:2 * c + 1]), T.cf[:, 16 * c:16 * c + 16], T.offc[:], ALU.subtract, ("s2u", "cf0", "cf1", "offc"), ("kid",))
+
+    def limit():
+        mm(T.pC[:, 0:16], T.ones[:], T.cov[:], True, True, ("ones", "cov"), "pC")
+        return [lambda: op("v", v.tensor_reduce, (T.cs[:], T.pC[:, 0:16], AxisListType.X, ALU.add), ("pC",), ("cs",), kw=dict(negate=True)),
+                lambda: cp(T.csi[:], T.cs[:], ("cs",), ("csi",)),
+                lambda: ts(T.csa[:], T.csi[:], 15, None, ALU.bitwise_and, None, ("csi",), ("csa",)),
+                lambda: ts(T.limA[:], T.csa[:], 65536.0, 65536.0 * (LIM - 1), ALU.mult, ALU.add, ("csa",), ("limA",))]
+
+    def dist(c0, c1, nm, stop):
+        for b in range(16):
+            mm(T.pv[:, c0 // 2:c1 // 2, :], T.LH[:, 128 * b:128 * b + 128], T.A[:, c0:c1, 16 * b:16 * b + 16], False, stop and b == 15, ("LH", nm), "pv")
+    keys(0)
+    for t in range(STEPS):
+        iw, ia, ibn, final = "inW%d" % t, "inCa%d" % t, "inCb%d" % t, t == STEPS - 1
+        fw = 2 * W if t else W
+        fr = ("feat", "featd") if t else ("feat",)
+        mm(T.pv[:], T.IB[:], T.Kc[:], True, False, ("IB", "Kc"), "pv")
+        mm(T.pL[:], T.IB[:], T.Kc[:], True, False, ("IB", "Kc"), "pL")
+        for x, (c0, c1) in enumerate(CH):
+            tt(T.D[:, 256 * c0:256 * c1], T.featW[:, 0:fw].indirect(T.inC[:, 272 * t + 16 * c0:272 * t + 16 * c1]), T.Wx[:, 256 * c0:256 * c1], ALU.subtract,
+               fr + ("Wx", ia) + ((ibn,) if c1 > 8 else ()), ("D%d" % x,))
+            if x == XF:
+                ts(T.G[:], inC(t), C(CEN if t else CEN0), None, ALU.subtract, None, (ia, ibn, "cen" if t else "cen0"), ("G",))
+                scatter()
+                op("v", v.transpose, (T.GT[:], T.G[:]), ("G",), ("GT",))
+            if x == 0:
+                act(T.raw[:], T.featW[:, 0:fw].indirect(T.inC[:, 272 * t + 16 * OWN:272 * t + 256]), AF.Copy, fr + (ibn,), ("raw",))
+                mm(T.pX[:], T.IB[:], T.raw[:], True, False, ("IB", "raw"), "pX")
+                mm(T.pX[:], T.IN[:], T.Wx[:, 256 * OWN:4096], False, True, ("IN", "Wx"), "pX")
+            act(T.A[:, c0:c1, :], T.D[:, 256 * c0:256 * c1], AF.Abs, ("D%d" % x,), ("A%d" % x,))
+            if x == 1:
+                act(T.A[:, OWN:16, :], T.pX[:], AF.Abs, ("pX",), ("A9",))
+            if x == 2:
+                act(T.Lp[:], T.pL[:], AF.Identity, ("pL", "limA"), ("Lp",), bias=T.limA[:])
+            if x == len(CH) - 1 and not final:
+                act(T.D[:, 256 * OWN:4096], T.pX[:], AF.Abs, ("pX",), ("D9",))
+            if x == XF:
+                for p, e in (("pL", True), ("pv", False)):
+                    for c in range(2):
+                        for s in range(2):
+                            o = 256 * c + 128 * s
+                            mm(T[p][:, :, 16 * c:16 * c + 16], T.PM[:, o:o + 128], T.GT[:, :, 16 * s:16 * s + 16], False, e and c + s == 2, ("PM", "GT"), p)
+            dist(c0, c1, "A%d" % x, x == len(CH) - 1)
+            if x == 1:
+                dist(OWN, 16, "A9", False)
+        if t == 0:
+            keys(4)
+            for q in range(4):
+                cp(T.kid[:, 1024 * q:1024 * q + 1024], T.kidi[:, 1024 * q:1024 * q + 1024], ("kidi%d" % q,), p=("kid",))
+        else:
+            scatter(NT)
+        tt(T.vm[:], T.pv[:], T.Lp[:], ALU.max, ("pv", "Lp"), ("vm",))
+        scatter()
+        scan(T.vI[:], T.RST[:], T.vm[:], ALU.max, ALU.min, ("RST", "vm"), "vI")
+        scatter()
+        ts(T.oa[:], last16(T.vI), 4095, None, ALU.bitwise_and, None, ("vI",), ("oa",))
+        oo = "outO%d" % t
+        if not final:
+            ts(T.kk[:], last16(T.vI), 12, 15, ALU.logical_shift_right, ALU.bitwise_and, ("vI",), ("kk",))
+        scatter()
+        cp(outO(t), T.oa[:], ("oa",), (oo,))
+        if not final:
+            tt(T.po[:], T.kk[:], T.pb[:], ALU.add, ("kk", "pb"), ("po",))
+        scatter()
+        tt(T.ky[:], T.keyW[:].indirect(outO(t)), T.diag[:], ALU.mult, ("keyW", oo, "diag"), ("ky",))
+        if not final:
+            cp(T.pu[:], T.po[:], ("po",), ("pu",))
+            act(outW(t), T.D[:].indirect(T.pu[:]), AF.Abs, tuple("D%d" % x for x in range(len(CH))) + ("D9", "pu"), ("outW%d" % t,))
+            send(inW(t + 1), outW(t), "w%d" % (t + 1), ("outW%d" % t,))
+        scatter()
+        scan(T.ks[:], T.R1[:], T.ky[:], ALU.mult, ALU.add, ("R1", "ky"), "ks")
+        scatter()
+        ts(T.key[:], last16(T.ks), 63, None, ALU.bitwise_and, None, ("ks",), ("key",))
+        scatter()
+        tt(T.eq[:], T.key[:].indirect(T.expl[:]), T.MK[:], ALU.is_equal, ("key", "expl", "MK"), ("eq",))
+        scatter()
+        tt(T.em[:], T.eq[:], T.pM[:, 0:256], ALU.mult, ("eq", "pM"), ("em",))
+        scatter()
+        scan(T.es[:], T.RZ[:], T.em[:], ALU.min, ALU.max, ("RZ", "em"), "es")
+        scatter(16)
+        ev = last16(T.es)
+        ts(T.eo[:], ev, 4095, None, ALU.bitwise_and, None, ("es",), ("eo",))
+        ts(T.sT[:], ev, 13, 1, ALU.logical_shift_right, ALU.bitwise_and, ("es",), ("sT",))
+        ts(T.sL[:], ev, 12, 1, ALU.logical_shift_right, ALU.bitwise_and, ("es",), ("sL",))
+        tt(T.de[:], T.eo[:], T.oa[:], ALU.subtract, ("eo", "oa"), ("de",))
+        q = 5 * t % 16
+        pr, prn = (inP(t), ibn) if t else (T.prev0[:], "prev0")
+        ts(T.ncd[:], ev, 1.0, C(DUMP), ALU.is_lt, ALU.mult, ("es", "dump"), ("ncd",))
+        tt(T.dk[:], T.key[:], T.MK[:, q::16], ALU.subtract, ("key", "MK"), ("dk",))
+        tt(T.tT[:], T.sT[:], T.de[:], ALU.mult, ("sT", "de"), ("tT",))
+        tt(T.tL[:], T.sL[:], T.de[:], ALU.mult, ("sL", "de"), ("tL",))
+        ts(T.pn[:], pr, T.CJ[:, q:q + 1], None, ALU.add, None, (prn, "CJ"), ("pn",))
+        ts(T.na[:], last16(T.vI), T.limA[:], 65536.0, ALU.subtract, ALU.is_ge, ("vI", "limA"), ("na",))
+        tt(T.l2[:, 0:16], T.tT[:], T.oa[:], ALU.add, ("tT", "oa"), p=("l2",))
+        tt(T.l2[:, 16:32], T.tL[:], T.oa[:], ALU.add, ("tL", "oa"), p=("l2",))
+        tt(T.s1[:], T.oa[:], T.ncd[:], ALU.max, ("oa", "ncd"), ("s1",))
+        tt(T.dk2[:], T.dk[:], T.na[:], ALU.mult, ("dk", "na"), ("dk2",))
+        cp(T.u2[:], T.l2[:], ("l2",), ("u2",))
+        for h in range(2):
+            act(T.top[:, 128 * h:128 * h + 128], T.kid[:, 0:W].indirect(T.u2[:, 8 * h:8 * h + 8]), AF.Identity, ("kid", "u2", "sct", "bit"), ("top%d" % h,),
+                bias=C(BIT), scale=C(SCT))
+        tt(T.dn[:], T.pn[:], T.pM[:, q:256:16], ALU.subtract, ("pn", "pM"), ("dn",))
+        cp(T.s1u[:], T.s1[:], ("s1",), ("s1u",))
+        tt(T.MK[:, q::16], T.MK[:, q::16], T.dk2[:], ALU.add, ("dk2",), ("MK",))
+        tt(T.dn2[:], T.dn[:], T.na[:], ALU.mult, ("dn", "na"), ("dn2",))
+        for h in range(2):
+            s = slice(128 * h, 128 * h + 128)
+            tt(T.cf[:, s], T.kid[:, 0:W].indirect(T.u2[:, 16 + 8 * h:24 + 8 * h]), T.top[:, s], ALU.max, ("kid", "u2", "top%d" % h), ("cf%d" % h,))
+        for h in range(2):
+            o = 272 * t + 128 * h
+            e = o + (144 if h and not final else 128)
+            if h:
+                tt(T.pM[:, q:256:16], T.dn2[:], T.pM[:, q:256:16], ALU.add, ("dn2",), ("pM",))
+            cp(T.outC[:, o:o + 128], T.cf[:, 128 * h:128 * h + 128], ("cf%d" % h,), ("oC%d" % h,))
+            send(T.inC[:, o + 272:e + 272], T.outC[:, o:e], "ab"[h] + "%d" % (t + 1), ("oC%d" % h, oo))
+        if not final:
+            act(T.cov[:], T.ncd[:], AF.Sign, ("ncd",), ("cov",))
+        act(T.gl[:], T.idW[:].indirect(T.s1u[:]), AF.Copy, ("idW", "s1u"), ("gl",))
+        lim, wq = [], []
+        if not final:
+            lim = limit()
+            arrive("w%d" % (t + 1), nin, ("inW%d" % (t + 1),))
+            arrive("a%d" % (t + 1), nin, ("inCa%d" % (t + 1),))
+            arrive("b%d" % (t + 1), nin, ("inCb%d" % (t + 1),))
+            for k in range(KD, 16):
+                expand(t + 1, "s" if k < 16 - KG else "g", k)
+            wq = list(range(KD))
+        def fill_in():
+            if lim:
+                lim.pop(0)()
+            if wq:
+                expand(t + 1, "v", wq.pop(0))
+        fill_in()
+        tt(T.eq2[:], T.s1[:].indirect(T.expl[:]), T.gl[:], ALU.is_equal, ("s1", "expl", "gl"), ("eq2",))
+        fill_in()
+        scan(T.dsum[:], T.R2[:], T.eq2[:], ALU.mult, ALU.add, ("R2", "eq2"), "dsum")
+        fill_in()
+        ts(T.dd[:], last16(T.dsum), C(THR), C(DUMP), ALU.is_ge, ALU.mult, ("dsum", "thr", "dump"), ("dd",))
+        fill_in()
+        tt(T.s2[:], T.s1[:], T.dd[:], ALU.max, ("s1", "dd"), ("s2",))
+        fill_in()
+        cp(T.s2u[:, 0::2], T.s2[:], ("s2",), ("s2u",))
+        scatters()
+        while wq:
+            fill_in()
+        if not final:
+            scatter()
+    calls = [lambda: tt(T.mo16[:], T.pM[:, 0:256], T.CJ2[:], ALU.subtract, ("pM", "CJ2"), ("mo16",)),
+             lambda: ts(T.mk16[:], T.MK[:], 1.0 / 64, None, ALU.mult, None, ("MK",), ("mk16",))]
+    for f in calls + flip_calls(T.mo16[:], "mo16", T.X, T.XT, "X") + flip_calls(T.mk16[:], "mk16", T.Y, T.YT, "Y"):
+        scatter()
+        f()
+    for b in range(16):
+        sh = T.SH[:, 128 * (-b % 16):128 * (-b % 16) + 128]
+        for e, (XT, nx, o) in enumerate(((T.XT, "XT", 0), (T.XT, "XT", 16), (T.YT, "YT", 0), (T.YT, "YT", 16))):
+            op("t", te.matmul, (T.pA[:, b:256:16], sh, XT[:, :, o + b], e == 0, e == 3), ("SH", nx), p=("pA",))
+    scatter(16)
+    yb = ["pB", "pC", "pW", "pX"]
+    for i in range(1, 5):
+        act(T[yb[i - 1]][:], T.kid[:, 512 * i:512 * i + 512], AF.Copy, ("kid",), (yb[i - 1],), scale=float(i + 1))
+    arrive("a%d" % STEPS, nin, ("inCa%d" % STEPS,))
+    arrive("b%d" % STEPS, nin, ("inCb%d" % STEPS,))
+    tt(T.acc[:], T.kid[:, 0:512], T[yb[0]][:], ALU.add, ("kid", yb[0]), ("acc0", "acc1"))
+    ts(T.yno[:], inC(STEPS), C(OFF), None, ALU.subtract, None, ("inCa%d" % STEPS, "inCb%d" % STEPS, "off"), ("yno",))
+    dma("y", T.yn[:], T.yno[:], "yn", r=("yno",))
+    act(T.ymo[:], T.pA[:, 0:256], AF.Copy, ("pA",), ("ymo",), scale=64.0, bias=131072.0)
+    dma("s", T.ymu[:], T.ymo[:], "ymu", r=("ymo",))
+    for i in range(2, 8):
+        p = yb[(i - 1) % 4]
+        if i > 4:
+            act(T[p][:], T.kid[:, 512 * i:512 * i + 512], AF.Copy, ("kid",), (p,), scale=float(i + 1))
+        for h in range(2):
+            s, a = slice(256 * h, 256 * h + 256), "acc%d" % h
+            tt(T.acc[:, s], T.acc[:, s], T[p][:, s], ALU.add, (a, p), (a,))
+    dma("y", T.yd[:], T.acc[:], "yd", r=("acc0", "acc1"))
+    finish("g")

@@ -1,489 +1,514 @@
-from concourse.mybir import AluOpType as ALU, AxisListType, ActivationFunctionType as AF
+from concourse.mybir import AluOpType as ALU, ActivationFunctionType as AF
 
 STEPS, W, L, LIM = 8, 4096, 256, 60
-CH = [(0, 2), (2, 6), (6, 10), (10, 14)]
-OWN = 14
-XF = 1
-KD, KG = 6, 3
-NT = 6
-BIG = float(2 ** 26)
+PARTS = [(8, 16), (0, 8)]
+CH = [("v", 2), ("s", 2), ("v", 2), ("s", 2)]
+BATCH = [4, 8]
+BIG, NONE, RS, KS, RC = float(2 ** 26), 2 ** 17, float(2 ** 17), float(2 ** 18), 120
+LAG, RELAY, FLYW, KEYQ = 2000.0, False, 2600.0, "svsvsvsv"
+NP, NC = len(PARTS), 16 // len(PARTS)
+WTQ, KGQ, TOPQ, HOPX, YP = "s", "s", "s", 210.0, 2
+KQ = [0, 1536, 3072, 3584, 4096]
+CS = 16 * NC + 8
+NS = 16 * NC
+CY, PE, GA, SCAT, HOP, FLY, LOAD, RATE, ROWS, LOOK = 0.85, 0.54, 1.56, 3.8, 210.0, 2600.0, 1600.0, 300.0, 80000.0, 3.0
 
 _f, _b, _h, _i, _u = "float32", "bfloat16", "float16", "int32", "uint16"
+_t = lambda n, d: ("sbuf", [128, n], d)
 SCRATCH = {
-    "featW": ("sbuf", [128, 2 * W], _b), "kidi": ("sbuf", [128, W], _i), "kid": ("sbuf", [128, W + 16], _f),
-    "keyW": ("sbuf", [128, W], _f), "idW": ("sbuf", [128, W + 16], _f),
-    "Wx": ("sbuf", [128, W], _b), "D": ("sbuf", [128, W], _b), "A": ("sbuf", [128, 16, 256], _b), "raw": ("sbuf", [128, 512], _b),
-    "LH": ("sbuf", [128, 2048], _b), "SH": ("sbuf", [128, 2048], _h), "R16": ("sbuf", [128, 8, 32], _h),
-    "i1": ("sbuf", [128, 128], _i), "i1b": ("sbuf", [128, 128], _i), "i2": ("sbuf", [128, 16], _i), "i2b": ("sbuf", [128, 16], _i),
-    "i3": ("sbuf", [128, 16], _i), "i3b": ("sbuf", [128, 16], _i), "i4": ("sbuf", [128, 16], _i), "i5": ("sbuf", [128, 16], _i), "i6": ("sbuf", [128, 16], _i),
-    "bi": ("sbuf", [128, 16], _i), "exb": ("sbuf", [128, 16], _u), "dg": ("sbuf", [128, 16], _f), "ib": ("sbuf", [128, 8], _i),
-    "a1": ("sbuf", [128, 16], _f), "a2": ("sbuf", [128, 16], _f), "a3": ("sbuf", [128, 16], _f), "a4": ("sbuf", [128, 16], _f),
-    "blk": ("sbuf", [128, 128], _f), "diag": ("sbuf", [128, 256], _f), "I16": ("sbuf", [128, 128], _h), "IB": ("sbuf", [128, 128], _b),
-    "IN": ("sbuf", [128, 128], _b), "If": ("sbuf", [128, 128], _f), "ones": ("sbuf", [128, 128], _b), "wblk": ("sbuf", [128, 128], _b),
-    "b8": ("sbuf", [128, 8], _b), "Kc": ("sbuf", [128, 256], _b), "expl": ("sbuf", [128, 16], _u),
-    "RST": ("sbuf", [128, 256], _f), "RZ": ("sbuf", [128, 256], _f), "R1": ("sbuf", [128, 256], _f), "R2": ("sbuf", [128, 256], _f),
-    "CJ": ("sbuf", [128, 16], _f), "CJ2": ("sbuf", [128, 256], _f),
-    "col": ("sbuf", [128, 16], _f), "offc": ("sbuf", [128, 16], _f), "wti": ("sbuf", [128, 1], _i), "wtf": ("sbuf", [128, 1], _f),
-    "ci": ("sbuf", [128, 256], _i), "mkb": ("sbuf", [128, 256], _b), "moi": ("sbuf", [128, 256], _i), "mk16": ("sbuf", [128, 256], _h), "mo16": ("sbuf", [128, 256], _h),
-    "lai": ("sbuf", [128, 16], _i), "LX": ("sbuf", [128, 32], _f), "LT": ("sbuf", [128, 32], _f), "prev0": ("sbuf", [128, 16], _f),
+    "featW": _t(W, _b), "kidi": _t(W, _i), "kid": _t(W + 16, _f), "keyW": _t(W, _b), "idW": _t(W + 16, _f),
+    "A": ("sbuf", [128, 16, 256], _b), "raw": _t(W, _b),
+    "XP": ("sbuf", [128, NS, 16], _b), "WT": _t(128 * NP, _b),
+    "LH": _t(2048, _b), "LW": _t(2048, _b), "EX": _t(2048, _b), "SH": _t(2048, _h), "R16": ("sbuf", [128, 8, 32], _h),
+    "i1": _t(128, _i), "i1b": _t(128, _i), "i2": _t(16, _i), "i2b": _t(16, _i), "i3": _t(16, _i), "i3b": _t(16, _i), "i4": _t(16, _i), "i5": _t(16, _i),
+    "bi": _t(16, _i), "exb": _t(16, _u), "dg": _t(16, _f), "ib": _t(8, _i), "a0": _t(16, _i), "a1": _t(16, _f), "a2": _t(16, _f), "a3": _t(16, _f), "a4": _t(16, _f), "a5": _t(16, _f),
+    "blk": _t(128, _b), "diag": _t(128, _b), "I16": _t(128, _h), "IN16": _t(128, _h), "IB": _t(128, _b), "IN": _t(128, _b), "INf": _t(128, _f), "F7": _t(128, _f), "F8": _t(128, _f), "IK": _t(128, _b),
+    "ones": _t(128, _f), "b8": _t(8, _b), "Kc": _t(128, _b), "ob": _t(128, _b), "expl": _t(16, _u),
+    "RST": _t(256, _f), "RN": _t(256, _f), "R2": _t(256, _f), "CJ": _t(16, _f), "CJ2": _t(256, _f), "col": _t(16, _f), "wti": _t(1, _i), "wtf": _t(1, _f),
+    "ci": _t(256, _i), "mkb": _t(256, _b), "moi": _t(256, _i), "mk16": _t(256, _h), "mo16": _t(256, _h), "mi": _t(256, _i), "mj": _t(256, _i), "mn": _t(256, _i),
+    "klb": _t(256, _b),
+    "lai": _t(16, _i), "LX": _t(32, _f), "LT": _t(32, _f), "prev0": _t(16, _f),
     "X": ("sbuf", [128, 16, 32], _h), "XT": ("sbuf", [128, 16, 32], _h), "Y": ("sbuf", [128, 16, 32], _h), "YT": ("sbuf", [128, 16, 32], _h),
-    "G": ("sbuf", [128, 8, 32], _h), "GT": ("sbuf", [128, 8, 32], _h), "PM": ("sbuf", [128, 512], _h), "S4": ("sbuf", [128, 4, 2, 16], _h),
-    "MK": ("sbuf", [128, 256], _f), "Lp": ("sbuf", [128, 256], _f), "vm": ("sbuf", [128, 256], _f), "vI": ("sbuf", [128, 256], _i),
-    "oa": ("sbuf", [128, 16], _i), "kk": ("sbuf", [128, 16], _i), "po": ("sbuf", [128, 16], _i), "pb": ("sbuf", [128, 16], _i), "pbb": ("sbuf", [128, 16], _i), "pu": ("sbuf", [128, 16], _u),
-    "ky": ("sbuf", [128, 256], _f), "ks": ("sbuf", [128, 256], _i), "key": ("sbuf", [128, 16], _i),
-    "eq": ("sbuf", [128, 256], _f), "em": ("sbuf", [128, 256], _f), "es": ("sbuf", [128, 256], _i),
-    "eo": ("sbuf", [128, 16], _i), "sT": ("sbuf", [128, 16], _i), "sL": ("sbuf", [128, 16], _i), "de": ("sbuf", [128, 16], _i),
-    "tT": ("sbuf", [128, 16], _i), "tL": ("sbuf", [128, 16], _i), "l2": ("sbuf", [128, 32], _i), "u2": ("sbuf", [128, 32], _u),
-    "top": ("sbuf", [128, 256], _f), "cf": ("sbuf", [128, 256], _f),
-    "na": ("sbuf", [128, 16], _f), "cov": ("sbuf", [128, 16], _b), "ncd": ("sbuf", [128, 16], _f), "s1": ("sbuf", [128, 16], _f), "s1u": ("sbuf", [128, 16], _u),
-    "gl": ("sbuf", [128, 256], _f), "eq2": ("sbuf", [128, 256], _f), "dsum": ("sbuf", [128, 256], _f), "dd": ("sbuf", [128, 16], _f), "s2": ("sbuf", [128, 16], _f), "s2u": ("sbuf", [128, 32], _u),
-    "dk": ("sbuf", [128, 16], _f), "dk2": ("sbuf", [128, 16], _f), "pn": ("sbuf", [128, 16], _f), "dn": ("sbuf", [128, 16], _f), "dn2": ("sbuf", [128, 16], _f),
-    "cs": ("sbuf", [128, 1], _f), "csi": ("sbuf", [128, 1], _i), "csa": ("sbuf", [128, 1], _i), "limA": ("sbuf", [128, 1], _f),
-    "yno": ("sbuf", [128, 256], _f), "ymo": ("sbuf", [128, 256], _f), "acc": ("sbuf", [128, 512], _f),
-    "outC": ("sbuf", [128, STEPS * 272], _u), "inC": ("sbuf", [128, (STEPS + 1) * 272], _u),
-    "outW": ("sbuf", [128, STEPS * 256], _b), "inW": ("sbuf", [128, STEPS * 256], _b),
-    "pv": ("psum", [128, 8, 32], _f), "pL": ("psum", [128, 8, 32], _f), "pM": ("psum", [128, 512], _f), "pC": ("psum", [128, 512], _f),
-    "pW": ("psum", [128, 512], _f), "pA": ("psum", [128, 512], _f), "pB": ("psum", [128, 512], _f), "pX": ("psum", [128, 512], _f),
+    "G": ("sbuf", [128, 8, 32], _h), "GT": ("sbuf", [128, 8, 32], _h), "PM": _t(512, _h), "PK": _t(512, _b), "S4": ("sbuf", [128, 4, 2, 16], _h),
+    "M": _t(256, _f), "Lp": _t(256, _f), "vm": _t(256, _f), "vI": _t(256, _i), "yy": _t(16, _i), "KG": _t(256, _b), "KT": ("sbuf", [128, 8, 32], _b), "AB": _t(256, _f), "es": _t(256, _i),
+    "x2": _t(32, _i), "l2": _t(32, _i), "l3": _t(32, _i), "u2": _t(32, _u), "top": _t(256, _f), "cf": _t(256, _f),
+    "na": _t(16, _f), "cov": _t(16, _f), "ncd": _t(16, _f), "s1": _t(8 * NP, _f), "s1u": _t(16, _u), "gl": _t(256, _f), "eq2": _t(256, _f), "dsum": _t(256, _f),
+    "dd": _t(16, _f), "s2": _t(16, _f), "s2u": _t(32, _u), "pn": _t(16, _f), "dn": _t(16, _f), "dn2": _t(16, _f),
+    "cs": _t(1, _f), "csi": _t(1, _i), "csa": _t(1, _i), "limA": _t(1, _f), "th": _t(16, _f),
+    "outF": _t(256, _f), "inF": _t(256, _f), "ymo": _t(256, _f), "acc": _t(512, _f),
+    "outC": _t(STEPS * NP * CS, _u), "inC": _t(STEPS * NP * CS, _u), "DW": _t(256, _b), "outW": _t(STEPS * 256, _b), "inW": _t(STEPS * 256, _b),
+    "pv0": ("psum", [128, 16, 32], _f), "pv1": ("psum", [128, 16, 32], _f), "pL": ("psum", [128, 16, 32], _f), "pS": ("psum", [128, 16, 32], _f),
+    "pX0": ("psum", [128, 512], _f), "pX1": ("psum", [128, 512], _f), "pX2": ("psum", [128, 512], _f), "pX3": ("psum", [128, 512], _f),
 }
-DMAS = ["cand", "want", "wts", "last", "mkey", "mobj", "f0", "fd", "k0", "k1", "k2", "k3", "yn", "ymu", "yd"]
-SEMAPHORES = ["sv", "st", "ss", "sg", "ls"] + ["d_" + n for n in DMAS] + ["w%d" % t for t in range(1, STEPS)] + [x + "%d" % t for t in range(1, STEPS + 1) for x in "ab"]
+DMAS = ["cand", "want", "wts", "last", "mkey", "mobj", "feat0", "feat", "ymu", "yd0", "yd1"] + ["k%d" % q for q in range(8)] + ["yn%d" % h for h in range(NP)]
+SEMAPHORES = ["sv", "st", "ss", "sg", "ls"] + ["d_" + n for n in DMAS] + [x + "%d_%d" % (t, h) for x in "cw" for t in range(1, STEPS + 1) for h in range(NP)]
+OWN = {"v": "sv", "t": "st", "s": "ss", "g": "sg"}
 
 
-def make(g, T):
-    Q = {"v": g.vector, "t": g.tensor, "s": g.scalar, "g": g, "y": g.sync}
-    own = {"v": "sv", "t": "st", "s": "ss", "g": "sg"}
-    cnt, known, hist, tags = {}, {q: {} for q in Q}, {}, {}
+def make():
+    ops, tags, lag = [], {}, [0.0]
 
     def tag(n):
         if n not in tags:
-            tags[n] = {"w": {}, "r": {}, "base": {}, "full": False}
+            tags[n] = {"w": [], "r": [], "base": [], "full": False, "mm": None}
         return tags[n]
 
-    def merge(a, b):
-        for s, c in b.items():
-            if a.get(s, 0) < c:
-                a[s] = c
-
-    def wait(q, needs):
-        for s in sorted(needs, key=lambda s: -len(hist.get((s, needs[s]), {}))):
-            c = needs[s]
-            if known[q].get(s, 0) < c:
-                Q[q].wait_ge(T.sem[s], c)
-                merge(known[q], hist.get((s, c), {}))
-                merge(known[q], {s: c})
-
-    def deps(q, r, w, p, acc):
-        need = {}
+    def add(q, call, ns, r=(), w=(), p=(), acc=False, sem=None, lat=0.0, after=()):
+        i, pre = len(ops), {}
         for n in r:
-            merge(need, tag(n)["w"])
+            d = tag(n)
+            pre.update({j: True for j in d["w"]})
+            if n[0] == "p" and n[1] in "vLSXT":
+                pre.update({j: True for j in d["r"] if ops[j]["q"] != q})
         for n in w:
             d = tag(n)
-            for m in (d["w"], d["r"], d["base"]):
-                merge(need, {s: c for s, c in m.items() if not (acc and s == own.get(q))})
+            pre.update({j: True for j in d["w"] + d["r"] + d["base"] if not (acc and ops[j]["q"] == q)})
         for n in p:
             d = tag(n)
             if d["full"] or d["r"]:
-                merge(d["base"], d["w"])
-                merge(d["base"], d["r"])
-                d["w"], d["r"], d["full"] = {}, {}, False
-            merge(need, d["base"])
-        return need
-
-    def mark(s, c, r, w, p, acc):
+                d["base"], d["w"], d["r"], d["full"] = d["w"] + d["r"], [], [], False
+            pre.update({j: True for j in d["base"]})
+        for j in list(after) + [tag(n)["mm"] for n in tuple(w) + tuple(p) if q == "t" and tag(n)["mm"] is not None]:
+            pre.setdefault(j, False)
         for n in r:
-            merge(tag(n)["r"], {s: c})
+            tag(n)["r"].append(i)
         for n in w:
+            d = tag(n)
             if acc:
-                merge(tag(n)["w"], {s: c})
-                tag(n)["r"] = {}
+                d["w"].append(i)
+                d["r"] = []
             else:
-                tags[n] = {"w": {s: c}, "r": {}, "base": {}, "full": True}
+                d["w"], d["r"], d["base"], d["full"] = [i], [], [], True
         for n in p:
-            merge(tag(n)["w"], {s: c})
+            tag(n)["w"].append(i)
+        if q == "t":
+            for n in tuple(w) + tuple(p):
+                tag(n)["mm"] = i
+        ops.append({"lag": lag[0], "q": q, "call": call, "ns": ns, "pre": pre, "sem": sem, "lat": lat})
+        return i
+    return ops, add, lag
 
-    def op(q, fn, args, r=(), w=(), p=(), acc=False, kw=None):
-        wait(q, deps(q, r, w, p, acc))
-        s = own[q]
-        cnt[s] = c = cnt.get(s, 0) + 1
-        fn(*args, **(kw or {})).then_inc(T.sem[s], 1)
-        hist[(s, c)] = dict(known[q])
-        mark(s, c, r, w, p, acc)
 
-    def dma(q, out, in_, name, r=(), w=(), p=()):
-        wait(q, deps(q, r, w, p, False))
-        s = "d_" + name
-        cnt[s] = 16
-        Q[q].dma_start(out, in_).then_inc(T.sem[s], 16)
-        hist[(s, 16)] = dict(known[q])
-        mark(s, 16, r, w, p, False)
+def order(ops):
+    n = len(ops)
+    post = [[] for i in range(n)]
+    for i, o in enumerate(ops):
+        for j in o["pre"]:
+            post[j].append(i)
+    gap = lambda j, i: (ops[j]["lat"] + (HOP if ops[i]["q"] == ops[j]["q"] else HOPX)) if ops[i]["pre"][j] else 0.0
+    way = [0.0] * n
+    for i in range(n - 1, -1, -1):
+        way[i] = ops[i]["ns"] + max([gap(i, k) + way[k] for k in post[i]] + [ops[i]["lat"]])
+    way = [way[i] - ops[i]["lag"] for i in range(n)]
+    left, ready, done = [len(o["pre"]) for o in ops], [0.0] * n, [0.0] * n
+    free, cand, seq = {}, {}, []
+    for i, o in enumerate(ops):
+        free[o["q"]] = 0.0
+        cand.setdefault(o["q"], [])
+        if not left[i]:
+            cand[o["q"]].append(i)
+    while len(seq) < n:
+        now, q = min((max(free[q], min(ready[i] for i in c)), q) for q, c in cand.items() if c)
+        i = max(cand[q], key=lambda i: way[i] - LOOK * max(0.0, ready[i] - now))
+        if ready[i] > now:
+            fit = [k for k in cand[q] if max(now, ready[k]) + ops[k]["ns"] <= ready[i] + 40.0]
+            if fit:
+                i = max(fit, key=lambda k: way[k] - LOOK * max(0.0, ready[k] - now))
+        cand[q].remove(i)
+        seq.append(i)
+        done[i] = max(now, ready[i]) + ops[i]["ns"]
+        if q != "x":
+            free[q] = done[i]
+        for k in post[i]:
+            ready[k] = max(ready[k], done[i] + gap(i, k))
+            left[k] -= 1
+            if not left[k]:
+                cand[ops[k]["q"]].append(k)
+    return seq
 
-    def arrive(s, c, w):
-        cnt[s] = c
-        mark(s, c, (), w, (), False)
 
-    def need(q, r):
-        wait(q, deps(q, r, (), (), False))
-
-    def finish(q):
-        for s in sorted(cnt):
-            if known[q].get(s, 0) < cnt[s]:
-                Q[q].wait_ge(T.sem[s], cnt[s])
-    return op, dma, arrive, need, finish, cnt
+def emit(g, T, ops, seq):
+    Q = {"v": g.vector, "t": g.tensor, "s": g.scalar, "g": g, "y": g.sync}
+    cnt, known, hist, at = {}, {q: {} for q in Q}, {}, {}
+    for i in seq:
+        o = ops[i]
+        q = o["q"]
+        if q == "x":
+            at[i] = o["sem"]
+            cnt[o["sem"][0]] = o["sem"][1]
+            continue
+        need = {}
+        for j, sem in o["pre"].items():
+            if sem:
+                s, c = at[j]
+                need[s] = max(need.get(s, 0), c)
+        for s in sorted(need, key=lambda s: -len(hist.get((s, need[s]), {}))):
+            if known[q].get(s, 0) < need[s]:
+                Q[q].wait_ge(T.sem[s], need[s])
+                for s2, c2 in list(hist.get((s, need[s]), {}).items()) + [(s, need[s])]:
+                    known[q][s2] = max(known[q].get(s2, 0), c2)
+        s, k = o["sem"] or (OWN[q], 1)
+        cnt[s] = cnt.get(s, 0) + k
+        at[i] = (s, cnt[s])
+        hist[at[i]] = dict(known[q])
+        ins = o["call"]()
+        if s != "ls":
+            ins.then_inc(T.sem[s], k)
+    for s in sorted(cnt):
+        if known["g"].get(s, 0) < cnt[s]:
+            g.wait_ge(T.sem[s], cnt[s])
 
 
 def rank_program(g, core, T, topo):
-    rank = T.rank_of(core)
+    rank, n = T.rank_of(core), len(T.cores)
+    wants = lambda b, t, h: b[:, 256 * t + 16 * PARTS[h][0]:256 * t + 16 * PARTS[h][1]]
+
+    def helper(a, b):
+        free = [c for c in topo.cores_of(a) if c not in T.cores and topo.may_write(c, b) and topo.die(c) != topo.die(a)]
+        return free[0] if RELAY and free and topo.chip(a) != topo.chip(b) else None
     if rank is None:
+        for a, b in zip(T.cores, T.cores[1:] + T.cores[:1]):
+            if helper(a, b) == core:
+                k = len(topo.engines(a, core)) - len(topo.engines(a, b))
+                for t in range(1, STEPS):
+                    for h in range(NP):
+                        sem = T.sem["w%d_%d" % (t, h)]
+                        g.wait_ge(sem, k)
+                        g.remote_dma(wants(T.inW, t, h), wants(T.inW, t, h), sem, T.sem.ls, topo.addr(b)[1], topo.addr(b)[0], topo.mask(core, b))
+                g.wait_ge(T.sem.ls, (STEPS - 1) * NP * len(topo.engines(core, b)))
         return
-    op, dma, arrive, need, finish, cnt = make(g, T)
+    ops, add, lag = make()
     v, te, sc = g.vector, g.tensor, g.scalar
-    n = len(T.cores)
     nxt, prv = T.cores[(rank + 1) % n], T.cores[(rank - 1) % n]
-    rid, pid, _se = topo.addr(nxt)
-    mask, nout, nin = topo.mask(core, nxt), len(topo.engines(core, nxt)), len(topo.engines(prv, core))
+    hlp, nin = helper(core, nxt), len(topo.engines(prv, core))
+    cy = lambda k: max(64.0, k) * CY
+    ga = lambda k: (60.0 + GA * k) * CY
 
-    def ts(out, in0, s1, s2, o0, o1, r, w=(), p=()):
+    def ts(ns, out, in0, s1, s2, o0, o1, r, w=(), p=()):
         args = (out, in0, s1, s2, o0) if o1 is None else (out, in0, s1, s2, o0, o1)
-        op("v", v.tensor_scalar, args, r, w, p)
+        add("v", lambda: v.tensor_scalar(*args), ns, r, w, p)
 
-    def tt(out, a, b, o, r, w=(), p=()):
-        op("v", v.tensor_tensor, (out, a, b, o), r, w, p)
+    def tt(ns, out, a, b, o, r, w=(), p=()):
+        add("v", lambda: v.tensor_tensor(out, a, b, o), ns, r, w, p)
 
-    def cp(out, a, r, w=(), p=()):
-        op("v", v.tensor_copy, (out, a), r, w, p)
+    def cp(ns, out, a, r, w=(), p=()):
+        add("v", lambda: v.tensor_copy(out, a), ns, r, w, p)
 
-    def scan(out, d0, d1, o0, o1, r, w):
-        op("v", v.tensor_tensor_scan, (out, d0, d1, 0.0, o0, o1), r, (w,))
+    def tr(ns, out, a, r, w):
+        add("v", lambda: v.transpose(out, a), ns, r, w)
 
-    def act(out, a, f, r, w=(), p=(), **kw):
-        op("s", sc.activation, (out, a, f), r, w, p, kw=kw)
+    def scan(ns, out, d0, d1, o0, o1, r, w):
+        add("v", lambda: v.tensor_tensor_scan(out, d0, d1, 0.0, o0, o1), ns, r, w)
 
-    def mm(out, l, rh, st, sp, r, w):
-        op("t", te.matmul, (out, l, rh, st, sp), r, (w,), acc=not st)
+    def act(ns, out, a, f, r, w=(), p=(), **kw):
+        add("s", lambda: sc.activation(out, a, f, **kw), ns, r, w, p)
 
-    def send(out, in_, sem, r):
-        need("g", r)
-        g.remote_dma(out, in_, T.sem[sem], T.sem.ls, pid, rid, mask)
-        cnt["ls"] = cnt.get("ls", 0) + nout
+    def mm(k, out, l, rh, st, sp, r, w, part=False):
+        if part:
+            add("t", lambda: te.matmul(out, l, rh, st, sp), max(64, k) * PE, r, p=(w,))
+        else:
+            add("t", lambda: te.matmul(out, l, rh, st, sp), max(64, k) * PE, r, (w,), acc=not st)
 
-    def fill(ap, x, w=(), p=()):
-        op("v", v.memset, (ap, x), (), w, p)
+    def fill(ns, ap, x, w=(), p=()):
+        add("v", lambda: v.memset(ap, x), ns, (), w, p)
 
-    def iota(out, pat, base, ch, w, **kw):
-        op("g", g.iota, (out, pat, base, ch), (), (w,), kw=kw)
+    def iota(k, out, pat, base, ch, w, **kw):
+        last["g"] = [add("g", lambda: g.iota(out, pat, base, ch, **kw), 140 + 2 * k * CY, (), (w,), after=last["g"])]
+    last = {"s": [], "y": [], "g": [], "bytes": [0.0]}
+
+    def dma(q, out, in_, name, nbytes, r=(), w=()):
+        last["bytes"][0] = nbytes + ROWS + (0.0 if r else last["bytes"][0])
+        last[q] = [add(q, lambda: (sc if q == "s" else g.sync).dma_start(out, in_), 60.0, r, w, sem=("d_" + name, 16), lat=LOAD + last["bytes"][0] / RATE, after=() if r else last[q])]
+
+    def send(out, in_, sem, r, w, via=None, fly=FLY):
+        rid, pid, _se = topo.addr(via or nxt)
+        mask = topo.mask(core, via) & ~topo.mask(core, nxt) if via else topo.mask(core, nxt)
+        i = add("g", lambda: g.remote_dma(out, in_, T.sem[sem], T.sem.ls, pid, rid, mask), 400.0, r, sem=("ls", bin(mask).count("1")))
+        add("x", None, fly, (), w, sem=(sem, nin), after=(i,))
     C = lambda j: T.col[:, j:j + 1]
-    M1, M0, SCT, BIT, CEN, DUMP, THR, OFF, CEN0 = range(9)
-    inC = lambda t: T.inC[:, 272 * t:272 * t + 256]
-    inP = lambda t: T.inC[:, 272 * t + 256:272 * t + 272]
-    outO = lambda t: T.outC[:, 272 * t + 256:272 * t + 272]
-    inW = lambda t: T.inW[:, 256 * t:256 * t + 256]
-    outW = lambda t: T.outW[:, 256 * t:256 * t + 256]
-    last16 = lambda b: b[:, 15::16]
+    M1, M0, SCT, BIT, DUMP, THR, OFF, K0, K1 = range(9)
+    S = cy(16)
 
-    dma("s", T.ci[:], T.cand[:], "cand", w=("ci",))
-    dma("y", inW(0), T.want[:], "want", w=("inW0",))
-    dma("y", T.featW[:, 0:W], T.feat[:], "f0", w=("feat",))
-    dma("s", T.mkb[:], T.mkey[:], "mkey", w=("mkb",))
-    dma("s", T.moi[:], T.mobj[:], "mobj", w=("moi",))
-    dma("s", T.wti[:], T.wts[:], "wts", w=("wti",))
-    dma("s", T.lai[:], T.last[:], "last", w=("lai",))
-    for q in range(4):
-        dma("y", T.kidi[:, 1024 * q:1024 * q + 1024], T.kids[:, 1024 * q:1024 * q + 1024], "k%d" % q, w=("kidi%d" % q,))
-    dma("y", T.featW[:, W:2 * W], T.feat[:], "fd", w=("featd",))
+    dma("y", T.wti[:], T.wts[:], "wts", 512, w=("wti",))
+    dma("y", T.featW[:, 0:W // 2], T.feat[:, 0:W // 2], "feat0", 524288, w=("feat0",))
+    dma("y", T.ci[:], T.cand[:], "cand", 131072, w=("ci",))
+    dma("y", T.inW[:, 0:256], T.want[:], "want", 65536, w=["inW0_%d" % h for h in range(NP)])
+    dma("y", T.featW[:, W // 2:W], T.feat[:, W // 2:W], "feat", 524288, w=("feat",))
+    dma("y", T.mkb[:], T.mkey[:], "mkey", 65536, w=("mkb",))
+    dma("y", T.moi[:], T.mobj[:], "mobj", 131072, w=("moi",))
+    dma("y", T.lai[:], T.last[:], "last", 8192, w=("lai",))
+    for q, (a, e) in enumerate(zip(KQ, KQ[1:])):
+        dma("y", T.kidi[:, a:e], T.kids[:, a:e], "k%d" % q, 512 * (e - a), w=("kidi%d" % q,))
 
-    iota(T.i5[:], [[0, 16]], 0, 1, "i5")
-    iota(T.i2[:], [[1, 16]], 128, -1, "i2")
-    iota(T.i1[:], [[16, 8], [0, 16]], 15, -1, "i1")
-    iota(T.i4[:], [[1, 16]], 0, 0, "i4")
-    iota(T.i3[:], [[1, 16]], 0, 1, "i3")
-    iota(T.i6[:], [[256, 16]], 0, 0, "i6")
-    iota(T.Kc[:], [[0, 16], [4096, 16]], 2048, 0, "Kc", allow_small_or_imprecise_dtypes=True)
-    iota(T.idW[:], [[1, W + 16]], 0, 0, "idW", allow_small_or_imprecise_dtypes=True)
-    fill(T.LH[:], 0.0, w=("LH",))
-    ts(T.i2b[:], T.i2[:], 15, None, ALU.bitwise_and, None, ("i2",), ("i2b",))
-    ts(T.bi[:], T.i5[:], 15, None, ALU.bitwise_and, None, ("i5",), ("bi",))
-    ts(T.i1b[:], T.i1[:], 4, None, ALU.arith_shift_right, None, ("i1",), ("i1b",))
-    ts(T.ib[:, 0:1], T.i5[:, 0:1], 4, 1, ALU.logical_shift_right, ALU.bitwise_and, ("i5",), ("ib0",))
-    ts(T.ib[:, 1:2], T.i5[:, 0:1], 3, 1, ALU.logical_shift_right, ALU.bitwise_and, ("i5",), ("ib1",))
-    ts(T.dg[:], T.i2b[:], 0.0, None, ALU.is_equal, None, ("i2b",), ("dg",))
-    cp(T.exb[:], T.bi[:], ("bi",), ("exb",))
-    ts(T.blk[:], T.i1b[:], 0.0, None, ALU.is_equal, None, ("i1b",), ("blk",))
-    act(T.diag[:], T.dg[:].indirect(T.exb[:]), AF.Copy, ("dg", "exb"), ("diag",))
-    ts(T.b8[:], T.blk[:, 0::16], 65536.0, None, ALU.mult, None, ("blk",), ("b8",))
-    cp(C(M1), T.ib[:, 0:1], ("ib0",), ("m1",))
-    ts(C(M0), T.ib[:, 0:1], -1.0, 1.0, ALU.mult, ALU.add, ("ib0",), ("m0",))
-    ts(C(SCT), T.ib[:, 1:2], -1.0, 1.0, ALU.mult, ALU.add, ("ib1",), ("sct",))
-    ts(C(DUMP), T.bi[:, 0:1], float(W), None, ALU.add, None, ("bi",), ("dump",))
-    fill(C(CEN0), 2048.0, w=("cen0",))
+    small = dict(allow_small_or_imprecise_dtypes=True)
+    iota(16, T.i5[:], [[0, 16]], 0, 1, "i5")
+    iota(16, T.i2[:], [[1, 16]], 128, -1, "i2")
+    iota(128, T.i1[:], [[16, 8], [0, 16]], 15, -1, "i1")
+    iota(16, T.i4[:], [[1, 16]], 0, 0, "i4")
+    iota(16, T.i3[:], [[1, 16]], 0, 1, "i3")
+    fill(S, T.Kc[:], 0.0, w=("Kc",))
+    fill(S, T.Kc[32:33, :], -RC * RS, w=("Kc",))
+    iota(128, T.Kc[0:1, :], [[0, 8], [8192, 16]], 6144, 0, "Kc", **small)
+    iota(W + 16, T.idW[:], [[1, W + 16]], W, 0, "idW", **small)
+    fill(cy(1024), T.LH[:], 0.0, w=("LH",))
+    ts(S, T.i2b[:], T.i2[:], 15, None, ALU.bitwise_and, None, ("i2",), ("i2b",))
+    ts(S, T.bi[:], T.i5[:], 15, None, ALU.bitwise_and, None, ("i5",), ("bi",))
+    ts(cy(128), T.i1b[:], T.i1[:], 4, None, ALU.arith_shift_right, None, ("i1",), ("i1b",))
+    ts(S, T.ib[:, 0:1], T.i5[:, 0:1], 4, 1, ALU.logical_shift_right, ALU.bitwise_and, ("i5",), ("ib0",))
+    ts(S, T.ib[:, 1:2], T.i5[:, 0:1], 3, 1, ALU.logical_shift_right, ALU.bitwise_and, ("i5",), ("ib1",))
+    ts(S, T.dg[:], T.i2b[:], 0.0, None, ALU.is_equal, None, ("i2b",), ("dg",))
+    cp(S, T.exb[:], T.bi[:], ("bi",), ("exb",))
+    ts(cy(128), T.blk[:], T.i1b[:], 0.0, None, ALU.is_equal, None, ("i1b",), ("blk",))
+    act(ga(128), T.diag[:], T.dg[:].indirect(T.exb[:, 0:8]), AF.Copy, ("dg", "exb"), ("diag",))
+    ts(S, T.b8[:], T.blk[:, 0::16], RS, None, ALU.mult, None, ("blk",), ("b8",))
+    cp(S, C(M1), T.ib[:, 0:1], ("ib0",), ("m1",))
+    ts(S, C(M0), T.ib[:, 0:1], -1.0, 1.0, ALU.mult, ALU.add, ("ib0",), ("m0",))
+    ts(S, C(SCT), T.ib[:, 1:2], -1.0, 1.0, ALU.mult, ALU.add, ("ib1",), ("sct",))
+    ts(S, C(DUMP), T.bi[:, 0:1], 2.0 * W, None, ALU.add, None, ("bi",), ("dump",))
     for b in range(16):
-        act(T.LH[:, 129 * b:129 * b + 113:16], T.b8[:], AF.Copy, ("b8",), p=("LH",))
-    tt(T.If[:], T.blk[:], T.diag[:, 0:128], ALU.mult, ("blk", "diag"), ("If",))
-    cp(T.inC[:, 0:256], T.ci[:], ("ci",), ("inCa0", "inCb0"))
-    cp(T.I16[:], T.If[:], ("If",), ("I16",))
-    cp(T.IB[:], T.If[:], ("If",), ("IB",))
-    ts(T.IN[:], T.If[:], -1.0, None, ALU.mult, None, ("If",), ("IN",))
+        act(S, T.LH[:, 129 * b:129 * b + 113:16], T.b8[:], AF.Copy, ("b8",), p=("LH",))
+    tt(cy(256), T.IB[:], T.blk[:], T.diag[:], ALU.mult, ("blk", "diag"), ("IB",))
+    cp(S, T.I16[:], T.IB[:], ("IB",), ("I16",))
+    for nm, x in (("IN", -1.0), ("IN16", -1.0), ("INf", -1.0), ("IK", KS)):
+        ts(cy(128 if nm == "INf" else 64), T[nm][:], T.IB[:], x, None, ALU.mult, None, ("IB",), (nm,))
 
-    def expand(t, q, k):
-        out, nm = T.Wx[:, k::16], "inW%d" % t
-        if q == "v":
-            cp(out, inW(t), (nm,), p=("Wx",))
-        elif q == "s":
-            act(out, inW(t), AF.Copy, (nm,), p=("Wx",))
-        else:
-            op("g", g.affine_select, (out, inW(t), [[0, 256]], ALU.is_equal, 0.0, 0, 0), (nm,), p=("Wx",))
-    for k in range(16):
-        expand(0, "v" if k < KD else "s", k)
-    cp(T.wtf[:], T.wti[:], ("wti",), ("wtf",))
-    ts(T.wblk[:], T.blk[:], T.wtf[:], None, ALU.mult, None, ("blk", "wtf"), ("wblk",))
-    fill(T.R1[:], 1.0, w=("R1",))
-    fill(T.R1[:, 0::16], 0.0, p=("R1",))
-    act(T.R2[:], T.R1[:], AF.Copy, ("R1",), ("R2",), scale=2.0)
-    act(T.RZ[:], T.R1[:], AF.Copy, ("R1",), ("RZ",), scale=BIG)
-    act(T.RST[:], T.R1[:], AF.Copy, ("R1",), ("RST",), scale=-BIG, bias=BIG)
-    ts(C(BIT), C(SCT), 4097.0, -1.0, ALU.mult, ALU.add, ("sct",), ("bit",))
-    ts(C(CEN), C(SCT), 4096.0, 2048.0, ALU.mult, ALU.add, ("sct",), ("cen",))
-    ts(C(OFF), C(SCT), 4096.0, None, ALU.mult, None, ("sct",), ("off",))
-    cp(T.expl[:], T.i4[:], ("i4",), ("expl",))
-    fill(T.limA[:], 65536.0 * (LIM - 1), w=("limA",))
-    ts(T.pbb[:], T.bi[:], 16.0, None, ALU.mult, None, ("bi",), ("pbb",))
-    ts(T.i3b[:], T.i3[:], 15, None, ALU.bitwise_and, None, ("i3",), ("i3b",))
-    tt(T.pb[:], T.pbb[:], T.i6[:], ALU.add, ("pbb", "i6"), ("pb",))
-    ts(T.a1[:], T.i3b[:], -16384.0, 262144.0 + 4096.0, ALU.mult, ALU.add, ("i3b",), ("a1",))
-    ts(T.a2[:], T.i3b[:], 10.0, 4096.0, ALU.is_lt, ALU.mult, ("i3b",), ("a2",))
-    ts(T.a3[:], T.i3b[:], 4.0, 4096.0, ALU.is_lt, ALU.mult, ("i3b",), ("a3",))
-    tt(T.a4[:], T.a1[:], T.a2[:], ALU.add, ("a1", "a2"), ("a4",))
-    tt(T.CJ[:], T.a4[:], T.a3[:], ALU.add, ("a4", "a3"), ("CJ",))
-    act(T.CJ2[:], T.CJ[:].indirect(T.exb[:]), AF.Copy, ("CJ", "exb"), ("CJ2",), bias=2048.0)
-    cp(T.R16[:, :, 0:16], T.I16[:], ("I16",), p=("R16",))
-    cp(T.R16[:, :, 16:32], T.I16[:], ("I16",), p=("R16",))
+    def double(X, l0, l1, src, rs, nm, who):
+        for x, (a, b, k) in enumerate(((0, None, 1), (1, None, 1), (2, 0, 2), (4, 0, 4), (8, 0, 8))):
+            out, in_, r = X[:, l0:l1, a:a + k], src if b is None else X[:, l0:l1, 0:k], rs if b is None else [nm + str(y) for y in range(x)]
+            m = (l1 - l0) * k
+            if who[x] == "v":
+                cp(cy(m / 2), out, in_, r, (nm + str(x),))
+            elif who[x] == "s":
+                act(cy(m), out, in_, AF.Copy, r, (nm + str(x),))
+            else:
+                add("g", lambda out=out, in_=in_, k=k: g.affine_select(out, in_, [[0, l1 - l0], [0, k]], ALU.is_equal, 0.0, 0, 0), 180 + 2 * m * CY, r, (nm + str(x),))
+        return [nm + str(y) for y in range(5)]
+    xp = double(T.XP, 0, NS, T.IN[:, 0:NS], ("IN",), "XP", "vvvvv")
+    for h, (c0, c1) in enumerate(PARTS):
+        cp(cy(16 * NC), T.inC[:, CS * h:CS * h + 16 * NC], T.ci[:, 16 * c0:16 * c1], ("ci",), ("inC0_%d" % h,))
+    ts(S, T.wtf[:], T.wti[:], 1.0 / RS, None, ALU.mult, None, ("wti",), ("wtf",))
+    fill(cy(256), T.R2[:], 2.0, w=("R2",))
+    fill(S, T.R2[:, 0::16], 0.0, p=("R2",))
+    act(cy(256), T.RN[:], T.R2[:], AF.Copy, ("R2",), ("RN",), scale=-NONE / 2, bias=float(NONE))
+    act(cy(256), T.RST[:], T.R2[:], AF.Copy, ("R2",), ("RST",), scale=-BIG, bias=BIG)
+    ts(S, C(BIT), C(SCT), 4097.0, -1.0, ALU.mult, ALU.add, ("sct",), ("bit",))
+    ts(S, C(OFF), C(SCT), 4096.0, None, ALU.mult, None, ("sct",), ("off",))
+    cp(S, T.expl[:], T.i4[:], ("i4",), ("expl",))
+    ts(S, C(K0), C(M0), 1.0 / 64, None, ALU.mult, None, ("m0",), ("k0",))
+    ts(S, C(K1), C(M1), 1.0 / 64, None, ALU.mult, None, ("m1",), ("k1",))
+    for i in range(8 - YP, 8):
+        act(cy(128), T["F%d" % (i + 1)][:], T.IB[:], AF.Copy, ("IB",), p=("F",), scale=float(i + 1))
+    fill(S, T.limA[:], RS * (LIM - 1), w=("limA",))
+    fill(S, T.ob[:], 1.0, w=("ob",))
+    fill(cy(128), T.ones[:], 1.0, w=("ones",))
+    ts(S, T.i3b[:], T.i3[:], 15, None, ALU.bitwise_and, None, ("i3",), ("i3b",))
+    ts(S, T.a0[:], T.i3[:], 14, None, ALU.bitwise_and, None, ("i3",), ("a0",))
+    ts(S, T.a2[:], T.i3b[:], 4.0, -2.0, ALU.is_ge, ALU.mult, ("i3b",), ("a2",))
+    ts(S, T.a3[:], T.i3b[:], 10.0, -2.0, ALU.is_ge, ALU.mult, ("i3b",), ("a3",))
+    tt(S, T.a1[:], T.a0[:], T.i3b[:], ALU.add, ("a0", "i3b"), ("a1",))
+    tt(S, T.a4[:], T.a2[:], T.a3[:], ALU.add, ("a2", "a3"), ("a4",))
+    tt(S, T.a5[:], T.a1[:], T.a4[:], ALU.add, ("a1", "a4"), ("a5",))
+    ts(S, T.CJ[:], T.a5[:], 4096.0, None, ALU.mult, None, ("a5",), ("CJ",))
+    act(ga(256), T.CJ2[:], T.CJ[:].indirect(T.exb[:]), AF.Copy, ("CJ", "exb"), ("CJ2",), bias=2048.0)
+    cp(S, T.R16[:, :, 0:16], T.I16[:], ("I16",), p=("R16",))
+    cp(S, T.R16[:, :, 16:32], T.I16[:], ("I16",), p=("R16",))
     for s in range(2):
-        cp(T.S4[:, :, s, :], T.R16[:, 1 - s::2, 0:16], ("R16",), p=("S4",))
+        cp(S, T.S4[:, :, s, :], T.R16[:, 1 - s::2, 0:16], ("R16",), p=("S4",))
     for e, m, nm in ((0, M0, "m0"), (1, M1, "m1")):
-        ts(T.PM[:, 384 * e:384 * e + 128], T.I16[:], C(m), None, ALU.mult, None, ("I16", nm), p=("PM",))
-        ts(T.PM[:, 128 + 128 * e:256 + 128 * e], T.S4[:], C(m), None, ALU.mult, None, ("S4", nm), p=("PM",))
+        ts(S, T.PM[:, 384 * e:384 * e + 128], T.I16[:], C(m), None, ALU.mult, None, ("I16", nm), p=("PM",))
+        ts(S, T.PM[:, 128 + 128 * e:256 + 128 * e], T.S4[:], C(m), None, ALU.mult, None, ("S4", nm), p=("PM",))
+    ts(cy(256), T.PK[:], T.PM[:], KS, None, ALU.mult, None, ("PM",), ("PK",))
     for b in range(16):
-        cp(T.SH[:, 128 * b:128 * b + 128], T.R16[:, :, b:b + 16], ("R16",), p=("SH",))
+        cp(S, T.SH[:, 128 * b:128 * b + 128], T.R16[:, :, b:b + 16], ("R16",), p=("SH",))
 
-    def flip_calls(src, ns, X, XT, nx):
-        return [lambda: ts(X[:, :, 0:16], src, C(M0), None, ALU.mult, None, (ns, "m0"), p=(nx,)),
-                lambda: ts(X[:, :, 16:32], src, C(M1), None, ALU.mult, None, (ns, "m1"), p=(nx,)),
-                lambda: op("v", v.transpose, (XT[:], X[:]), (nx,), (nx + "T",))]
-
-    def halves(out, XT, nx, w):
-        mm(out, T.I16[:], XT[:, :, 0:16], True, False, ("I16", nx + "T"), w)
-        mm(out, T.I16[:], XT[:, :, 16:32], False, True, ("I16", nx + "T"), w)
-    cp(T.mk16[:], T.mkb[:], ("mkb",), ("mk16",))
-    ts(T.mo16[:], T.moi[:], 2048.0, None, ALU.subtract, None, ("moi",), ("mo16",))
-    for ps, src in (("pA", "mk16"), ("pB", "mo16")):
+    def flip(src, ns, X, XT, nx, c0=0, c1=16, sub=0.0):
+        k = 16 * (c1 - c0)
+        ts(cy(k), X[:, c0:c1, 0:16], src, sub, C(M0), ALU.subtract, ALU.mult, (ns, "m0"), p=(nx,))
+        ts(cy(k), X[:, c0:c1, 16:32], src, sub, C(M1), ALU.subtract, ALU.mult, (ns, "m1"), p=(nx,))
+        tr(cy(k), XT[:, c0:c1, :], X[:, c0:c1, :], (nx,), (nx + "T",))
+    cp(cy(128), T.mk16[:], T.mkb[:], ("mkb",), ("mk16",))
+    ts(cy(256), T.mo16[:], T.moi[:], 2048.0, None, ALU.subtract, None, ("moi",), ("mo16",))
+    for ps, src in (("pv1", "mk16"), ("pL", "mo16")):
         for b in range(16):
-            op("t", te.matmul, (T[ps][:, b:256:16], T.SH[:, 128 * b:128 * b + 128], T[src][:, b::16], True, True), ("SH", src), p=(ps,))
-    for f in flip_calls(T.pA[:, 0:256], "pA", T.X, T.XT, "X") + flip_calls(T.pB[:, 0:256], "pB", T.Y, T.YT, "Y"):
-        f()
-    halves(T.pA[:, 0:256], T.XT, "X", "pA")
-    halves(T.pB[:, 0:256], T.YT, "Y", "pB")
-    ts(T.LX[:, 0:16], T.lai[:], C(M0), None, ALU.mult, None, ("lai", "m0"), p=("LX",))
-    ts(T.LX[:, 16:32], T.lai[:], C(M1), None, ALU.mult, None, ("lai", "m1"), p=("LX",))
-    op("v", v.transpose, (T.LT[:], T.LX[:]), ("LX",), ("LT",))
-    tt(T.prev0[:], T.LT[:, 0:16], T.LT[:, 16:32], ALU.add, ("LT",), ("prev0",))
-    scan(T.dsum[:], T.R2[:], T.diag[:], ALU.mult, ALU.add, ("R2", "diag"), "dsum")
-    ts(C(THR), T.dsum[:, 15:16], 2.0, None, ALU.mult, None, ("dsum",), ("thr",))
-    ts(T.offc[:], T.dg[:], 0.0, C(OFF), ALU.mult, ALU.add, ("dg", "off"), ("offc",))
-    act(T.MK[:], T.pA[:, 0:256], AF.Copy, ("pA",), ("MK",))
-    tt(T.pM[:, 0:256], T.pB[:, 0:256], T.CJ2[:], ALU.add, ("pB", "CJ2"), ("pM",))
-    fill(T.ones[:], 1.0, w=("ones",))
+            mm(16, T[ps][:, 0:8, b::16], T.SH[:, 128 * b:128 * b + 128], T[src][:, b::16], True, True, ("SH", src), ps, part=True)
+    flip(T.pv1[:, 0:8, :], "pv1", T.X, T.XT, "X")
+    flip(T.pL[:, 0:8, :], "pL", T.Y, T.YT, "Y")
+    for e, (l, nl, XT, nx) in enumerate((T.IK, "IK", T.XT, "XT") if x < 2 else (T.IN16, "IN16", T.YT, "YT") for x in range(4)):
+        mm(256, T.pv1[:, 0:8, :], l[:], XT[:, :, 16 * (e % 2):16 * (e % 2) + 16], e == 0, e == 3, (nl, nx), "pv1")
+    tt(cy(256), T.M[:], T.pv1[:, 0:8, :], T.CJ2[:], ALU.subtract, ("pv1", "CJ2"), ["M%d" % h for h in range(NP)])
+    ts(S, T.LX[:, 0:16], T.lai[:], C(M0), None, ALU.mult, None, ("lai", "m0"), p=("LX",))
+    ts(S, T.LX[:, 16:32], T.lai[:], C(M1), None, ALU.mult, None, ("lai", "m1"), p=("LX",))
+    tr(S, T.LT[:], T.LX[:], ("LX",), ("LT",))
+    tt(S, T.prev0[:], T.LT[:, 0:16], T.LT[:, 16:32], ALU.add, ("LT",), ("prev0",))
+    scan(S, T.th[:], T.R2[:, 0:16], T.dg[:], ALU.mult, ALU.add, ("R2", "dg"), ("th",))
+    ts(S, C(THR), T.th[:, 15:16], 2.0, None, ALU.mult, None, ("th",), ("thr",))
+    ts(cy(512), T.LW[:, 0:1024], T.LH[:, 0:1024], T.wtf[:], None, ALU.mult, None, ("LH", "wtf"), ("LW0",))
+    act(cy(1024), T.LW[:, 1024:2048], T.LH[:, 1024:2048], AF.Copy, ("LH", "wtf"), ("LW1",), scale=T.wtf[:])
+    for b in range(16):
+        act(cy(128), T.EX[:, 128 * b:128 * b + 128], T.blk[:], AF.Copy, ("blk", "dg"), p=("EX",), scale=T.dg[:, b:b + 1])
+    for b in range(16):
+        mm(256, T.pS[:, 0:8, :], T.LW[:, 128 * b:128 * b + 128], T.featW[:, 256 * b:256 * b + 256], b == 0, b == 15, ("LW1", "feat") if b > 7 else ("LW0", "feat0"), "pS")
+    tag_all = lambda s: [s + "%d" % h for h in range(NP)]
+    cp(cy(256), T.mi[:], T.pS[:, 0:8, :], ("pS",), tag_all("mi"))
+    ts(cy(256), T.mj[:], T.mi[:], 63, None, ALU.bitwise_and, None, tag_all("mi"), tag_all("mj"))
+    cp(cy(256), T.klb[:], T.mj[:], tag_all("mj"), ("klb",))
 
-    kbank = ["pC", "pW", "pA", "pB"]
+    def keys():
+        for i in range(8):
+            ps = "pX%d" % (i % 4)
+            for e in range(2):
+                b = 2 * i + e
+                mm(256, T[ps][:, 256 * e:256 * e + 256], T.EX[:, 128 * b:128 * b + 128], T.klb[:], True, True, ("EX", "klb"), ps, part=True)
+            if KEYQ[i] == "s":
+                act(cy(512), T.keyW[:, 512 * i:512 * i + 512], T[ps][:], AF.Copy, (ps,), p=("keyW",))
+            else:
+                cp(cy(512), T.keyW[:, 512 * i:512 * i + 512], T[ps][:], (ps,), p=("keyW",))
+    for q, (a, e) in enumerate(zip(KQ, KQ[1:])):
+        for x in range(a, e, 512):
+            cp(cy(512), T.kid[:, x:x + 512], T.kidi[:, x:x + 512], ("kidi%d" % q,), p=("kid",))
 
-    def keys(i0):
-        for i in range(i0, i0 + 4):
-            p = kbank[i % 4]
-            mm(T[p][:], T.wblk[:], T.featW[:, 512 * i:512 * i + 512], True, True, ("wblk", "feat"), p)
-        for i in range(i0, i0 + 4):
-            p = kbank[i % 4]
-            act(T.keyW[:, 512 * i:512 * i + 512], T[p][:], AF.Copy, (p,), p=("keyW",))
-
-    scq = []
-
-    def scatters():
-        scq.extend(range(15, -1, -1))
-
-    def scatter(k=1):
-        for i in range(min(k, len(scq))):
-            c = scq.pop(0)
-            tt(T.kid[:].indirect(T.s2u[:, 2 * c:2 * c + 1]), T.cf[:, 16 * c:16 * c + 16], T.offc[:], ALU.subtract, ("s2u", "cf0", "cf1", "offc"), ("kid",))
-
-    def limit():
-        mm(T.pC[:, 0:16], T.ones[:], T.cov[:], True, True, ("ones", "cov"), "pC")
-        return [lambda: op("v", v.tensor_reduce, (T.cs[:], T.pC[:, 0:16], AxisListType.X, ALU.add), ("pC",), ("cs",), kw=dict(negate=True)),
-                lambda: cp(T.csi[:], T.cs[:], ("cs",), ("csi",)),
-                lambda: ts(T.csa[:], T.csi[:], 15, None, ALU.bitwise_and, None, ("csi",), ("csa",)),
-                lambda: ts(T.limA[:], T.csa[:], 65536.0, 65536.0 * (LIM - 1), ALU.mult, ALU.add, ("csa",), ("limA",))]
-
-    def dist(c0, c1, nm, stop):
-        for b in range(16):
-            mm(T.pv[:, c0 // 2:c1 // 2, :], T.LH[:, 128 * b:128 * b + 128], T.A[:, c0:c1, 16 * b:16 * b + 16], False, stop and b == 15, ("LH", nm), "pv")
-    keys(0)
+    nx = [0]
     for t in range(STEPS):
-        iw, ia, ibn, final = "inW%d" % t, "inCa%d" % t, "inCb%d" % t, t == STEPS - 1
-        fw = 2 * W if t else W
-        fr = ("feat", "featd") if t else ("feat",)
-        mm(T.pv[:], T.IB[:], T.Kc[:], True, False, ("IB", "Kc"), "pv")
-        mm(T.pL[:], T.IB[:], T.Kc[:], True, False, ("IB", "Kc"), "pL")
-        for x, (c0, c1) in enumerate(CH):
-            tt(T.D[:, 256 * c0:256 * c1], T.featW[:, 0:fw].indirect(T.inC[:, 272 * t + 16 * c0:272 * t + 16 * c1]), T.Wx[:, 256 * c0:256 * c1], ALU.subtract,
-               fr + ("Wx", ia) + ((ibn,) if c1 > 8 else ()), ("D%d" % x,))
-            if x == XF:
-                ts(T.G[:], inC(t), C(CEN if t else CEN0), None, ALU.subtract, None, (ia, ibn, "cen" if t else "cen0"), ("G",))
-                scatter()
-                op("v", v.transpose, (T.GT[:], T.G[:]), ("G",), ("GT",))
-            if x == 0:
-                act(T.raw[:], T.featW[:, 0:fw].indirect(T.inC[:, 272 * t + 16 * OWN:272 * t + 256]), AF.Copy, fr + (ibn,), ("raw",))
-                mm(T.pX[:], T.IB[:], T.raw[:], True, False, ("IB", "raw"), "pX")
-                mm(T.pX[:], T.IN[:], T.Wx[:, 256 * OWN:4096], False, True, ("IN", "Wx"), "pX")
-            act(T.A[:, c0:c1, :], T.D[:, 256 * c0:256 * c1], AF.Abs, ("D%d" % x,), ("A%d" % x,))
-            if x == 1:
-                act(T.A[:, OWN:16, :], T.pX[:], AF.Abs, ("pX",), ("A9",))
-            if x == 2:
-                act(T.Lp[:], T.pL[:], AF.Identity, ("pL", "limA"), ("Lp",), bias=T.limA[:])
-            if x == len(CH) - 1 and not final:
-                act(T.D[:, 256 * OWN:4096], T.pX[:], AF.Abs, ("pX",), ("D9",))
-            if x == XF:
-                for p, e in (("pL", True), ("pv", False)):
-                    for c in range(2):
-                        for s in range(2):
-                            o = 256 * c + 128 * s
-                            mm(T[p][:, :, 16 * c:16 * c + 16], T.PM[:, o:o + 128], T.GT[:, :, 16 * s:16 * s + 16], False, e and c + s == 2, ("PM", "GT"), p)
-            dist(c0, c1, "A%d" % x, x == len(CH) - 1)
-            if x == 1:
-                dist(OWN, 16, "A9", False)
-        if t == 0:
-            keys(4)
-            for q in range(4):
-                cp(T.kid[:, 1024 * q:1024 * q + 1024], T.kidi[:, 1024 * q:1024 * q + 1024], ("kidi%d" % q,), p=("kid",))
-        else:
-            scatter(NT)
-        tt(T.vm[:], T.pv[:], T.Lp[:], ALU.max, ("pv", "Lp"), ("vm",))
-        scatter()
-        scan(T.vI[:], T.RST[:], T.vm[:], ALU.max, ALU.min, ("RST", "vm"), "vI")
-        scatter()
-        ts(T.oa[:], last16(T.vI), 4095, None, ALU.bitwise_and, None, ("vI",), ("oa",))
-        oo = "outO%d" % t
+        final, q = t == STEPS - 1, 5 * t % 16
+        for h, (c0, c1) in enumerate(PARTS):
+            N = lambda s: s + "%d" % h
+            lag[0] = LAG * h
+            l0, l1, nl, o, hc = 16 * c0, 16 * c1, 16 * NC, CS * (NP * t + h), NC // 2
+            ls, lb, pr = slice(l0, l1), slice(c0, c1), slice(c0 // 2, c1 // 2)
+            iw, ic, pv = "inW%d_%d" % (t, h), "inC%d_%d" % (t, h), "pv%d" % (h % 2)
+            last16 = lambda b: b[:, l0 + 15:l1:16]
+            Wa = T.inW[:, 256 * t + l0:256 * t + l1]
+            WT = T.WT[0:nl, 128 * h:128 * h + 128]
+            mm(128, T[pv][0:nl, 0:4, :], Wa, T.IB[:], True, True, (iw, "IB"), pv)
+            (cp if WTQ == "v" else lambda *a: act(*a[:3], AF.Copy, *a[3:]))(cy(128), WT, T[pv][0:nl, 0:4, :], (pv,), (N("WT"),))
+            c = c0
+            for e, k in CH:
+                px, a = "pX%d" % (nx[0] % 4), 16 * (c - c0)
+                nx[0] += 1
+                raw, src = T.raw[:, 256 * c:256 * (c + k)], T.featW[:].indirect(T.inC[:, o + a:o + a + 16 * k])
+                if e == "v":
+                    cp(ga(256 * k), raw, src, ("feat", "feat0", ic), ("raw%d" % c,))
+                else:
+                    act(ga(256 * k), raw, src, AF.Copy, ("feat", "feat0", ic), ("raw%d" % c,))
+                mm(256 * k, T[px][:, 0:256 * k], WT, T.XP[0:nl, a:a + 16 * k, :], True, False, [N("WT")] + xp, px)
+                mm(256 * k, T[px][:, 0:256 * k], T.IB[:], raw, False, True, ("IB", "raw%d" % c), px)
+                act(cy(256 * k), T.A[:, c:c + k, :], T[px][:, 0:256 * k], AF.Abs, (px,), ["A%d" % y for y in range(c, c + k)])
+                c += k
+            if t == h == 0:
+                keys()
+            ts(cy(nl / 2), T.G[:, pr, :], T.inC[:, o:o + nl], 2048.0, None, ALU.subtract, None, (ic,), (N("G"),))
+            tr(cy(nl / 2), T.GT[:, pr, :], T.G[:, pr, :], (N("G"),), (N("GT"),))
+
+            def turned(ps, PM, nm, XT, nxt_, stop):
+                for e in range(2):
+                    for s in range(2):
+                        mm(8 * NC, T[ps][:, 0:hc, 16 * e:16 * e + 16], PM[:, 256 * e + 128 * s:256 * e + 128 * s + 128], XT[:, pr, 16 * s:16 * s + 16], False, stop and e + s == 2, (nm, nxt_), ps)
+            for ps in (pv, "pL"):
+                mm(nl, T[ps][:, 0:hc, :], T.ob[0:33, :], T.Kc[0:33, 0:nl], True, False, ("ob", "Kc"), ps)
+                turned(ps, T.PM, "PM", T.GT, N("GT"), ps == "pL")
+            act(cy(nl), T.Lp[:, ls], T.pL[:, 0:hc, :], AF.Identity, ("pL", "limA"), (N("Lp"),), bias=T.limA[:])
+            for a, e in zip([0] + BATCH, BATCH):
+                for b in range(16):
+                    mm(16 * (e - a), T[pv][:, a // 2:e // 2, :], T.LH[:, 128 * b:128 * b + 128], T.A[:, c0 + a:c0 + e, 16 * b:16 * b + 16], False, b == 15 and e == NC,
+                       ["LH"] + ["A%d" % y for y in range(c0 + a, c0 + e)], pv)
+            tt(cy(nl), T.vm[:, ls], T[pv][:, 0:hc, :], T.Lp[:, ls], ALU.max, (pv, N("Lp")), (N("vm"),))
+            scan(cy(nl), T.vI[:, ls], T.RST[:, 0:nl], T.vm[:, ls], ALU.max, ALU.min, ("RST", N("vm")), (N("vI"),))
+            ts(S, T.yy[:, lb], last16(T.vI), 8191, None, ALU.bitwise_and, None, (N("vI"),), (N("yy"),))
+            ou, oo = T.outC[:, o + nl:o + nl + NC], "outO%d_%d" % (t, h)
+            ts(S, ou, T.yy[:, lb], 4096.0, None, ALU.subtract, None, (N("yy"),), (oo,))
+            if KGQ == "v":
+                cp(ga(nl), T.KG[:, ls], T.keyW[:].indirect(ou), ("keyW", oo), (N("KG"),))
+            else:
+                act(ga(nl), T.KG[:, ls], T.keyW[:].indirect(ou), AF.Copy, ("keyW", oo), (N("KG"),))
+            if not final:
+                ow = T.outW[:, 256 * t + l0:256 * t + l1]
+                tt(ga(nl), T.DW[:, ls], T.featW[:].indirect(ou), Wa, ALU.subtract, ("feat", "feat0", oo, iw), (N("DW"),))
+                act(cy(nl), ow, T.DW[:, ls], AF.Abs, (N("DW"),), ("outW%d_%d" % (t, h),))
+                send(T.inW[:, 256 * (t + 1) + l0:256 * (t + 1) + l1], ow, "w%d_%d" % (t + 1, h), ("outW%d_%d" % (t, h),), ("inW%d_%d" % (t + 1, h),), hlp, FLYW)
+            tr(cy(nl / 2), T.KT[:, pr, :], T.KG[:, ls], (N("KG"),), (N("KT"),))
+            mm(4 * nl, T.pS[:, 0:hc, :], T.INf[:], T.M[:, ls], True, False, ("INf", N("M")), "pS")
+            turned("pS", T.PK, "PK", T.KT, N("KT"), True)
+            act(cy(nl), T.AB[:, ls], T.pS[:, 0:hc, :], AF.Abs, ("pS",), (N("AB"),))
+            scan(cy(nl), T.es[:, ls], T.RN[:, 0:nl], T.AB[:, ls], ALU.max, ALU.min, ("RN", N("AB")), (N("es"),))
+            ev = last16(T.es)
+            two = lambda b, e: b[:, 2 * c0 + NC * e:2 * c0 + NC * e + NC]
+            both = lambda b: b[:, 2 * c0:2 * c1]
+            for e, bit in enumerate((16, 2)):
+                ts(S, two(T.x2, e), ev, 4095 + 4096 * bit + NONE, None, ALU.bitwise_and, None, (N("es"),), (N("x2%d_" % e),))
+            for e in range(2):
+                tt(S, two(T.l2, e), two(T.x2, e), T.yy[:, lb], ALU.min, (N("x2%d_" % e), N("yy")), p=(N("l2"),))
+            ts(S, both(T.l3), both(T.l2), 4095, None, ALU.bitwise_and, None, (N("l2"),), (N("l3"),))
+            cp(S, both(T.u2), both(T.l3), (N("l3"),), (N("u2"),))
+            if TOPQ == "v":
+                ts(ga(nl), T.top[:, ls], T.kid[:, 0:W].indirect(two(T.u2, 0)), C(SCT), C(BIT), ALU.mult, ALU.add, ("kid", N("u2"), "sct", "bit"), (N("top"),))
+            else:
+                act(ga(nl), T.top[:, ls], T.kid[:, 0:W].indirect(two(T.u2, 0)), AF.Identity, ("kid", N("u2"), "sct", "bit"), (N("top"),), bias=C(BIT), scale=C(SCT))
+            tt(ga(nl), T.cf[:, ls], T.kid[:, 0:W].indirect(two(T.u2, 1)), T.top[:, ls], ALU.max, ("kid", N("u2"), N("top")), (N("cf"),))
+            oc = "outC%d_%d" % (t, h)
+            if final:
+                ts(cy(nl), T.outF[:, ls], T.cf[:, ls], C(OFF), None, ALU.subtract, None, (N("cf"), "off"), (oc,))
+                send(T.inF[:, ls], T.outF[:, ls], "c%d_%d" % (t + 1, h), (oc,), (N("inF"),))
+                dma("y", T.yn[:, ls], T.inF[:, ls], N("yn"), 512 * nl, r=(N("inF"),))
+            else:
+                ts(cy(nl), T.outC[:, o:o + nl], T.cf[:, ls], C(OFF), None, ALU.subtract, None, (N("cf"), "off"), (oc,))
+                send(T.inC[:, o + NP * CS:o + NP * CS + CS], T.outC[:, o:o + CS], "c%d_%d" % (t + 1, h), (oc, oo), ("inC%d_%d" % (t + 1, h),))
+            prev, prn = (T.inC[:, o + nl:o + nl + NC], ic) if t else (T.prev0[:, lb], "prev0")
+            ts(S, T.pn[:, lb], prev, T.CJ[:, q:q + 1], None, ALU.add, None, (prn, "CJ"), (N("pn"),))
+            ts(S, T.na[:, lb], last16(T.vI), T.limA[:], (1 - RC) * RS, ALU.subtract, ALU.is_ge, (N("vI"), "limA"), (N("na"),))
+            tt(S, T.dn[:, lb], T.pS[:, 0:hc, q::16], T.pn[:, lb], ALU.subtract, ("pS", N("pn")), (N("dn"),))
+            tt(S, T.dn2[:, lb], T.dn[:, lb], T.na[:, lb], ALU.mult, (N("dn"), N("na")), (N("dn2"),))
+            tt(S, T.M[:, l0 + q:l1:16], T.M[:, l0 + q:l1:16], T.dn2[:, lb], ALU.add, (N("dn2"), N("M")), (N("M"),))
+            s1 = T.s1[:, 8 * h:8 * h + NC]
+            ts(S, T.ncd[:, lb], ev, float(NONE), C(DUMP), ALU.is_ge, ALU.mult, (N("es"), "dump"), (N("ncd"),))
+            tt(S, s1, T.yy[:, lb], T.ncd[:, lb], ALU.max, (N("yy"), N("ncd")), (N("s1"),))
+            ts(S, T.s1u[:, lb], s1, 4096.0, None, ALU.subtract, None, (N("s1"),), (N("s1u"),))
+            act(ga(nl), T.gl[:, ls], T.idW[:].indirect(T.s1u[:, lb]), AF.Copy, ("idW", N("s1u")), (N("gl"),))
+            tt(ga(nl), T.eq2[:, ls], s1.indirect(T.expl[:, 0:NC]), T.gl[:, ls], ALU.is_equal, (N("s1"), "expl", N("gl")), (N("eq2"),))
+            scan(cy(nl), T.dsum[:, ls], T.R2[:, 0:nl], T.eq2[:, ls], ALU.mult, ALU.add, ("R2", N("eq2")), (N("dsum"),))
+            ts(S, T.dd[:, lb], last16(T.dsum), C(THR), C(DUMP), ALU.is_ge, ALU.mult, (N("dsum"), "thr", "dump"), (N("dd"),))
+            tt(S, T.s2[:, lb], s1, T.dd[:, lb], ALU.max, (N("s1"), N("dd")), (N("s2"),))
+            ts(S, T.s2u[:, 2 * c0:2 * c1:2], T.s2[:, lb], 4096.0, None, ALU.subtract, None, (N("s2"),), (N("s2u"),))
+        lag[0] = 0.0
         if not final:
-            ts(T.kk[:], last16(T.vI), 12, 15, ALU.logical_shift_right, ALU.bitwise_and, ("vI",), ("kk",))
-        scatter()
-        cp(outO(t), T.oa[:], ("oa",), (oo,))
-        if not final:
-            tt(T.po[:], T.kk[:], T.pb[:], ALU.add, ("kk", "pb"), ("po",))
-        scatter()
-        tt(T.ky[:], T.keyW[:].indirect(outO(t)), T.diag[:], ALU.mult, ("keyW", oo, "diag"), ("ky",))
-        if not final:
-            cp(T.pu[:], T.po[:], ("po",), ("pu",))
-            act(outW(t), T.D[:].indirect(T.pu[:]), AF.Abs, tuple("D%d" % x for x in range(len(CH))) + ("D9", "pu"), ("outW%d" % t,))
-            send(inW(t + 1), outW(t), "w%d" % (t + 1), ("outW%d" % t,))
-        scatter()
-        scan(T.ks[:], T.R1[:], T.ky[:], ALU.mult, ALU.add, ("R1", "ky"), "ks")
-        scatter()
-        ts(T.key[:], last16(T.ks), 63, None, ALU.bitwise_and, None, ("ks",), ("key",))
-        scatter()
-        tt(T.eq[:], T.key[:].indirect(T.expl[:]), T.MK[:], ALU.is_equal, ("key", "expl", "MK"), ("eq",))
-        scatter()
-        tt(T.em[:], T.eq[:], T.pM[:, 0:256], ALU.mult, ("eq", "pM"), ("em",))
-        scatter()
-        scan(T.es[:], T.RZ[:], T.em[:], ALU.min, ALU.max, ("RZ", "em"), "es")
-        scatter(16)
-        ev = last16(T.es)
-        ts(T.eo[:], ev, 4095, None, ALU.bitwise_and, None, ("es",), ("eo",))
-        ts(T.sT[:], ev, 13, 1, ALU.logical_shift_right, ALU.bitwise_and, ("es",), ("sT",))
-        ts(T.sL[:], ev, 12, 1, ALU.logical_shift_right, ALU.bitwise_and, ("es",), ("sL",))
-        tt(T.de[:], T.eo[:], T.oa[:], ALU.subtract, ("eo", "oa"), ("de",))
-        q = 5 * t % 16
-        pr, prn = (inP(t), ibn) if t else (T.prev0[:], "prev0")
-        ts(T.ncd[:], ev, 1.0, C(DUMP), ALU.is_lt, ALU.mult, ("es", "dump"), ("ncd",))
-        tt(T.dk[:], T.key[:], T.MK[:, q::16], ALU.subtract, ("key", "MK"), ("dk",))
-        tt(T.tT[:], T.sT[:], T.de[:], ALU.mult, ("sT", "de"), ("tT",))
-        tt(T.tL[:], T.sL[:], T.de[:], ALU.mult, ("sL", "de"), ("tL",))
-        ts(T.pn[:], pr, T.CJ[:, q:q + 1], None, ALU.add, None, (prn, "CJ"), ("pn",))
-        ts(T.na[:], last16(T.vI), T.limA[:], 65536.0, ALU.subtract, ALU.is_ge, ("vI", "limA"), ("na",))
-        tt(T.l2[:, 0:16], T.tT[:], T.oa[:], ALU.add, ("tT", "oa"), p=("l2",))
-        tt(T.l2[:, 16:32], T.tL[:], T.oa[:], ALU.add, ("tL", "oa"), p=("l2",))
-        tt(T.s1[:], T.oa[:], T.ncd[:], ALU.max, ("oa", "ncd"), ("s1",))
-        tt(T.dk2[:], T.dk[:], T.na[:], ALU.mult, ("dk", "na"), ("dk2",))
-        cp(T.u2[:], T.l2[:], ("l2",), ("u2",))
-        for h in range(2):
-            act(T.top[:, 128 * h:128 * h + 128], T.kid[:, 0:W].indirect(T.u2[:, 8 * h:8 * h + 8]), AF.Identity, ("kid", "u2", "sct", "bit"), ("top%d" % h,),
-                bias=C(BIT), scale=C(SCT))
-        tt(T.dn[:], T.pn[:], T.pM[:, q:256:16], ALU.subtract, ("pn", "pM"), ("dn",))
-        cp(T.s1u[:], T.s1[:], ("s1",), ("s1u",))
-        tt(T.MK[:, q::16], T.MK[:, q::16], T.dk2[:], ALU.add, ("dk2",), ("MK",))
-        tt(T.dn2[:], T.dn[:], T.na[:], ALU.mult, ("dn", "na"), ("dn2",))
-        for h in range(2):
-            s = slice(128 * h, 128 * h + 128)
-            tt(T.cf[:, s], T.kid[:, 0:W].indirect(T.u2[:, 16 + 8 * h:24 + 8 * h]), T.top[:, s], ALU.max, ("kid", "u2", "top%d" % h), ("cf%d" % h,))
-        for h in range(2):
-            o = 272 * t + 128 * h
-            e = o + (144 if h and not final else 128)
-            if h:
-                tt(T.pM[:, q:256:16], T.dn2[:], T.pM[:, q:256:16], ALU.add, ("dn2",), ("pM",))
-            cp(T.outC[:, o:o + 128], T.cf[:, 128 * h:128 * h + 128], ("cf%d" % h,), ("oC%d" % h,))
-            send(T.inC[:, o + 272:e + 272], T.outC[:, o:e], "ab"[h] + "%d" % (t + 1), ("oC%d" % h, oo))
-        if not final:
-            act(T.cov[:], T.ncd[:], AF.Sign, ("ncd",), ("cov",))
-        act(T.gl[:], T.idW[:].indirect(T.s1u[:]), AF.Copy, ("idW", "s1u"), ("gl",))
-        lim, wq = [], []
-        if not final:
-            lim = limit()
-            arrive("w%d" % (t + 1), nin, ("inW%d" % (t + 1),))
-            arrive("a%d" % (t + 1), nin, ("inCa%d" % (t + 1),))
-            arrive("b%d" % (t + 1), nin, ("inCb%d" % (t + 1),))
-            for k in range(KD, 16):
-                expand(t + 1, "s" if k < 16 - KG else "g", k)
-            wq = list(range(KD))
-        def fill_in():
-            if lim:
-                lim.pop(0)()
-            if wq:
-                expand(t + 1, "v", wq.pop(0))
-        fill_in()
-        tt(T.eq2[:], T.s1[:].indirect(T.expl[:]), T.gl[:], ALU.is_equal, ("s1", "expl", "gl"), ("eq2",))
-        fill_in()
-        scan(T.dsum[:], T.R2[:], T.eq2[:], ALU.mult, ALU.add, ("R2", "eq2"), "dsum")
-        fill_in()
-        ts(T.dd[:], last16(T.dsum), C(THR), C(DUMP), ALU.is_ge, ALU.mult, ("dsum", "thr", "dump"), ("dd",))
-        fill_in()
-        tt(T.s2[:], T.s1[:], T.dd[:], ALU.max, ("s1", "dd"), ("s2",))
-        fill_in()
-        cp(T.s2u[:, 0::2], T.s2[:], ("s2",), ("s2u",))
-        scatters()
-        while wq:
-            fill_in()
-        if not final:
-            scatter()
-    calls = [lambda: tt(T.mo16[:], T.pM[:, 0:256], T.CJ2[:], ALU.subtract, ("pM", "CJ2"), ("mo16",)),
-             lambda: ts(T.mk16[:], T.MK[:], 1.0 / 64, None, ALU.mult, None, ("MK",), ("mk16",))]
-    for f in calls + flip_calls(T.mo16[:], "mo16", T.X, T.XT, "X") + flip_calls(T.mk16[:], "mk16", T.Y, T.YT, "Y"):
-        scatter()
-        f()
+            act(S, T.cov[:], T.ncd[:], AF.Sign, ["ncd%d" % h for h in range(NP)], ("cov", "cs"), scale=-1.0, accum_out=T.cs[:])
+            mm(256, T.pL[:, 0, 0:1], T.ones[:], T.cs[:], True, True, ("ones", "cs"), "pL")
+            cp(S, T.csi[:], T.pL[:, 0, 0:1], ("pL",), ("csi",))
+            ts(S, T.csa[:], T.csi[:], 15, None, ALU.bitwise_and, None, ("csi",), ("csa",))
+            ts(S, T.limA[:], T.csa[:], RS, RS * (LIM - 1), ALU.mult, ALU.add, ("csa",), ("limA",))
+        for h, (c0, c1) in enumerate(PARTS):
+            for c in range(c1 - 1, c0 - 1, -1):
+                a = CS * (NP * t + h) + 16 * (c - c0)
+                src = T.outF[:, 16 * c:16 * c + 16] if final else T.outC[:, a:a + 16]
+                cp((60 + 16 * SCAT) * CY, T.kid[:].indirect(T.s2u[:, 2 * c:2 * c + 1]), src, ("s2u%d" % h, "outC%d_%d" % (t, h)), ("kid",))
+    for h, (c0, c1) in enumerate(PARTS):
+        N = lambda s: s + "%d" % h
+        ls, nl = slice(16 * c0, 16 * c1), 16 * NC
+        ts(cy(nl), T.mi[:, ls], T.M[:, ls], 1.0 / KS, 0.25, ALU.mult, ALU.add, (N("M"),), (N("mi"),))
+        ts(cy(nl), T.mn[:, ls], T.M[:, ls], -1.0, None, ALU.mult, None, (N("M"),), (N("mn"),))
+        ts(cy(nl), T.mj[:, ls], T.mn[:, ls], 4095, None, ALU.bitwise_and, None, (N("mn"),), (N("mj"),))
+        for src, ns, X, XT, nm, sub, ms in ((T.mj, "mj", T.X, T.XT, "X", 2048.0, (M0, M1)), (T.mi, "mi", T.Y, T.YT, "Y", 0.0, (K0, K1))):
+            for e, m in enumerate(ms):
+                ts(cy(nl), X[:, c0:c1, 16 * e:16 * e + 16], src[:, ls], sub, C(m), ALU.subtract, ALU.mult, (N(ns), "m0", "m1", "k0", "k1", nm + "T"), (N(nm + "%d_" % e),))
+            tr(cy(nl), XT[:, c0:c1, :], X[:, c0:c1, :], (N(nm + "0_"), N(nm + "1_")), (N(nm + "T"),))
     for b in range(16):
         sh = T.SH[:, 128 * (-b % 16):128 * (-b % 16) + 128]
-        for e, (XT, nx, o) in enumerate(((T.XT, "XT", 0), (T.XT, "XT", 16), (T.YT, "YT", 0), (T.YT, "YT", 16))):
-            op("t", te.matmul, (T.pA[:, b:256:16], sh, XT[:, :, o + b], e == 0, e == 3), ("SH", nx), p=("pA",))
-    scatter(16)
-    yb = ["pB", "pC", "pW", "pX"]
-    for i in range(1, 5):
-        act(T[yb[i - 1]][:], T.kid[:, 512 * i:512 * i + 512], AF.Copy, ("kid",), (yb[i - 1],), scale=float(i + 1))
-    arrive("a%d" % STEPS, nin, ("inCa%d" % STEPS,))
-    arrive("b%d" % STEPS, nin, ("inCb%d" % STEPS,))
-    tt(T.acc[:], T.kid[:, 0:512], T[yb[0]][:], ALU.add, ("kid", yb[0]), ("acc0", "acc1"))
-    ts(T.yno[:], inC(STEPS), C(OFF), None, ALU.subtract, None, ("inCa%d" % STEPS, "inCb%d" % STEPS, "off"), ("yno",))
-    dma("y", T.yn[:], T.yno[:], "yn", r=("yno",))
-    act(T.ymo[:], T.pA[:, 0:256], AF.Copy, ("pA",), ("ymo",), scale=64.0, bias=131072.0)
-    dma("s", T.ymu[:], T.ymo[:], "ymu", r=("ymo",))
-    for i in range(2, 8):
-        p = yb[(i - 1) % 4]
-        if i > 4:
-            act(T[p][:], T.kid[:, 512 * i:512 * i + 512], AF.Copy, ("kid",), (p,), scale=float(i + 1))
-        for h in range(2):
-            s, a = slice(256 * h, 256 * h + 256), "acc%d" % h
-            tt(T.acc[:, s], T.acc[:, s], T[p][:, s], ALU.add, (a, p), (a,))
-    dma("y", T.yd[:], T.acc[:], "yd", r=("acc0", "acc1"))
-    finish("g")
+        for e, (XT, nm) in enumerate(((T.XT, "XT"), (T.XT, "XT"), (T.YT, "YT"), (T.YT, "YT"))):
+            mm(16, T.pX0[:, b:256:16], sh, XT[:, :, 16 * (e % 2) + b], e == 0, e == 3, ["SH"] + tag_all(nm), "pX0", part=True)
+    act(cy(256), T.ymo[:], T.pX0[:, 0:256], AF.Copy, ("pX0",), ("ymo",), scale=64.0, bias=131072.0)
+    dma("s", T.ymu[:], T.ymo[:], "ymu", 131072, r=("ymo",))
+    yb = ["pX1", "pX2", "pX3", "pL"]
+    for x in range(2):
+        col = lambda i: T.kid[:, 512 * i + 256 * x:512 * i + 256 * x + 256]
+        acc, na, pe = T.acc[:, 256 * x:256 * x + 256], "acc%d" % x, "pv%d" % x
+        for i in range(8 - YP, 8):
+            mm(1024, T[pe][:, 0:8, :], T["F%d" % (i + 1)][:], col(i), i == 8 - YP, i == 7, ("F", "kid"), pe)
+        for i in range(1, 8 - YP):
+            ps = yb[nx[0] % 4]
+            nx[0] += 1
+            out = T[ps][:, 0:256] if ps[1] in "TX" else T[ps][:, 0:8, :]
+            act(cy(256), out, col(i), AF.Copy, ("kid",), (ps,), scale=float(i + 1))
+            tt(cy(256), acc, col(0) if i == 1 else acc, out, ALU.add, ("kid" if i == 1 else na, ps), (na,))
+        if YP:
+            tt(cy(256), acc, acc, T[pe][:, 0:8, :], ALU.add, (na, pe), (na,))
+        dma("ys"[x], T.yd[:, 256 * x:256 * x + 256], acc, "yd%d" % x, 131072, r=(na,))
+    emit(g, T, ops, order(ops))

@@ -2,13 +2,18 @@ from concourse.mybir import AluOpType as ALU, ActivationFunctionType as AF
 
 STEPS, W, L, LIM = 8, 4096, 256, 60
 PARTS = [(8, 16), (0, 8)]
-CH = [("v", 2), ("s", 2), ("v", 2), ("s", 2)]
+NX, WXQ, SHQ = 128, "vvvvvvvvvvvvgggg", "vsvsvsvsvsvsvsvs"
+CH = [[("f", 2)], [("s", 2)], [("f", 2)], [("s", 2)]]
 BATCH = [4, 8]
 BIG, NONE, RS, KS, RC = float(2 ** 26), 2 ** 17, float(2 ** 17), float(2 ** 18), 120
-LAG, RELAY, FLYW, KEYQ = 2000.0, False, 2600.0, "svsvsvsv"
+JM, JW, DWQ, LAGJ, KIDQ = range(8), (), "s", 0.0, "gggggvgv"
+KB, ENDQ, LAGW = ["pX2", "pX3", "pS", "pv1"], "", 0.0
+LAG, RELAY, FLYW, KEYQ = 1.0, False, 2600.0, "svsvsvsv"
+LAGS, LOOKS, ORDER, STG = [1200.0, 1500.0, 1800.0, 2100.0, 2400.0, 2700.0, 3000.0], [2.0, 4.0, 7.0], {}, True
 NP, NC = len(PARTS), 16 // len(PARTS)
-WTQ, KGQ, TOPQ, HOPX, YP = "s", "s", "s", 210.0, 2
+WTQ, KGQ, TOPQ, HOPX, YP = "s", "v", "s", 210.0, 2
 KQ = [0, 1536, 3072, 3584, 4096]
+LOADS = ["wts", "feat0", "cand", "want", "feat", "mkey", "mobj", "last"]
 CS = 16 * NC + 8
 NS = 16 * NC
 CY, PE, GA, SCAT, HOP, FLY, LOAD, RATE, ROWS, LOOK = 0.85, 0.54, 1.56, 3.8, 210.0, 2600.0, 1600.0, 300.0, 80000.0, 3.0
@@ -16,14 +21,13 @@ CY, PE, GA, SCAT, HOP, FLY, LOAD, RATE, ROWS, LOOK = 0.85, 0.54, 1.56, 3.8, 210.
 _f, _b, _h, _i, _u = "float32", "bfloat16", "float16", "int32", "uint16"
 _t = lambda n, d: ("sbuf", [128, n], d)
 SCRATCH = {
-    "featW": _t(W, _b), "kidi": _t(W, _i), "kid": _t(W + 16, _f), "keyW": _t(W, _b), "idW": _t(W + 16, _f),
-    "A": ("sbuf", [128, 16, 256], _b), "raw": _t(W, _b),
-    "XP": ("sbuf", [128, NS, 16], _b), "WT": _t(128 * NP, _b),
-    "LH": _t(2048, _b), "LW": _t(2048, _b), "EX": _t(2048, _b), "SH": _t(2048, _h), "R16": ("sbuf", [128, 8, 32], _h),
+    "featW": _t(W, _b), "kidi": _t(W, _i), "kid": _t(W + 16 + NS, _f), "yc": _t(8, _f), "end": _t(W + 16, _f), "keyW": _t(W, _b), "idW": _t(W + 16, _f),
+    "A": ("sbuf", [128, 16, 256], _b), "raw": _t(W, _b), "Wx": _t(W, _b),
+    "LH": _t(144, _b), "LW": _t(144, _b), "EX": _t(2048, _b), "SH": _t(2048, _b), "R16": ("sbuf", [128, 8, 32], _b),
     "i1": _t(128, _i), "i1b": _t(128, _i), "i2": _t(16, _i), "i2b": _t(16, _i), "i3": _t(16, _i), "i3b": _t(16, _i), "i4": _t(16, _i), "i5": _t(16, _i),
     "bi": _t(16, _i), "exb": _t(16, _u), "dg": _t(16, _f), "ib": _t(8, _i), "a0": _t(16, _i), "a1": _t(16, _f), "a2": _t(16, _f), "a3": _t(16, _f), "a4": _t(16, _f), "a5": _t(16, _f),
     "blk": _t(128, _b), "diag": _t(128, _b), "I16": _t(128, _h), "IN16": _t(128, _h), "IB": _t(128, _b), "IN": _t(128, _b), "INf": _t(128, _f), "F7": _t(128, _f), "F8": _t(128, _f), "IK": _t(128, _b),
-    "ones": _t(128, _f), "b8": _t(8, _b), "Kc": _t(128, _b), "ob": _t(128, _b), "expl": _t(16, _u),
+    "ones": _t(128, _f), "Kc": _t(128, _b), "ob": _t(128, _b), "expl": _t(16, _u),
     "RST": _t(256, _f), "RN": _t(256, _f), "R2": _t(256, _f), "CJ": _t(16, _f), "CJ2": _t(256, _f), "col": _t(16, _f), "wti": _t(1, _i), "wtf": _t(1, _f),
     "ci": _t(256, _i), "mkb": _t(256, _b), "moi": _t(256, _i), "mk16": _t(256, _h), "mo16": _t(256, _h), "mi": _t(256, _i), "mj": _t(256, _i), "mn": _t(256, _i),
     "klb": _t(256, _b),
@@ -90,41 +94,43 @@ def make():
 
 
 def order(ops):
-    n = len(ops)
+    n, ns = len(ops), [o["ns"] for o in ops]
     post = [[] for i in range(n)]
     for i, o in enumerate(ops):
-        for j in o["pre"]:
-            post[j].append(i)
-    gap = lambda j, i: (ops[j]["lat"] + (HOP if ops[i]["q"] == ops[j]["q"] else HOPX)) if ops[i]["pre"][j] else 0.0
-    way = [0.0] * n
+        for j, sem in o["pre"].items():
+            post[j].append((i, ops[j]["lat"] + HOP if sem else 0.0))
+    way0 = [0.0] * n
     for i in range(n - 1, -1, -1):
-        way[i] = ops[i]["ns"] + max([gap(i, k) + way[k] for k in post[i]] + [ops[i]["lat"]])
-    way = [way[i] - ops[i]["lag"] for i in range(n)]
-    left, ready, done = [len(o["pre"]) for o in ops], [0.0] * n, [0.0] * n
-    free, cand, seq = {}, {}, []
-    for i, o in enumerate(ops):
-        free[o["q"]] = 0.0
-        cand.setdefault(o["q"], [])
-        if not left[i]:
-            cand[o["q"]].append(i)
-    while len(seq) < n:
-        now, q = min((max(free[q], min(ready[i] for i in c)), q) for q, c in cand.items() if c)
-        i = max(cand[q], key=lambda i: way[i] - LOOK * max(0.0, ready[i] - now))
-        if ready[i] > now:
-            fit = [k for k in cand[q] if max(now, ready[k]) + ops[k]["ns"] <= ready[i] + 40.0]
-            if fit:
-                i = max(fit, key=lambda k: way[k] - LOOK * max(0.0, ready[k] - now))
-        cand[q].remove(i)
-        seq.append(i)
-        done[i] = max(now, ready[i]) + ops[i]["ns"]
-        if q != "x":
-            free[q] = done[i]
-        for k in post[i]:
-            ready[k] = max(ready[k], done[i] + gap(i, k))
-            left[k] -= 1
-            if not left[k]:
-                cand[ops[k]["q"]].append(k)
-    return seq
+        way0[i] = ns[i] + max([d + way0[k] for k, d in post[i]] + [ops[i]["lat"]])
+
+    def run(lag, look):
+        way = [way0[i] - lag * ops[i]["lag"] for i in range(n)]
+        left, ready, end = [len(o["pre"]) for o in ops], [0.0] * n, 0.0
+        free, cand, seq = {o["q"]: 0.0 for o in ops}, {o["q"]: [] for o in ops}, []
+        for i, o in enumerate(ops):
+            if not left[i]:
+                cand[o["q"]].append(i)
+        while len(seq) < n:
+            now, q = min((max(free[q], min(ready[i] for i in c)), q) for q, c in cand.items() if c)
+            worth = lambda i: way[i] - look * max(0.0, ready[i] - now)
+            i = max(cand[q], key=worth)
+            if ready[i] > now:
+                i = max([k for k in cand[q] if max(now, ready[k]) + ns[k] <= ready[i] + 40.0] or [i], key=worth)
+            cand[q].remove(i)
+            seq.append(i)
+            done = max(now, ready[i]) + ns[i]
+            end = max(end, done + ops[i]["lat"])
+            if q != "x":
+                free[q] = done
+            for k, d in post[i]:
+                ready[k] = max(ready[k], done + d)
+                left[k] -= 1
+                if not left[k]:
+                    cand[ops[k]["q"]].append(k)
+        return end, seq
+    if n not in ORDER:
+        ORDER[n] = min(run(lag, look) for lag in LAGS for look in LOOKS)
+    return ORDER[n][1]
 
 
 def emit(g, T, ops, seq):
@@ -203,6 +209,14 @@ def rank_program(g, core, T, topo):
     def act(ns, out, a, f, r, w=(), p=(), **kw):
         add("s", lambda: sc.activation(out, a, f, **kw), ns, r, w, p)
 
+    def copy(e, k, out, a, r, w=(), p=(), fast=1.0):
+        if e == "v":
+            cp(cy(k * fast), out, a, r, w, p)
+        elif e == "s":
+            act(cy(k), out, a, AF.Copy, r, w, p)
+        else:
+            add("g", lambda: g.affine_select(out, a, [[0, k]], ALU.is_equal, 0.0, 0, 0), 180 + 2 * k * CY, r, w, p)
+
     def mm(k, out, l, rh, st, sp, r, w, part=False):
         if part:
             add("t", lambda: te.matmul(out, l, rh, st, sp), max(64, k) * PE, r, p=(w,))
@@ -226,17 +240,16 @@ def rank_program(g, core, T, topo):
         i = add("g", lambda: g.remote_dma(out, in_, T.sem[sem], T.sem.ls, pid, rid, mask), 400.0, r, sem=("ls", bin(mask).count("1")))
         add("x", None, fly, (), w, sem=(sem, nin), after=(i,))
     C = lambda j: T.col[:, j:j + 1]
-    M1, M0, SCT, BIT, DUMP, THR, OFF, K0, K1 = range(9)
+    M1, M0, SCT, BIT, DUMP, THR, OFF, K0, K1, YC = range(10)
     S = cy(16)
+    at = lambda t, c: 2 * CS * t + 16 * c + (16 if c >= NC else 0)
 
-    dma("y", T.wti[:], T.wts[:], "wts", 512, w=("wti",))
-    dma("y", T.featW[:, 0:W // 2], T.feat[:, 0:W // 2], "feat0", 524288, w=("feat0",))
-    dma("y", T.ci[:], T.cand[:], "cand", 131072, w=("ci",))
-    dma("y", T.inW[:, 0:256], T.want[:], "want", 65536, w=["inW0_%d" % h for h in range(NP)])
-    dma("y", T.featW[:, W // 2:W], T.feat[:, W // 2:W], "feat", 524288, w=("feat",))
-    dma("y", T.mkb[:], T.mkey[:], "mkey", 65536, w=("mkb",))
-    dma("y", T.moi[:], T.mobj[:], "mobj", 131072, w=("moi",))
-    dma("y", T.lai[:], T.last[:], "last", 8192, w=("lai",))
+    loads = {"wts": (T.wti[:], T.wts[:], 512, ("wti",)), "feat0": (T.featW[:, 0:W // 2], T.feat[:, 0:W // 2], 524288, ("feat0",)),
+             "cand": (T.ci[:], T.cand[:], 131072, ("ci",)), "want": (T.inW[:, 0:256], T.want[:], 65536, ["inW0_%d" % h for h in range(NP)]),
+             "feat": (T.featW[:, W // 2:W], T.feat[:, W // 2:W], 524288, ("feat",)), "mkey": (T.mkb[:], T.mkey[:], 65536, ("mkb",)),
+             "mobj": (T.moi[:], T.mobj[:], 131072, ("moi",)), "last": (T.lai[:], T.last[:], 8192, ("lai",))}
+    for nm in LOADS:
+        dma("y", loads[nm][0], loads[nm][1], nm, loads[nm][2], w=loads[nm][3])
     for q, (a, e) in enumerate(zip(KQ, KQ[1:])):
         dma("y", T.kidi[:, a:e], T.kids[:, a:e], "k%d" % q, 512 * (e - a), w=("kidi%d" % q,))
 
@@ -250,7 +263,7 @@ def rank_program(g, core, T, topo):
     fill(S, T.Kc[32:33, :], -RC * RS, w=("Kc",))
     iota(128, T.Kc[0:1, :], [[0, 8], [8192, 16]], 6144, 0, "Kc", **small)
     iota(W + 16, T.idW[:], [[1, W + 16]], W, 0, "idW", **small)
-    fill(cy(1024), T.LH[:], 0.0, w=("LH",))
+    fill(cy(128), T.LH[:], 0.0, w=("LH",))
     ts(S, T.i2b[:], T.i2[:], 15, None, ALU.bitwise_and, None, ("i2",), ("i2b",))
     ts(S, T.bi[:], T.i5[:], 15, None, ALU.bitwise_and, None, ("i5",), ("bi",))
     ts(cy(128), T.i1b[:], T.i1[:], 4, None, ALU.arith_shift_right, None, ("i1",), ("i1b",))
@@ -260,32 +273,21 @@ def rank_program(g, core, T, topo):
     cp(S, T.exb[:], T.bi[:], ("bi",), ("exb",))
     ts(cy(128), T.blk[:], T.i1b[:], 0.0, None, ALU.is_equal, None, ("i1b",), ("blk",))
     act(ga(128), T.diag[:], T.dg[:].indirect(T.exb[:, 0:8]), AF.Copy, ("dg", "exb"), ("diag",))
-    ts(S, T.b8[:], T.blk[:, 0::16], RS, None, ALU.mult, None, ("blk",), ("b8",))
+    ts(S, T.LH[:, 15:143:16], T.blk[:, 0::16], RS, None, ALU.mult, None, ("blk",), ("LH",))
     cp(S, C(M1), T.ib[:, 0:1], ("ib0",), ("m1",))
     ts(S, C(M0), T.ib[:, 0:1], -1.0, 1.0, ALU.mult, ALU.add, ("ib0",), ("m0",))
     ts(S, C(SCT), T.ib[:, 1:2], -1.0, 1.0, ALU.mult, ALU.add, ("ib1",), ("sct",))
     ts(S, C(DUMP), T.bi[:, 0:1], 2.0 * W, None, ALU.add, None, ("bi",), ("dump",))
-    for b in range(16):
-        act(S, T.LH[:, 129 * b:129 * b + 113:16], T.b8[:], AF.Copy, ("b8",), p=("LH",))
+    ts(S, C(YC), T.bi[:, 0:1], W + 16.0, None, ALU.add, None, ("bi",), ("ycc",))
+    ts(S, T.yc[:], T.i4[:, 0:8], 16.0, C(YC), ALU.mult, ALU.add, ("i4", "ycc"), ("yc",))
+    fill(S, T.kid[:, W:W + 16], 0.0, p=("kid",))
     tt(cy(256), T.IB[:], T.blk[:], T.diag[:], ALU.mult, ("blk", "diag"), ("IB",))
     cp(S, T.I16[:], T.IB[:], ("IB",), ("I16",))
     for nm, x in (("IN", -1.0), ("IN16", -1.0), ("INf", -1.0), ("IK", KS)):
         ts(cy(128 if nm == "INf" else 64), T[nm][:], T.IB[:], x, None, ALU.mult, None, ("IB",), (nm,))
 
-    def double(X, l0, l1, src, rs, nm, who):
-        for x, (a, b, k) in enumerate(((0, None, 1), (1, None, 1), (2, 0, 2), (4, 0, 4), (8, 0, 8))):
-            out, in_, r = X[:, l0:l1, a:a + k], src if b is None else X[:, l0:l1, 0:k], rs if b is None else [nm + str(y) for y in range(x)]
-            m = (l1 - l0) * k
-            if who[x] == "v":
-                cp(cy(m / 2), out, in_, r, (nm + str(x),))
-            elif who[x] == "s":
-                act(cy(m), out, in_, AF.Copy, r, (nm + str(x),))
-            else:
-                add("g", lambda out=out, in_=in_, k=k: g.affine_select(out, in_, [[0, l1 - l0], [0, k]], ALU.is_equal, 0.0, 0, 0), 180 + 2 * m * CY, r, (nm + str(x),))
-        return [nm + str(y) for y in range(5)]
-    xp = double(T.XP, 0, NS, T.IN[:, 0:NS], ("IN",), "XP", "vvvvv")
     for h, (c0, c1) in enumerate(PARTS):
-        cp(cy(16 * NC), T.inC[:, CS * h:CS * h + 16 * NC], T.ci[:, 16 * c0:16 * c1], ("ci",), ("inC0_%d" % h,))
+        cp(cy(16 * NC), T.inC[:, at(0, c0):at(0, c0) + 16 * NC], T.ci[:, 16 * c0:16 * c1], ("ci",), ("inC0_%d" % h,))
     ts(S, T.wtf[:], T.wti[:], 1.0 / RS, None, ALU.mult, None, ("wti",), ("wtf",))
     fill(cy(256), T.R2[:], 2.0, w=("R2",))
     fill(S, T.R2[:, 0::16], 0.0, p=("R2",))
@@ -310,16 +312,19 @@ def rank_program(g, core, T, topo):
     tt(S, T.a5[:], T.a1[:], T.a4[:], ALU.add, ("a1", "a4"), ("a5",))
     ts(S, T.CJ[:], T.a5[:], 4096.0, None, ALU.mult, None, ("a5",), ("CJ",))
     act(ga(256), T.CJ2[:], T.CJ[:].indirect(T.exb[:]), AF.Copy, ("CJ", "exb"), ("CJ2",), bias=2048.0)
-    cp(S, T.R16[:, :, 0:16], T.I16[:], ("I16",), p=("R16",))
-    cp(S, T.R16[:, :, 16:32], T.I16[:], ("I16",), p=("R16",))
+    cp(S, T.R16[:, :, 0:16], T.IB[:], ("IB",), p=("R16",))
+    cp(S, T.R16[:, :, 16:32], T.IB[:], ("IB",), p=("R16",))
+    for b in range(16):
+        if SHQ[b] == "v":
+            cp(S, T.SH[:, 128 * b:128 * b + 128], T.R16[:, :, b:b + 16], ("R16",), p=("SH",))
+        else:
+            act(cy(128), T.SH[:, 128 * b:128 * b + 128], T.R16[:, :, b:b + 16], AF.Copy, ("R16",), p=("SH",))
     for s in range(2):
         cp(S, T.S4[:, :, s, :], T.R16[:, 1 - s::2, 0:16], ("R16",), p=("S4",))
     for e, m, nm in ((0, M0, "m0"), (1, M1, "m1")):
         ts(S, T.PM[:, 384 * e:384 * e + 128], T.I16[:], C(m), None, ALU.mult, None, ("I16", nm), p=("PM",))
         ts(S, T.PM[:, 128 + 128 * e:256 + 128 * e], T.S4[:], C(m), None, ALU.mult, None, ("S4", nm), p=("PM",))
     ts(cy(256), T.PK[:], T.PM[:], KS, None, ALU.mult, None, ("PM",), ("PK",))
-    for b in range(16):
-        cp(S, T.SH[:, 128 * b:128 * b + 128], T.R16[:, :, b:b + 16], ("R16",), p=("SH",))
 
     def flip(src, ns, X, XT, nx, c0=0, c1=16, sub=0.0):
         k = 16 * (c1 - c0)
@@ -342,12 +347,11 @@ def rank_program(g, core, T, topo):
     tt(S, T.prev0[:], T.LT[:, 0:16], T.LT[:, 16:32], ALU.add, ("LT",), ("prev0",))
     scan(S, T.th[:], T.R2[:, 0:16], T.dg[:], ALU.mult, ALU.add, ("R2", "dg"), ("th",))
     ts(S, C(THR), T.th[:, 15:16], 2.0, None, ALU.mult, None, ("th",), ("thr",))
-    ts(cy(512), T.LW[:, 0:1024], T.LH[:, 0:1024], T.wtf[:], None, ALU.mult, None, ("LH", "wtf"), ("LW0",))
-    act(cy(1024), T.LW[:, 1024:2048], T.LH[:, 1024:2048], AF.Copy, ("LH", "wtf"), ("LW1",), scale=T.wtf[:])
+    ts(cy(128), T.LW[:], T.LH[:], T.wtf[:], None, ALU.mult, None, ("LH", "wtf"), ("LW",))
     for b in range(16):
         act(cy(128), T.EX[:, 128 * b:128 * b + 128], T.blk[:], AF.Copy, ("blk", "dg"), p=("EX",), scale=T.dg[:, b:b + 1])
     for b in range(16):
-        mm(256, T.pS[:, 0:8, :], T.LW[:, 128 * b:128 * b + 128], T.featW[:, 256 * b:256 * b + 256], b == 0, b == 15, ("LW1", "feat") if b > 7 else ("LW0", "feat0"), "pS")
+        mm(256, T.pS[:, 0:8, :], T.LW[:, 15 - b:143 - b], T.featW[:, 256 * b:256 * b + 256], b == 0, b == 15, ("LW", "feat" if b > 7 else "feat0"), "pS")
     tag_all = lambda s: [s + "%d" % h for h in range(NP)]
     cp(cy(256), T.mi[:], T.pS[:, 0:8, :], ("pS",), tag_all("mi"))
     ts(cy(256), T.mj[:], T.mi[:], 63, None, ALU.bitwise_and, None, tag_all("mi"), tag_all("mj"))
@@ -355,43 +359,85 @@ def rank_program(g, core, T, topo):
 
     def keys():
         for i in range(8):
-            ps = "pX%d" % (i % 4)
+            ps = KB[i % len(KB)]
             for e in range(2):
                 b = 2 * i + e
-                mm(256, T[ps][:, 256 * e:256 * e + 256], T.EX[:, 128 * b:128 * b + 128], T.klb[:], True, True, ("EX", "klb"), ps, part=True)
+                mm(256, T[ps][:, 256 * e:256 * e + 256] if ps[1] == "X" else T[ps][:, 8 * e:8 * e + 8, :], T.EX[:, 128 * b:128 * b + 128], T.klb[:], True, True, ("EX", "klb"), ps, part=True)
             if KEYQ[i] == "s":
                 act(cy(512), T.keyW[:, 512 * i:512 * i + 512], T[ps][:], AF.Copy, (ps,), p=("keyW",))
             else:
                 cp(cy(512), T.keyW[:, 512 * i:512 * i + 512], T[ps][:], (ps,), p=("keyW",))
     for q, (a, e) in enumerate(zip(KQ, KQ[1:])):
         for x in range(a, e, 512):
-            cp(cy(512), T.kid[:, x:x + 512], T.kidi[:, x:x + 512], ("kidi%d" % q,), p=("kid",))
+            if KIDQ[x // 512] == "v":
+                cp(cy(512), T.kid[:, x:x + 512], T.kidi[:, x:x + 512], ("kidi%d" % q,), p=("kid",))
+            elif KIDQ[x // 512] == "s":
+                act(cy(512), T.kid[:, x:x + 512], T.kidi[:, x:x + 512], AF.Copy, ("kidi%d" % q,), p=("kid",))
+            else:
+                add("g", lambda x=x: g.affine_select(T.kid[:, x:x + 512], T.kidi[:, x:x + 512], [[0, 512]], ALU.is_equal, 0.0, 0, 0), 180 + 1024 * CY, ("kidi%d" % q,), p=("kid",))
 
+    def mounts(t, c0, c1, hs):
+        N, lb, q = lambda *s: [x + "%d" % h for x in s for h in hs], slice(c0, c1), 5 * t % 16
+        prev, prn = (T.inC[:, 2 * CS * t + 128 + c0:2 * CS * t + 128 + c1], N("inC%d_" % t)) if t else (T.prev0[:, lb], ["prev0"])
+        ts(S, T.pn[:, lb], prev, T.CJ[:, q:q + 1], None, ALU.add, None, prn + ["CJ"], N("pn"))
+        ts(S, T.na[:, lb], T.vI[:, 16 * c0 + 15:16 * c1:16], T.limA[:], (1 - RC) * RS, ALU.subtract, ALU.is_ge, N("vI") + ["limA"], N("na"))
+        tt(S, T.dn[:, lb], T.pS[:, c0 // 2:c1 // 2, q::16], T.pn[:, lb], ALU.subtract, ["pS"] + N("pn"), N("dn"))
+        tt(S, T.dn2[:, lb], T.dn[:, lb], T.na[:, lb], ALU.mult, N("dn", "na"), N("dm"))
+        tt(S, T.M[:, 16 * c0 + q:16 * c1:16], T.M[:, 16 * c0 + q:16 * c1:16], T.dn2[:, lb], ALU.add, N("dm", "M"), N("M"))
+
+    def writers(c0, c1, hs):
+        N, lb, ls, nl = lambda *s: [x + "%d" % h for x in s for h in hs], slice(c0, c1), slice(16 * c0, 16 * c1), 16 * (c1 - c0)
+        s1, last16 = T.s1[:, lb], lambda b: b[:, 16 * c0 + 15:16 * c1:16]
+        ts(S, T.ncd[:, lb], last16(T.es), float(NONE), C(DUMP), ALU.is_ge, ALU.mult, N("es") + ["dump"], N("ncd"))
+        tt(S, s1, T.yy[:, lb], T.ncd[:, lb], ALU.max, N("yy", "ncd"), N("s1_"))
+        ts(S, T.s1u[:, lb], s1, 4096.0, None, ALU.subtract, None, N("s1_"), N("s1u"))
+        act(ga(nl), T.gl[:, ls], T.idW[:].indirect(T.s1u[:, lb]), AF.Copy, ["idW"] + N("s1u"), N("gl"))
+        tt(ga(nl), T.eq2[:, ls], s1.indirect(T.expl[:, 0:c1 - c0]), T.gl[:, ls], ALU.is_equal, N("s1_", "gl") + ["expl"], N("eq2_"))
+        scan(cy(nl), T.dsum[:, ls], T.R2[:, 0:nl], T.eq2[:, ls], ALU.mult, ALU.add, ["R2"] + N("eq2_"), N("dsum"))
+        ts(S, T.dd[:, lb], last16(T.dsum), C(THR), C(DUMP), ALU.is_ge, ALU.mult, N("dsum") + ["thr", "dump"], N("dd"))
+        tt(S, T.s2[:, lb], s1, T.dd[:, lb], ALU.max, N("s1_", "dd"), N("s2_"))
+        ts(S, T.s2u[:, 2 * c0:2 * c1:2], T.s2[:, lb], 4096.0, None, ALU.subtract, None, N("s2_"), N("s2u"))
     nx = [0]
     for t in range(STEPS):
         final, q = t == STEPS - 1, 5 * t % 16
         for h, (c0, c1) in enumerate(PARTS):
             N = lambda s: s + "%d" % h
             lag[0] = LAG * h
-            l0, l1, nl, o, hc = 16 * c0, 16 * c1, 16 * NC, CS * (NP * t + h), NC // 2
+            l0, l1, nl, o, ob, hc = 16 * c0, 16 * c1, 16 * NC, at(t, c0), 2 * CS * t + 128 + c0, NC // 2
             ls, lb, pr = slice(l0, l1), slice(c0, c1), slice(c0 // 2, c1 // 2)
             iw, ic, pv = "inW%d_%d" % (t, h), "inC%d_%d" % (t, h), "pv%d" % (h % 2)
             last16 = lambda b: b[:, l0 + 15:l1:16]
             Wa = T.inW[:, 256 * t + l0:256 * t + l1]
-            WT = T.WT[0:nl, 128 * h:128 * h + 128]
-            mm(128, T[pv][0:nl, 0:4, :], Wa, T.IB[:], True, True, (iw, "IB"), pv)
-            (cp if WTQ == "v" else lambda *a: act(*a[:3], AF.Copy, *a[3:]))(cy(128), WT, T[pv][0:nl, 0:4, :], (pv,), (N("WT"),))
-            c = c0
-            for e, k in CH:
-                px, a = "pX%d" % (nx[0] % 4), 16 * (c - c0)
-                nx[0] += 1
-                raw, src = T.raw[:, 256 * c:256 * (c + k)], T.featW[:].indirect(T.inC[:, o + a:o + a + 16 * k])
-                if e == "v":
-                    cp(ga(256 * k), raw, src, ("feat", "feat0", ic), ("raw%d" % c,))
+            for k in range(16 if NX else 0):
+                out, src = T.Wx[:, 16 * l0 + k:16 * (l0 + NX):16], T.inW[:, 256 * t + l0:256 * t + l0 + NX]
+                if WXQ[k] == "v" or t == 0:
+                    cp(cy(NX / 2), out, src, (iw,), p=(N("Wx"),))
+                elif WXQ[k] == "s":
+                    act(cy(NX), out, src, AF.Copy, (iw,), p=(N("Wx"),))
                 else:
-                    act(ga(256 * k), raw, src, AF.Copy, ("feat", "feat0", ic), ("raw%d" % c,))
-                mm(256 * k, T[px][:, 0:256 * k], WT, T.XP[0:nl, a:a + 16 * k, :], True, False, [N("WT")] + xp, px)
-                mm(256 * k, T[px][:, 0:256 * k], T.IB[:], raw, False, True, ("IB", "raw%d" % c), px)
+                    add("g", lambda out=out, src=src: g.affine_select(out, src, [[0, NX]], ALU.is_equal, 0.0, 0, 0), 180 + 2 * NX * CY, (iw,), p=(N("Wx"),))
+            c = c0
+            for calls in CH:
+                a, k, x = 16 * (c - c0), sum(m for e, m in calls), 0
+                if calls[0][0] == "f":
+                    for e, m in calls:
+                        tt(ga(256 * m), T.raw[:, 256 * (c + x):256 * (c + x + m)], T.featW[:].indirect(T.inC[:, o + a + 16 * x:o + a + 16 * (x + m)]),
+                           T.Wx[:, 256 * (c + x):256 * (c + x + m)], ALU.subtract, ("feat", "feat0", ic, N("Wx")), ("raw%d" % (c + x),))
+                        x += m
+                    act(cy(256 * k), T.A[:, c:c + k, :], T.raw[:, 256 * c:256 * (c + k)], AF.Abs, ["raw%d" % y for y in range(c, c + k)], ["A%d" % y for y in range(c, c + k)])
+                    c += k
+                    continue
+                px = "pX%d" % (nx[0] % 4)
+                nx[0] += 1
+                mm(256 * k, T[px][:, 0:256 * k], T.IN[:], T.Wx[:, 256 * c:256 * (c + k)], True, False, ("IN", N("Wx")), px)
+                for e, m in calls:
+                    raw, src = T.raw[:, 256 * (c + x):256 * (c + x + m)], T.featW[:].indirect(T.inC[:, o + a + 16 * x:o + a + 16 * (x + m)])
+                    if e == "v":
+                        cp(ga(256 * m), raw, src, ("feat", "feat0", ic), ("raw%d" % (c + x),))
+                    else:
+                        act(ga(256 * m), raw, src, AF.Copy, ("feat", "feat0", ic), ("raw%d" % (c + x),))
+                    mm(256 * m, T[px][:, 256 * x:256 * (x + m)], T.IB[:], raw, False, x + m == k, ("IB", "raw%d" % (c + x)), px)
+                    x += m
                 act(cy(256 * k), T.A[:, c:c + k, :], T[px][:, 0:256 * k], AF.Abs, (px,), ["A%d" % y for y in range(c, c + k)])
                 c += k
             if t == h == 0:
@@ -402,19 +448,19 @@ def rank_program(g, core, T, topo):
             def turned(ps, PM, nm, XT, nxt_, stop):
                 for e in range(2):
                     for s in range(2):
-                        mm(8 * NC, T[ps][:, 0:hc, 16 * e:16 * e + 16], PM[:, 256 * e + 128 * s:256 * e + 128 * s + 128], XT[:, pr, 16 * s:16 * s + 16], False, stop and e + s == 2, (nm, nxt_), ps)
+                        mm(8 * NC, T[ps][:, pr if ps == "pS" else slice(0, hc), 16 * e:16 * e + 16], PM[:, 256 * e + 128 * s:256 * e + 128 * s + 128], XT[:, pr, 16 * s:16 * s + 16], False, stop and e + s == 2, (nm, nxt_), ps)
             for ps in (pv, "pL"):
                 mm(nl, T[ps][:, 0:hc, :], T.ob[0:33, :], T.Kc[0:33, 0:nl], True, False, ("ob", "Kc"), ps)
                 turned(ps, T.PM, "PM", T.GT, N("GT"), ps == "pL")
             act(cy(nl), T.Lp[:, ls], T.pL[:, 0:hc, :], AF.Identity, ("pL", "limA"), (N("Lp"),), bias=T.limA[:])
             for a, e in zip([0] + BATCH, BATCH):
                 for b in range(16):
-                    mm(16 * (e - a), T[pv][:, a // 2:e // 2, :], T.LH[:, 128 * b:128 * b + 128], T.A[:, c0 + a:c0 + e, 16 * b:16 * b + 16], False, b == 15 and e == NC,
+                    mm(16 * (e - a), T[pv][:, a // 2:e // 2, :], T.LH[:, 15 - b:143 - b], T.A[:, c0 + a:c0 + e, 16 * b:16 * b + 16], False, b == 15 and e == NC,
                        ["LH"] + ["A%d" % y for y in range(c0 + a, c0 + e)], pv)
             tt(cy(nl), T.vm[:, ls], T[pv][:, 0:hc, :], T.Lp[:, ls], ALU.max, (pv, N("Lp")), (N("vm"),))
             scan(cy(nl), T.vI[:, ls], T.RST[:, 0:nl], T.vm[:, ls], ALU.max, ALU.min, ("RST", N("vm")), (N("vI"),))
             ts(S, T.yy[:, lb], last16(T.vI), 8191, None, ALU.bitwise_and, None, (N("vI"),), (N("yy"),))
-            ou, oo = T.outC[:, o + nl:o + nl + NC], "outO%d_%d" % (t, h)
+            ou, oo = T.outC[:, ob:ob + NC], "outO%d_%d" % (t, h)
             ts(S, ou, T.yy[:, lb], 4096.0, None, ALU.subtract, None, (N("yy"),), (oo,))
             if KGQ == "v":
                 cp(ga(nl), T.KG[:, ls], T.keyW[:].indirect(ou), ("keyW", oo), (N("KG"),))
@@ -422,13 +468,19 @@ def rank_program(g, core, T, topo):
                 act(ga(nl), T.KG[:, ls], T.keyW[:].indirect(ou), AF.Copy, ("keyW", oo), (N("KG"),))
             if not final:
                 ow = T.outW[:, 256 * t + l0:256 * t + l1]
-                tt(ga(nl), T.DW[:, ls], T.featW[:].indirect(ou), Wa, ALU.subtract, ("feat", "feat0", oo, iw), (N("DW"),))
-                act(cy(nl), ow, T.DW[:, ls], AF.Abs, (N("DW"),), ("outW%d_%d" % (t, h),))
+                if DWQ == "v":
+                    tt(ga(nl), T.DW[:, ls], T.featW[:].indirect(ou), Wa, ALU.subtract, ("feat", "feat0", oo, iw), (N("DW"),))
+                    act(cy(nl), ow, T.DW[:, ls], AF.Abs, (N("DW"),), ("outW%d_%d" % (t, h),))
+                else:
+                    act(ga(nl), T.DW[:, ls], T.featW[:].indirect(ou), AF.Copy, ("feat", "feat0", oo), (N("DW"),))
+                    mm(nl, T[pv][:, 0:hc, :], T.IN[:], Wa, True, False, ("IN", iw), pv)
+                    mm(nl, T[pv][:, 0:hc, :], T.IB[:], T.DW[:, ls], False, True, ("IB", N("DW")), pv)
+                    act(cy(nl), ow, T[pv][:, 0:hc, :], AF.Abs, (pv,), ("outW%d_%d" % (t, h),))
                 send(T.inW[:, 256 * (t + 1) + l0:256 * (t + 1) + l1], ow, "w%d_%d" % (t + 1, h), ("outW%d_%d" % (t, h),), ("inW%d_%d" % (t + 1, h),), hlp, FLYW)
             tr(cy(nl / 2), T.KT[:, pr, :], T.KG[:, ls], (N("KG"),), (N("KT"),))
-            mm(4 * nl, T.pS[:, 0:hc, :], T.INf[:], T.M[:, ls], True, False, ("INf", N("M")), "pS")
+            mm(4 * nl, T.pS[:, pr, :], T.INf[:], T.M[:, ls], True, False, ("INf", N("M")), "pS")
             turned("pS", T.PK, "PK", T.KT, N("KT"), True)
-            act(cy(nl), T.AB[:, ls], T.pS[:, 0:hc, :], AF.Abs, ("pS",), (N("AB"),))
+            act(cy(nl), T.AB[:, ls], T.pS[:, pr, :], AF.Abs, ("pS",), (N("AB"),))
             scan(cy(nl), T.es[:, ls], T.RN[:, 0:nl], T.AB[:, ls], ALU.max, ALU.min, ("RN", N("AB")), (N("es"),))
             ev = last16(T.es)
             two = lambda b, e: b[:, 2 * c0 + NC * e:2 * c0 + NC * e + NC]
@@ -436,14 +488,19 @@ def rank_program(g, core, T, topo):
             for e, bit in enumerate((16, 2)):
                 ts(S, two(T.x2, e), ev, 4095 + 4096 * bit + NONE, None, ALU.bitwise_and, None, (N("es"),), (N("x2%d_" % e),))
             for e in range(2):
-                tt(S, two(T.l2, e), two(T.x2, e), T.yy[:, lb], ALU.min, (N("x2%d_" % e), N("yy")), p=(N("l2"),))
-            ts(S, both(T.l3), both(T.l2), 4095, None, ALU.bitwise_and, None, (N("l2"),), (N("l3"),))
-            cp(S, both(T.u2), both(T.l3), (N("l3"),), (N("u2"),))
-            if TOPQ == "v":
-                ts(ga(nl), T.top[:, ls], T.kid[:, 0:W].indirect(two(T.u2, 0)), C(SCT), C(BIT), ALU.mult, ALU.add, ("kid", N("u2"), "sct", "bit"), (N("top"),))
+                tt(S, two(T.l2, e), two(T.x2, e), T.yc[:] if STG else T.yy[:, lb], ALU.min, (N("x2%d_" % e), "yc" if STG else N("yy")), p=(N("l2"),))
+            if STG:
+                act(ga(nl), T.kid[:, W + 16:W + 16 + nl], T.kid[:, 0:W].indirect(ou), AF.Copy, ("kid", oo), ("stg",))
+                cp(S, both(T.u2), both(T.l2), (N("l2"),), (N("u2"),))
             else:
-                act(ga(nl), T.top[:, ls], T.kid[:, 0:W].indirect(two(T.u2, 0)), AF.Identity, ("kid", N("u2"), "sct", "bit"), (N("top"),), bias=C(BIT), scale=C(SCT))
-            tt(ga(nl), T.cf[:, ls], T.kid[:, 0:W].indirect(two(T.u2, 1)), T.top[:, ls], ALU.max, ("kid", N("u2"), N("top")), (N("cf"),))
+                ts(S, both(T.l3), both(T.l2), 4095, None, ALU.bitwise_and, None, (N("l2"),), (N("l3"),))
+                cp(S, both(T.u2), both(T.l3), (N("l3"),), (N("u2"),))
+            win = T.kid[:] if STG else T.kid[:, 0:W]
+            if TOPQ == "v":
+                ts(ga(nl), T.top[:, ls], win.indirect(two(T.u2, 0)), C(SCT), C(BIT), ALU.mult, ALU.add, ("kid", "stg", N("u2"), "sct", "bit"), (N("top"),))
+            else:
+                act(ga(nl), T.top[:, ls], win.indirect(two(T.u2, 0)), AF.Identity, ("kid", "stg", N("u2"), "sct", "bit"), (N("top"),), bias=C(BIT), scale=C(SCT))
+            tt(ga(nl), T.cf[:, ls], win.indirect(two(T.u2, 1)), T.top[:, ls], ALU.max, ("kid", "stg", N("u2"), N("top")), (N("cf"),))
             oc = "outC%d_%d" % (t, h)
             if final:
                 ts(cy(nl), T.outF[:, ls], T.cf[:, ls], C(OFF), None, ALU.subtract, None, (N("cf"), "off"), (oc,))
@@ -451,23 +508,18 @@ def rank_program(g, core, T, topo):
                 dma("y", T.yn[:, ls], T.inF[:, ls], N("yn"), 512 * nl, r=(N("inF"),))
             else:
                 ts(cy(nl), T.outC[:, o:o + nl], T.cf[:, ls], C(OFF), None, ALU.subtract, None, (N("cf"), "off"), (oc,))
-                send(T.inC[:, o + NP * CS:o + NP * CS + CS], T.outC[:, o:o + CS], "c%d_%d" % (t + 1, h), (oc, oo), ("inC%d_%d" % (t + 1, h),))
-            prev, prn = (T.inC[:, o + nl:o + nl + NC], ic) if t else (T.prev0[:, lb], "prev0")
-            ts(S, T.pn[:, lb], prev, T.CJ[:, q:q + 1], None, ALU.add, None, (prn, "CJ"), (N("pn"),))
-            ts(S, T.na[:, lb], last16(T.vI), T.limA[:], (1 - RC) * RS, ALU.subtract, ALU.is_ge, (N("vI"), "limA"), (N("na"),))
-            tt(S, T.dn[:, lb], T.pS[:, 0:hc, q::16], T.pn[:, lb], ALU.subtract, ("pS", N("pn")), (N("dn"),))
-            tt(S, T.dn2[:, lb], T.dn[:, lb], T.na[:, lb], ALU.mult, (N("dn"), N("na")), (N("dn2"),))
-            tt(S, T.M[:, l0 + q:l1:16], T.M[:, l0 + q:l1:16], T.dn2[:, lb], ALU.add, (N("dn2"), N("M")), (N("M"),))
-            s1 = T.s1[:, 8 * h:8 * h + NC]
-            ts(S, T.ncd[:, lb], ev, float(NONE), C(DUMP), ALU.is_ge, ALU.mult, (N("es"), "dump"), (N("ncd"),))
-            tt(S, s1, T.yy[:, lb], T.ncd[:, lb], ALU.max, (N("yy"), N("ncd")), (N("s1"),))
-            ts(S, T.s1u[:, lb], s1, 4096.0, None, ALU.subtract, None, (N("s1"),), (N("s1u"),))
-            act(ga(nl), T.gl[:, ls], T.idW[:].indirect(T.s1u[:, lb]), AF.Copy, ("idW", N("s1u")), (N("gl"),))
-            tt(ga(nl), T.eq2[:, ls], s1.indirect(T.expl[:, 0:NC]), T.gl[:, ls], ALU.is_equal, (N("s1"), "expl", N("gl")), (N("eq2"),))
-            scan(cy(nl), T.dsum[:, ls], T.R2[:, 0:nl], T.eq2[:, ls], ALU.mult, ALU.add, ("R2", N("eq2")), (N("dsum"),))
-            ts(S, T.dd[:, lb], last16(T.dsum), C(THR), C(DUMP), ALU.is_ge, ALU.mult, (N("dsum"), "thr", "dump"), (N("dd"),))
-            tt(S, T.s2[:, lb], s1, T.dd[:, lb], ALU.max, (N("s1"), N("dd")), (N("s2"),))
-            ts(S, T.s2u[:, 2 * c0:2 * c1:2], T.s2[:, lb], 4096.0, None, ALU.subtract, None, (N("s2"),), (N("s2u"),))
+                a = min(o, ob)
+                send(T.inC[:, a + 2 * CS:a + 3 * CS], T.outC[:, a:a + CS], "c%d_%d" % (t + 1, h), (oc, oo), ("inC%d_%d" % (t + 1, h),))
+            if t not in JM:
+                mounts(t, c0, c1, [h])
+            lag[0] = LAGW * h
+            if t not in JW:
+                writers(c0, c1, [h])
+        lag[0] = LAGJ
+        if t in JM:
+            mounts(t, 0, 16, range(NP))
+        if t in JW:
+            writers(0, 16, range(NP))
         lag[0] = 0.0
         if not final:
             act(S, T.cov[:], T.ncd[:], AF.Sign, ["ncd%d" % h for h in range(NP)], ("cov", "cs"), scale=-1.0, accum_out=T.cs[:])
@@ -477,9 +529,13 @@ def rank_program(g, core, T, topo):
             ts(S, T.limA[:], T.csa[:], RS, RS * (LIM - 1), ALU.mult, ALU.add, ("csa",), ("limA",))
         for h, (c0, c1) in enumerate(PARTS):
             for c in range(c1 - 1, c0 - 1, -1):
-                a = CS * (NP * t + h) + 16 * (c - c0)
+                a = at(t, c)
                 src = T.outF[:, 16 * c:16 * c + 16] if final else T.outC[:, a:a + 16]
-                cp((60 + 16 * SCAT) * CY, T.kid[:].indirect(T.s2u[:, 2 * c:2 * c + 1]), src, ("s2u%d" % h, "outC%d_%d" % (t, h)), ("kid",))
+                kid = "end" if final and ENDQ else "kid"
+                cp((60 + 16 * SCAT) * CY, T[kid][:, 0:W + 16].indirect(T.s2u[:, 2 * c:2 * c + 1]), src, ("s2u%d" % h, "outC%d_%d" % (t, h)), (kid,))
+        if t == STEPS - 2:
+            for x, e in enumerate(ENDQ):
+                copy(e, 256, T.end[:, 256 * x:256 * x + 256], T.kid[:, 256 * x:256 * x + 256], ("kid",), p=("end",))
     for h, (c0, c1) in enumerate(PARTS):
         N = lambda s: s + "%d" % h
         ls, nl = slice(16 * c0, 16 * c1), 16 * NC
@@ -497,18 +553,20 @@ def rank_program(g, core, T, topo):
     act(cy(256), T.ymo[:], T.pX0[:, 0:256], AF.Copy, ("pX0",), ("ymo",), scale=64.0, bias=131072.0)
     dma("s", T.ymu[:], T.ymo[:], "ymu", 131072, r=("ymo",))
     yb = ["pX1", "pX2", "pX3", "pL"]
+    kid = "end" if ENDQ else "kid"
+    col = lambda i, x: T[kid][:, 512 * i + 256 * x:512 * i + 256 * x + 256]
+    acc = lambda x: T.acc[:, 256 * x:256 * x + 256]
     for x in range(2):
-        col = lambda i: T.kid[:, 512 * i + 256 * x:512 * i + 256 * x + 256]
-        acc, na, pe = T.acc[:, 256 * x:256 * x + 256], "acc%d" % x, "pv%d" % x
         for i in range(8 - YP, 8):
-            mm(1024, T[pe][:, 0:8, :], T["F%d" % (i + 1)][:], col(i), i == 8 - YP, i == 7, ("F", "kid"), pe)
-        for i in range(1, 8 - YP):
+            mm(1024, T["pv%d" % x][:, 0:8, :], T["F%d" % (i + 1)][:], col(i, x), i == 8 - YP, i == 7, ("F", kid), "pv%d" % x)
+    for i in range(1, 8 - YP):
+        for x in range(2):
             ps = yb[nx[0] % 4]
             nx[0] += 1
-            out = T[ps][:, 0:256] if ps[1] in "TX" else T[ps][:, 0:8, :]
-            act(cy(256), out, col(i), AF.Copy, ("kid",), (ps,), scale=float(i + 1))
-            tt(cy(256), acc, col(0) if i == 1 else acc, out, ALU.add, ("kid" if i == 1 else na, ps), (na,))
-        if YP:
-            tt(cy(256), acc, acc, T[pe][:, 0:8, :], ALU.add, (na, pe), (na,))
-        dma("ys"[x], T.yd[:, 256 * x:256 * x + 256], acc, "yd%d" % x, 131072, r=(na,))
+            out = T[ps][:, 0:256] if ps[1] == "X" else T[ps][:, 0:8, :]
+            act(cy(256), out, col(i, x), AF.Copy, (kid,), (ps,), scale=float(i + 1))
+            tt(cy(256), acc(x), col(0, x) if i == 1 else acc(x), out, ALU.add, (kid if i == 1 else "acc%d" % x, ps), ("acc%d" % x,))
+    for x in range(2):
+        tt(cy(256), acc(x), acc(x), T["pv%d" % x][:, 0:8, :], ALU.add, ("acc%d" % x, "pv%d" % x), ("acc%d" % x,))
+        dma("ys"[x], T.yd[:, 256 * x:256 * x + 256], acc(x), "yd%d" % x, 131072, r=("acc%d" % x,))
     emit(g, T, ops, order(ops))

@@ -1,64 +1,143 @@
+from concourse.bass import DstId, RemoteDMATransfer
 from concourse.mybir import AluOpType as ALU, ActivationFunctionType as AF
 
 STEPS, W, L, LIM = 8, 4096, 256, 60
 PARTS = [(8, 16), (0, 8)]
-NX, WXQ, SHQ = 128, "vvvvvvvvvvvvgggg", "vsvsvsvsvsvsvsvs"
-CH = [[("f", 2)], [("s", 2)], [("f", 2)], [("s", 2)]]
-BATCH = [4, 8]
-BIG, NONE, RS, KS, RC = float(2 ** 26), 2 ** 17, float(2 ** 17), float(2 ** 18), 120
-JM, JW, DWQ, LAGJ, KIDQ = range(8), (), "s", 0.0, "gggggvgv"
-KB, ENDQ, LAGW = ["pX2", "pX3", "pS", "pv1"], "", 0.0
-LAG, RELAY, FLYW, KEYQ = 1.0, False, 2600.0, "svsvsvsv"
-LAGS, LOOKS, ORDER, STG = [1200.0, 1500.0, 1800.0, 2100.0, 2400.0, 2700.0, 3000.0], [2.0, 4.0, 7.0], {}, True
-NP, NC = len(PARTS), 16 // len(PARTS)
-WTQ, KGQ, TOPQ, HOPX, YP = "s", "v", "s", 210.0, 2
-KQ = [0, 1536, 3072, 3584, 4096]
-LOADS = ["wts", "feat0", "cand", "want", "feat", "mkey", "mobj", "last"]
-CS = 16 * NC + 8
-NS = 16 * NC
-CY, PE, GA, SCAT, HOP, FLY, LOAD, RATE, ROWS, LOOK = 0.85, 0.54, 1.56, 3.8, 210.0, 2600.0, 1600.0, 300.0, 80000.0, 3.0
+SHQ, KIDQ, KEYQ, KGQ, LPQ, TOPQ = "sg" * 8, "ggggggvv", "svsvsvsv", "ss", "ss", "s"
+WXQ, WX0 = ["s" * 11 + "g" * 5, "s" * 10 + "g" * 6], ["vvvvvvvvssssssss", "ssssvvgggggggggg"]
+CH = [[("f", 2), ("f", 2), ("f", 2), ("s", 2)], [("f", 2), ("f", 2), ("f", 1), ("f", 1), ("s", 2)]]
+BATCH, TV = [[(0, 4), (4, 8)]] * 2, [0, 0]
+JW = False
+BIG, NONE, RS, KS, RC, DB = float(2 ** 26), 2 ** 17, float(2 ** 17), float(2 ** 18), 120, 8192.0
+KB, MB = ["pX2", "pX1", "pv0", "pX2", "pX2", "pX1", "pS", "pX2"], "pv1"
+LAG, LAGJ, LAGW = 1.0, 0.0, 0.0
+PERIOD, END = 12327.0, 8000.0
+ROUND = {
+    "v": """G0@25 raw10@621 GT0@990 raw8@2554 raw12@2927 G1@3633 GT1@3923 raw2@3923 ncd0@3994 outO0@4040 raw0@4216 vI0@4346 raw4@4936 yy0@4937 xo0@5306 raw5@5586 KT0@5910 outW0@6102 vI1@7001 es0@7053 xx0@7101 cf0@7383 x20'@7420 x20@7496 outO1@7748 x21'@7978 xo1@8016 yy1@8021 na@8130 l20@8179 cf1@8216 x21@8228 KT1@8264 u20@8482 s2u0'@9200 outW1@9202 dn@9234 kid'@9280 pn'@9304 ncd1@9876 l21@10088 es1@10171 outC0@10171 u21@10270 csi@10291 xx1@10424 pn@10493 s2u0@10577 kid@10610 outC1@11026 csa@11400 dm@11424 M0@11492 wr0@11498 kid''@13264 limT@13444 wr1@13641 limA@14090 s2u1@14882 s2u1'@14974 kid'''@15306 kid''''@17653 kid'''''@18001 kid'''''''@18721 kid''''''@20156""",
+    "s": """A8@-1810 Wx0@-248 A14@1132 A10@1166 raw14@1339 A12@2237 Wx1@2311 Lp0@2330 AB0@2370 KG0@2727 A0@3294 A6@3574 raw6@3639 A2@3656 Lp1@4015 A4@6022 A5@6022 stg0@7188 top0@7440 KG1@8414 stg1@9140 cov@9176 AB1@10103 wa0@11528 top1@11806 wa1@14258""",
+    "g": """Wx0@-1300 Wx1@643 sendw0@5497 sendw1@7869 sendc0@11164 sendc1@11865""",
+    "t": """add14@-1186 kL0@703 sub14@758 sub6@1083 kv0@1264 tL1@1584 tL0@1751 sum8@1803 kL1@2118 cw0@2261 tv0@2387 kv1@2503 sum0@2677 sum12@3090 add6@4662 sum4@4706 tv1@5134 kS0@5232 tS0@5864 own0@6309 eqa0@6428 tS1@6505 kS1@7242 cw1@10528 eqb1@10552 eqa1@11317 cnt@11835 own1@11863 eqb0@12101""",
+}
+NP = len(PARTS)
+YP, YQ = [2, 1], [0, 256, 512]
+ROUND = {
+    "v": """<klb@-9839 <raw8@-7903 <mo16@-7436 <raw10@-6936 <keyW'@-6779 <mi@-6732 <keyW@-5823 <mj@-5278 <raw4@-4982 <raw12@-3881 <XG@-2816 raw10@-1648 G0@-861 <vI0@747 GT0@2460 G1@2466 <outW0@2831 raw12@3244 raw8@3244 raw0@3299 <raw2@3497 GT1@3497 raw2@3558 <outO0@3590 vI0@3853 <KT0@3855 <raw0@3897 yy0@3917 <yy0@4070 <raw5@4290 pn@4341 <vI1@4571 raw4@4620 outO0@4885 x20'@5019 vI1@5020 KT0@5221 raw5@5236 xo0@5269 x20@5458 outW0@5515 <kid'@5912 u20@5946 xx0@5949 <es0@6051 es0@6070 outO1@6233 xx0'@6427 yy1@7272 es1@7519 l20@7823 outW1@7879 outC0@8037 wr0@8114 u21@8170 ncd0@8305 cf0@8573 l21@8746 csa@8993 ncd1@9087 x21'@9087 x21@9144 KT1@9211 >kid''''@9235 dm@9325 xx1'@9369 na@9452 xo1@9481 dn@9515 s2u0@9613 >kid@10087 >kid'''''@10131 cf1@10238 >kid'''''''@10460 xx1@10662 >kid'@11079 kid@11548 outC1@11548 csi@11614 <kid@11687 kid'@11767 M0@11890 >YT@11992 wr1@11992 >X@12131 >X'@12143 >kid'''@12377 >wr1@12409 kid''@12636 >XT@13241 >kid''@13609 limA@13638 >s2u1@13673 >kid''''''@14541 s2u1@16290 kid'''@16853 kid''''@17825 kid'''''@17843 kid'''''''@18358 kid''''''@19050""",
+    "s": """<mk16@-8412 <XF@-5087 <XF'@-4445 <keyW'@-4322 <keyW@-3930 <raw14@-2754 Wx1@-228 KG0@-111 Wx0@563 <A10@642 A6@677 Lp1@890 <M0@948 A12@992 A2@1116 A8@1329 A0@1593 <A14@1657 Lp0@1700 raw14@1779 <A12@1914 A14@2092 <A8@2411 A10@2426 <raw6@3251 raw6@3274 <A6@3745 <KG0@3774 A5@4327 A4@5221 <AB0@5339 <A0@5593 AB0@5988 <A2@6028 stg0@6477 >klb@6487 KG1@6951 <A4@6967 AB1@7669 stg1@7910 top0@7910 <A5@8024 >Y@9088 >mk16@9339 top1@9613 cov@9796 wa0@9884 wa1@10597 >wa1@12354 limT@12568 >Y'@12681""",
+    "g": """Wx0@-2056 Wx1@709 sendw0@4223 sendw1@7378 sendc0@8837 sendc1@11636""",
+    "t": """<ksum0@-8605 <rot@-8397 <join@-4933 <ksum1@-3625 <rows0@-3337 <rows1@-3335 <code@-2559 sub6@-1873 sub14@-1836 <rows2@-1410 <rows3@-1410 <add14@-32 cw0@145 kv0@268 kL0@473 <rows4@1087 add14@1221 kL1@1521 tv0@1870 kv1@1884 tL0@2324 <kS0@2454 tv1@2454 sum12@2622 <sub6@2722 <rows5@2745 <add6@2762 <sum12@2820 <rows7@3010 <sum8@3197 sum8@3198 <rows6@3360 tL1@3601 kS0@4025 add6@4224 sum4@5644 >pX2'@5783 sum0@5855 >eq1@6019 kS1@6359 tS0@6400 eq0@7202 >pX2@8004 >pX2''@8411 tS1@8672 eq1@9426 cnt@9623 cw1@9634 >back@16219""",
+}
+PERIOD, WXQ, KIDQ, KEYQ = 12153.0, ["ssssssssssvvgggg", "ssssssssvvgggggg"], "gggggggv", "svsvssss"
+ROUND = {
+    "v": """-mo16@-11333 -mi@-7653 -klb@-7476 -mj@-5630 -keyW@-3364 -XG@-2323 Wx0c@-1817 <Wx1c@-1573 <Wx1b@-1102 <GT1@-423 <mi@-217 Wx1c@-80 <raw10@-13 <Wx1a@67 G0@210 <mj@255 raw10@264 <raw8@470 GT0@994 raw8@1048 -keyW'@1621 raw12@1778 <vI0@1940 <klb@2094 <raw0@2111 <outO0@2409 <raw12@2415 G1@2500 raw0@2560 GT1@3290 raw2@3340 <raw2@3390 <raw5@3559 vI0@4231 raw4@4347 yy0@4737 <raw4@4822 <outW0@4885 outO0@5001 raw5@5056 <yy0@5243 xo0'@5446 outW0@5501 KT0@5735 xo0@5789 <es0@5868 pn@5998 <KT0@6508 es0@6727 vI1@6968 x20@7083 -kid'@7124 x20'@7138 ncd0@7192 yy1@7293 l20@7402 xx0@7457 outO1@7558 u20@7667 xx0'@7721 outW1@7822 na@8043 xo1@8097 <vI1@8122 outC0@8152 KT1@8372 outD0@8427 xo1'@8648 >kid''@8721 +YT@8723 >xx1@9220 >xx1'@9220 +X@9295 es1@9304 +X'@9376 >kid'''@9397 dn@9413 >wr1@9458 wr0@9467 >outC0@9610 x21'@9644 ncd1@9698 x21@9753 dm@9807 s2u0'@9861 s2u0@9916 l21@10017 xx1@10071 xx1'@10126 >kid@10178 M0@10180 u21@10281 >outC1@10398 outD1@10546 >ncd1@10604 csi@10767 outC1@10821 csa@11042 kid@11252 limA@11406 wr1@11575 >s2u1@11721 >s2u1'@11721 kid'@11751 +XT@11789 limT@11906 s2u1'@11964 s2u1@12018 kid''@12181 >kid'@12533 >kid''''''@12820 >kid'''''''@13132 >kid''''@13392 >kid'''''@14377 kid'''@16230 kid''''@16945 kid'''''@17997 kid''''''@18362 kid'''''''@18726""",
+    "s": """-mk16@-7593 -keyW'@-5946 <Lp1@-3635 Wx0a@-3011 Wx0b@-2657 Wx0c@-2331 <Wx1d@-2271 -XF@-2186 -keyW@-1954 <Lp0@-759 Wx1a@-690 Wx1b@-336 -XF'@-149 raw14@210 <Wx1c@1089 A10@1204 <keyW'@1481 A14@1639 <A14@1827 <A8@1885 <raw14@1897 Lp0@2074 A8@2190 A12@2718 <A12@2796 raw6@3153 <keyW''@3310 <A6@3484 <A10@3667 A0@3883 <keyW@3979 <A5@3994 A2@4318 <A0@4725 Lp1@4754 <KG0@4818 A6@4869 KG0@5304 <keyW'''@5500 A4@5525 <raw6@5629 -M0@5687 A5@5743 <A2@5940 <A4@6029 AB0@6348 <AB0@6381 stg0@6937 KG1@7822 top0@8043 cf0@8264 stg1@8484 wa0@8783 AB1@8985 cov@9985 +mk16@10218 >wa1@10430 cf1@10546 +klb@10555 top1@10767 wa1@11188 +Y@11887 +Y'@12163""",
+    "g": """Wx0h@-2447 Wx0g@-1761 Wx1f@-126 Wx1g@560 Wx1h@1246 sendw0@5931 sendw1@8253 sendc0@8858 sendc1@11252""",
+    "t": """+pX2@-24374 -ksum0@-8853 kL0@-1121 sub14@-1048 kS0@-495 -rot@-8 kv0@20 <kS0@26 <tL0@56 kv1@94 cw0@167 -rows3@178 <ksum1@290 -rows1@579 -rows2@579 <sub14@579 -rows0@616 add14@1149 <add14@1365 tL0@1426 sub6@1564 <kL1@1670 <tv0@1671 -code@1739 kL1@2400 tv0@2473 sum8@2835 <sub6@2888 sum12@3423 <rows4@4057 add6@4093 <rows5@4110 <rows6@4148 tL1@4370 tv1@5079 sum0@5373 <rows7@5753 <sum8@5753 -join@5766 tS0@5999 <tL1@6008 sum4@6170 <sum12@6565 <add6@6755 kS1@6758 own0@7034 eq0@7985 tS1@8637 cw1@9170 own1@9282 +pX2'@9577 cnt@10249 eq1@10390 >own1@11203 +pX2''@11609 >eq1@13289 +back@15657""",
+}
+PERIOD = 12068.0
+ROUND = {
+    "v": """s2u1@12196 G0@210 raw10@264 GT0@994 Wx1c@1048 raw8@1157 raw12@1887 raw0@2780 G1@2723 raw2@3567 GT1@3510 kid''@16361 vI0@4446 s2u1'@12250 kid'''@16725 yy0@4811 raw4@4865 outO0@5255 raw5@5310 kid''''@17769 KT0@5951 outW0@6005 kid'''''@18294 kid''''''@18659 xo0'@6744 xo0@6799 pn@6853 es0@6908 kid'''''''@19085 vI1@7183 ncd0@7299 x20@7353 x20'@7408 yy1@7509 xx0'@7563 xx0@7618 l20@7672 outO1@7773 na@7828 u20@7936 outW1@8038 outC0@8258 KT1@8479 outD0@8533 xo1'@8754 xo1@8809 wr0@9087 es1@9411 dn@9519 ncd1@9729 x21@9784 x21'@9838 xx1@9994 xx1'@10048 l21@10103 dm@10157 Wx0c@-1857 u21@10367 s2u0@10421 s2u0'@10476 csi@10833 outC1@10887 outD1@11108 M0@11328 csa@11383 kid@11538 limA@11693 wr1@11807 limT@11984 kid'@12042
+        -mo16@-13488 -mi@-12207 -mj@-6926 <Wx1c@-1789 -klb@-1354 <mj@-666 <mi@-151 <raw10@677 -XG@678 <outO0@793 <vI0@1152 <Wx1a@1265 -keyW'@1843 -keyW@1907 <klb@1973 <Wx1b@2102 <raw8@2119 <raw0@2432 <raw12@3456 <raw2@3667 <es0@4045 <yy0@4501 <outW0@4588 <raw5@5022 <GT1@5869 -kid'@6372 <raw4@6522 <KT0@6615 <vI1@7960 >xx1'@9684 >outC1@10092 >s2u1@10200 >s2u1'@10265 >xx1@10430 >kid'''@10687 >wr1@10687 >kid''@10740 >kid@10813 >outC0@11009 >ncd1@11696 +X'@12127 +YT@12269 +X@12338 >kid'''''''@12445 >kid''''@12879 +XT@13129 >kid'@13225 >kid''''''@13474 >kid'''''@14840""",
+    "s": """raw14@210 Wx1b@939 A10@1266 A14@1701 Lp0@2136 A8@2252 A12@2827 raw6@3262 A0@3992 A2@4447 Lp1@4883 A6@4998 KG0@5520 A4@5741 A5@5958 AB0@6563 stg0@7381 KG1@8038 cf0@8258 top0@8479 wa0@8700 AB1@9092 Wx0a@-2422 stg1@9999 cov@10220 Wx0c@-1793 Wx0b@-1630 cf1@10764 top1@10985 wa1@11420 Wx1a@-390
+        -mk16@-8055 -keyW'@-4551 <Lp1@-3748 -XF'@-1916 -keyW@-1574 -XF@-1099 <Wx1d@-654 <Lp0@-24 <A12@923 <keyW''@1447 -M0@1448 <Wx1c@1524 <keyW@1582 <A14@2078 <keyW'@2127 <A8@2264 <A10@3175 <raw14@3193 <A6@3916 <KG0@4428 <A0@4467 <A5@5187 <keyW'''@5187 <A2@5323 <A4@5370 <raw6@6797 <AB0@6850 +mk16@7909 >wa1@10099 +klb@10837 +Y'@11330 +Y@12350""",
+    "g": """Wx1h@173 Wx1g@860 Wx1f@1546 sendw0@6436 sendw1@8468 sendc0@8964 Wx0h@-1859 Wx0g@-1172 sendc1@11582""",
+    "t": """kv0@183 sub14@256 kv1@809 add14@1149 kL0@1426 tL0@1499 sub6@1638 kL1@2462 tv0@2535 sum8@2897 sum12@3485 add6@4202 tL1@4502 tv1@5208 sum0@5502 tS0@6215 sum4@6386 kS1@6973 own0@7250 eq0@7882 tS1@8743 cw1@9087 own1@9199 cnt@10484 eq1@10623 cw0@-261 kS0@-149
+        +pX2@-27424 -ksum0@-9742 <kL1@-390 -rows3@93 <ksum1@436 <add14@666 -rot@1099 -rows1@1099 <sub14@1761 -rows2@1816 <tL0@2160 -rows0@2375 -code@3001 <tv0@3003 <rows5@4378 <rows4@4465 -join@4482 <rows6@4704 <sum8@4704 <rows7@5271 <add6@6100 <sum12@6859 <sub6@6893 <kS0@6935 <tL1@6943 +pX2'@9350 +pX2''@10881 >own1@11001 >eq1@13348 +back@15960""",
+}
+KIDQ = "ggggggvv"
+ROUND = {
+    "v": """s2u1@12196 G0@210 raw10@264 GT0@994 Wx1c@1048 raw8@1157 raw12@1887 raw0@2723 G1@3453 raw2@3507 GT1@4237 kid''@16361 vI0@4446 s2u1'@16631 kid'''@16725 yy0@4811 raw4@4865 outO0@5255 raw5@5310 kid''''@17769 KT0@5951 outW0@6005 kid'''''@18294 kid''''''@18659 xo0'@6744 xo0@6799 pn@6853 es0@6908 kid'''''''@19085 vI1@7183 ncd0@7299 x20@7353 x20'@7408 yy1@7509 xx0'@7563 xx0@7618 l20@7672 outO1@7773 na@7828 u20@7936 outW1@8038 outC0@8258 KT1@8479 outD0@8533 xo1'@8754 xo1@8809 wr0@9087 es1@9411 dn@9519 ncd1@9729 x21@9784 x21'@9838 xx1@9994 xx1'@10048 l21@10103 dm@10157 Wx0c@-1857 u21@10367 s2u0@10421 s2u0'@10476 csi@10833 outC1@10887 outD1@11108 M0@11328 csa@11383 kid@11538 limA@11693 wr1@11807 limT@11984 kid'@12042
+        -mi@-12207 -mo16@-12109 -XG@-2523 -keyW@-1815 <vI0@-1710 <Wx1c@-1465 -mj@-1408 <klb@-1346 <raw8@-1202 -klb@-637 <mi@-380 <outO0@319 <Wx1b@578 -keyW'@918 <Wx1a@1977 <raw10@2228 <mj@2317 <raw0@2515 <raw12@3981 <raw2@4028 <raw4@4064 <raw5@4081 <yy0@4172 <outW0@4297 <es0@5824 -kid''@6095 <GT1@6632 <KT0@6938 -kid'@7469 <vI1@8032 >xx1'@8552 >xx1@8614 >kid@8992 >outC0@9087 >dn@9803 >M0@9862 >dm@9962 >kid'@11231 >outC1@11231 +XT@11371 >ncd1@12030 >kid'''''@12754 >kid''''''@12921 >kid''''@13447 +YT@13620 >kid'''''''@13846 +X@13944 +X'@13979 >kid''@14495 >kid'''@14675 >s2u1'@15067 >s2u1@15101 >wr1@15730""",
+    "s": """raw14@210 Wx1b@939 A10@1266 A14@1701 Lp0@2136 A8@2252 A12@2827 raw6@3262 A0@3992 A2@4447 Lp1@4883 A6@4998 KG0@5520 A4@5741 A5@5958 AB0@6563 stg0@7381 KG1@8038 cf0@8258 top0@8479 wa0@8700 AB1@9092 Wx0a@-2422 stg1@9999 cov@10220 Wx0c@-1793 Wx0b@-1630 cf1@10764 top1@10985 wa1@11420 Wx1a@-390
+        -mk16@-9283 -keyW'@-4485 <Lp1@-2811 <Wx1d@-2166 -XF@-1508 -keyW@-1444 -XF'@-1380 <A8@1021 <Lp0@1043 <Wx1c@1393 <keyW''@1701 -M0@2092 <raw14@2162 <keyW'@2192 <keyW@2425 <A12@2561 <A0@2632 <A14@3305 <A10@3632 <keyW'''@4682 <A4@5175 <raw6@5231 <A2@5404 <A6@5436 <A5@5477 <KG0@5890 <AB0@7145 >top1@7972 >cf1@8011 +Y'@8985 +Y@9025 >wa1@9044 +mk16@10336 +klb@12417 +ymo@18297""",
+    "g": """Wx1h@173 Wx1g@860 Wx1f@1546 sendw0@6436 sendw1@8468 sendc0@8964 Wx0h@-1859 Wx0g@-1172 sendc1@11582
+        -kid@-1997 -kid''@-1315 -kid'@-858 <sendw0@969 -kid''''@1454 -kid'''@2393 -kid'''''@3225 <sendw1@4315 <sendc0@5852""",
+    "t": """kv0@183 sub14@256 kv1@809 add14@1149 kL0@1426 tL0@1499 sub6@1638 kL1@2462 tv0@2535 sum8@2897 sum12@3485 add6@4202 tL1@4502 tv1@5208 sum0@5502 tS0@6215 sum4@6386 kS1@6973 own0@7250 eq0@7882 tS1@8743 cw1@9087 own1@9199 cnt@10484 eq1@10623 cw0@-261 kS0@-149
+        -ksum0@-8676 <add14@-1303 <tv0@-1283 -rows3@667 <kS0@991 <ksum1@1110 -rot@1252 <rows4@3006 <sum8@3145 <rows6@3412 -rows2@3523 <tL0@3524 -code@3532 -rows0@3591 <sub14@3628 -rows1@3682 <rows7@3939 <kL1@4289 <rows5@4328 <tL1@5002 <sum12@5097 -join@5663 <add6@5919 <sub6@6107 +pX2''@9418 >own1@9521 +pX2@9766 >eq1@10818 +pX2'@10980 +back2@11638 +back1@13011 +yd0@13254 +back0@13743 +yd1@13800 +back3@14904""",
+}
+KB = ["pX2", "pX1", "pv0", "pX2", "pX2", "pX1", "pS", "pX0"]
+EDGE = {
+    "v": """-mi@-8949 -mo16@-6865 -mj@-6710 -inC1@-3723 <Wx0b@-2929 <GT0@-2899 <GT1@-2293 <mj@-2248 <G0@-2166 <raw10@-1928 -klb@-1839 <raw8@-1728 -inC0@-1591 -keyW@-1518 <Wx0a@-1045 <mi@-510 -keyW'@-421 <raw5@-255 <raw0@-236 <klb@289 <raw12@358 <outO0@1029 <vI0@1065 <yy0@2159 -XG@2290 <G1@2777 <raw2@3109 <Wx1b@3222 <vI1@4127 <KT0@4479 -kid'@4661 <x20'@4766 <es0@4947 <outW0@5396 <x20@5616 <raw4@5671 -kid''@5804 <l20@6003 <u20@6648 <outD0@8106 <outC0@9950
+        >outC0@8260 >outD0@8530 >x21'@9151 >x21@9208 >xx1@9220 >xx1'@9279 >dm@9328 >dn@9554 >ncd1@9820 >M0@9850 >u21@9904 >kid@10029 >outD1@10064 >l21@10135 +Y@10244 >outC1@10244 >kid''@11270 >kid'@11323 >s2u1@11472 >s2u1'@11855 >kid'''@12150 >wr1@12340 +klb@12366 >kid''''@12413 >yf0@12500 >kid''''''@12560 +X1@12880 >kid'''''@12880 >kid'''''''@12975 +X0@13246 +XT1@13714 +XT0@13839 >yf1@14710""",
+    "s": """-mk16@-6111 <raw14@-4083 -keyW'@-3701 <Wx0d@-3399 -XF@-2000 <Wx1a@-1543 <A8@-1460 <Wx0c@-1393 -keyW@-1367 <A14@-1212 <A10@-452 -XF'@-70 <A12@946 <raw6@1637 <Lp0@1696 <keyW''@1783 <keyW@1800 <keyW'@2058 <A0@2231 <A4@2255 <keyW'''@2401 -M0@3456 <KG0@3730 <Lp1@4380 <AB0@4864 <A5@5484 <A2@5607 <A6@5607 <stg0@6483
+        >cf1@9761 +mk16@9981 >top1@10201 >wa1@11070 +ymo@16422""",
+    "g": """<Wx1d@-3408 <Wx1e@-1089 <Wx1g@-943 <Wx1h@346 <Wx1f@743 -kid'@2852 -kid@3236 -kid''@6158 <sendc0@7603 <sendw0@7712 <sendw1@7823 -kid'''''@8115 -kid'''@8147 -kid''''@8438""",
+    "t": """<sub14@-4503 -ksum0@-4189 -rot@-4040 -rows0@-3996 -rows1@-3996 <ksum1@-3463 <add14@-3432 -rows3@-3181 <tL0@-3180 -rows2@-468 <sum0@-356 <tS0@-143 -code@89 <tv1@305 <kL1@604 <tv0@781 <kS0@809 <add6@888 <rows7@903 <sum8@908 <rows6@940 <rows4@959 <rows5@1339 -join@1387 <sum12@1401 <sub6@2651 <tL1@2848 <sum4@6169
+        >eq1@8281 +code@9478 >own1@9801 +turn0@10365 +turn1@10912 +turn2@11700 +yd0@13438 +back@14523 +yd1@15815""",
+}
+PERIOD, LPQ = 12359.0, "sv"
+ROUND = {
+    "v": """G0@210 raw10@264 s2u1@13354 GT0@1048 raw8@1103 Wx1c@1833 limT@14301 raw12@1999 G1@2937 raw0@2992 GT1@3722 raw2@3776 raw4@4506 vI0@4896 kid''@17372 Lp1@5166 yy0@5282 s2u1'@17696 kid'''@17750 outO0@5546 raw5@5601 kid''''@18351 pn@6145 KT0@6241 kid'''''@18715 outW0@6510 kid''''''@19090 xo0@6885 xo0'@6939 kid'''''''@19455 es0@7249 vI1@7474 ncd0@7590 x20'@7644 x20@7699 yy1@7800 xx0'@7854 xx0@7909 l20@7963 outO1@8064 na@8119 u20@8227 outW1@8329 outD0@8549 KT1@8770 outC0@8824 xo1'@9045 xo1@9100 wr0@9378 es1@9701 dn@9810 ncd1@10020 x21@10075 x21'@10129 dm@10183 xx1@10285 xx1'@10339 l21@10393 Wx0c@-1645 s2u0'@10823 u21@10877 s2u0@10932 csi@11117 outC1@11171 outD1@11392 M0@11613 csa@11667 kid@11823 limA@11977 wr1@12091 kid'@12268""",
+    "s": """raw14@210 Wx1b@939 A10@1266 A14@1701 Lp0@2136 A8@2252 A12@2939 raw6@3374 A0@4104 A2@4716 A6@5151 KG0@5811 A4@6031 A5@6249 AB0@6854 stg0@7459 KG1@8329 top0@8549 cf0@8770 wa0@8991 AB1@9383 stg1@9491 Wx0a@-2208 cov@10504 Wx0c@-1800 Wx0b@-1637 top1@11142 cf1@11363 wa1@11704 Wx1a@-390""",
+    "g": """Wx1h@173 Wx1f@860 Wx1g@1546 sendw0@6941 sendw1@8759 sendc0@9255 Wx0g@-1645 Wx0h@-958 sendc1@12087""",
+    "t": """sub14@194 add14@1149 tL0@1426 sub6@1564 kv0@2209 kv1@2283 kL1@2462 tv0@2535 sum8@2897 sum12@3584 tL1@4172 add6@4314 tv1@5492 sum0@5786 tS0@6506 sum4@6677 own0@7264 kS1@7817 eq0@8173 tS1@9034 cw1@9378 own1@9490 cnt@10769 eq1@10907 cw0@-268 kL0@-155 kS0@-82""",
+}
+UNUSED2 = {
+    "v": """-mj@-9014 -mo16@-7800 -mi@-7258 -inC0@-4174 -inC1@-4030 <Wx0a@-3315 <Wx0b@-3296 <GT0@-3262 <GT1@-2833 -keyW@-2815 -klb@-2637 <raw10@-2490 <G0@-2480 <raw8@-2101 <raw0@-912 <mj@-661 <mi@-503 <raw4@-432 <vI0@71 -keyW'@909 <klb@909 <raw12@1654 <G1@2266 <yy0@2297 -XG@2404 <raw2@2435 <outO0@3447 <outW0@3794 -kid'@3979 <Wx1b@4005 <KT0@4111 <x20'@4385 <x20@4467 <vI1@4479 <l20@5544 -kid''@5756 <raw5@5879 <es0@5928 <u20@7001 >outC1@7914 >outC0@8061 <outC0@8310 >outD0@8522 >outD1@8712 >kid@8830 <outD0@8842 >xx1@9200 >xx1'@9279 >dm@9328 >dn@9570 >x21'@9629 >x21@9650 >M0@9695 >s2u1@9940 >ncd1@10157 >l21@10570 >u21@10660 >kid''@10897 +klb@10957 +Y@11155 >kid'@11798 >kid''''@11832 >wr1@11895 >kid'''@12034 >s2u1'@12243 >yf0@12581 >kid'''''@12700 >kid''''''@12740 +X1@12880 >kid'''''''@13165 +X0@13246 +XT1@13556 +XT0@15471 >yf1@15608""",
+    "s": """-mk16@-6100 -keyW'@-4354 <raw14@-4174 <Wx0d@-3078 -XF@-2814 <Wx0c@-2814 <Lp0@-1844 <A8@-1594 <A14@-1211 <Wx1a@-1159 -keyW@-743 -XF'@-741 <A10@478 <raw6@1384 <A4@1566 <A12@1781 <keyW'@1781 <keyW''@1783 <A5@2162 <keyW'''@3035 <A0@3414 -M0@3456 <keyW@3514 <KG0@3830 <Lp1@4025 <A2@5758 <A6@5828 <AB0@5901 <stg0@6946 >top1@8769 >cf1@9073 +mk16@9379 >wa1@11803 +ymo@17767""",
+    "g": """<Wx1d@-3917 <Wx1e@-1026 <Wx1g@-943 <Wx1f@309 <Wx1h@847 -kid'@2747 -kid@3974 -kid'''@6113 <sendc0@6392 -kid''@8437 <sendw0@8437 -kid''''@8438 -kid'''''@8509 <sendw1@9947""",
+    "t": """<add14@-4519 -ksum0@-4425 -rot@-4043 <ksum1@-4035 <tL0@-3916 -rows3@-2513 <sum0@-1124 -rows1@-581 -rows0@-547 <tS0@-522 -code@-376 -rows2@-330 <sub14@-330 <tv1@-73 <kS0@21 <kL1@240 <sum8@625 <rows4@758 <rows7@758 <tL1@870 <rows5@1201 <rows6@1201 <sum12@1872 <tv0@2175 <add6@2348 -join@2651 <sub6@2651 <sum4@5842 >eq1@8337 >own1@9551 +turn1@10448 +code@10468 +turn0@11687 +turn2@11783 +yd0@12998 +back@14080 +yd1@16391""",
+}
+UNUSED = {
+    "v": """Wx1c@53 G0@210 raw10@264 GT0@994 raw8@1048 raw12@1778 kid''@14619 G1@2662 raw0@2717 raw2@3447 GT1@4177 vI0@4282 s2u1@16508 kid'''@16563 yy0@4608 raw4@4662 outO0@5053 s2u1'@17218 raw5@5161 outW0@5552 KT0@5803 kid''''@17969 xo0@6012 kid'''''@18333 pn@6376 xo0'@6431 kid''''''@18697 es0@6741 kid'''''''@19062 vI1@7105 ncd0@7221 x20@7275 x20'@7330 yy1@7431 xx0@7485 xx0'@7540 l20@7594 outO1@7695 u20@7858 outW1@7960 outC0@8180 KT1@8401 xo1@8455 outD0@8510 na@8731 xo1'@8785 wr0@9009 es1@9332 dn@9441 s2u0@9496 ncd1@9651 x21@9706 x21'@9760 xx1@9916 dm@9970 l21@10024 xx1'@10079 M0@10234 u21@10289 outC1@10553 outD1@10774 csi@10995 s2u0'@11049 Wx0d@-1006 csa@11259 kid@11314 limA@11524 wr1@11578 kid'@11755 limT@11909""",
+    "s": """raw14@210 Wx1b@939 A10@1266 A14@1701 Lp0@2136 A8@2252 A12@2718 raw6@3153 A0@3883 A2@4387 Lp1@4822 A6@4937 KG0@5373 A4@5593 A5@5811 AB0@6416 stg0@7315 KG1@7960 top0@8180 cf0@8401 wa0@8622 AB1@9014 stg1@9122 Wx0a@-2767 cov@9916 Wx0b@-2140 Wx0c@-1813 cf1@10623 top1@10844 wa1@11141 Wx1a@-510""",
+    "g": """Wx1f@53 Wx1g@740 Wx1h@1426 sendw0@5982 sendw1@8390 sendc0@8941 Wx0h@-2203 sendc1@11205""",
+    "t": """kS0@82 kv1@359 add14@1149 kL0@1426 tL0@1499 sub6@1638 kv0@2191 tv0@2462 kL1@2756 sum8@2897 sum12@3485 add6@4093 tL1@4441 tv1@5147 sum0@5441 tS0@6068 sum4@6239 kS1@6826 own0@7103 eq0@7804 tS1@8665 cw1@9009 own1@9121 cnt@10180 eq1@10343 cw0@-582 sub14@-470""",
+}
+ROUND = {q: " ".join([w for w in ROUND[q].split() if w[0] not in "<>-+"] + EDGE[q].split()) for q in ROUND}
+KQ = [0, 512, 1536, 2560, 3584, 4096]
+LOADS = ["wts", "feat0", "mkey", "mobj", "cand", "want", "feat", "last"]
+CT = 272
+D = 32
+CY, PE, GA, SCAT, HOP, FLY, FLYW, LOAD, RATE, ROWS = 0.85, 0.54, 1.56, 3.8, 210.0, 2600.0, 2600.0, 1600.0, 300.0, 80000.0
 
 _f, _b, _h, _i, _u = "float32", "bfloat16", "float16", "int32", "uint16"
 _t = lambda n, d: ("sbuf", [128, n], d)
+_l = lambda n, d: ("sbuf", [128, n, 17], d)
 SCRATCH = {
-    "featW": _t(W, _b), "kidi": _t(W, _i), "kid": _t(W + 16 + NS, _f), "yc": _t(8, _f), "end": _t(W + 16, _f), "keyW": _t(W, _b), "idW": _t(W + 16, _f),
-    "A": ("sbuf", [128, 16, 256], _b), "raw": _t(W, _b), "Wx": _t(W, _b),
+    "featW": _t(W, _b), "kidi": _t(W, _i), "kid": _t(D + W + L, _f), "yc": _t(32, _f), "keyW": _t(W, _b),
+    "A": _l(256, _b), "limT": _t(136, _b), "RS3": ("sbuf", [128, 4, 52], _f), "raw": _t(W, _b), "Wx": _t(W, _b),
     "LH": _t(144, _b), "LW": _t(144, _b), "EX": _t(2048, _b), "SH": _t(2048, _b), "R16": ("sbuf", [128, 8, 32], _b),
-    "i1": _t(128, _i), "i1b": _t(128, _i), "i2": _t(16, _i), "i2b": _t(16, _i), "i3": _t(16, _i), "i3b": _t(16, _i), "i4": _t(16, _i), "i5": _t(16, _i),
-    "bi": _t(16, _i), "exb": _t(16, _u), "dg": _t(16, _f), "ib": _t(8, _i), "a0": _t(16, _i), "a1": _t(16, _f), "a2": _t(16, _f), "a3": _t(16, _f), "a4": _t(16, _f), "a5": _t(16, _f),
-    "blk": _t(128, _b), "diag": _t(128, _b), "I16": _t(128, _h), "IN16": _t(128, _h), "IB": _t(128, _b), "IN": _t(128, _b), "INf": _t(128, _f), "F7": _t(128, _f), "F8": _t(128, _f), "IK": _t(128, _b),
-    "ones": _t(128, _f), "Kc": _t(128, _b), "ob": _t(128, _b), "expl": _t(16, _u),
-    "RST": _t(256, _f), "RN": _t(256, _f), "R2": _t(256, _f), "CJ": _t(16, _f), "CJ2": _t(256, _f), "col": _t(16, _f), "wti": _t(1, _i), "wtf": _t(1, _f),
-    "ci": _t(256, _i), "mkb": _t(256, _b), "moi": _t(256, _i), "mk16": _t(256, _h), "mo16": _t(256, _h), "mi": _t(256, _i), "mj": _t(256, _i), "mn": _t(256, _i),
-    "klb": _t(256, _b),
+    "i1": _t(128, _i), "i1b": _t(128, _i), "i2": _t(16, _i), "i2b": _t(16, _i), "i3": _t(16, _i), "i3b": _t(16, _i), "i4": _t(128, _i), "i5": _t(16, _i), "i6": _t(32, _i),
+    "bi": _t(16, _i), "exb": _t(16, _u), "dg": _t(16, _f), "dgn": _t(16, _f), "ib": _t(8, _i), "a0": _t(16, _i), "a1": _t(16, _f), "a2": _t(16, _f), "a3": _t(16, _f), "a4": _t(16, _f), "a5": _t(16, _f),
+    "blk": _t(128, _b), "diag": _t(128, _b), "I16": _t(128, _h), "IB": _t(128, _b), "IN": _t(128, _b), "INf": _t(128, _f), "If": _t(128, _f), "FF": _t(1024, _f),
+    "half": _t(128, _f), "Kc": _l(8, _b), "ob": _t(136, _b), "T1": _t(128, _b), "CW": ("sbuf", [128, 4, 52], _b),
+    "RST": _t(208, _f), "RN": _t(128, _f), "CJ": _t(16, _f), "CJ2": _t(256, _f), "col": _t(16, _f), "wti": _t(1, _i), "wtf": _t(1, _f),
+    "ci": _t(256, _i), "mkb": _t(256, _b), "moi": _t(256, _i), "mk16": _t(256, _b), "mo16": _t(256, _h), "mi": _t(256, _i), "mj": _t(256, _i),
+    "klb": ("sbuf", [128, 8, 32], _b),
     "lai": _t(16, _i), "LX": _t(32, _f), "LT": _t(32, _f), "prev0": _t(16, _f),
-    "X": ("sbuf", [128, 16, 32], _h), "XT": ("sbuf", [128, 16, 32], _h), "Y": ("sbuf", [128, 16, 32], _h), "YT": ("sbuf", [128, 16, 32], _h),
+    "X": ("sbuf", [128, 16, 32], _h), "XT": ("sbuf", [128, 16, 32], _h), "Y": ("sbuf", [128, 8, 32], _b), "PF": _t(512, _f),
+    "XF": ("sbuf", [128, 16, 32], _f), "XG": ("sbuf", [128, 16, 32], _f),
     "G": ("sbuf", [128, 8, 32], _h), "GT": ("sbuf", [128, 8, 32], _h), "PM": _t(512, _h), "PK": _t(512, _b), "S4": ("sbuf", [128, 4, 2, 16], _h),
-    "M": _t(256, _f), "Lp": _t(256, _f), "vm": _t(256, _f), "vI": _t(256, _i), "yy": _t(16, _i), "KG": _t(256, _b), "KT": ("sbuf", [128, 8, 32], _b), "AB": _t(256, _f), "es": _t(256, _i),
-    "x2": _t(32, _i), "l2": _t(32, _i), "l3": _t(32, _i), "u2": _t(32, _u), "top": _t(256, _f), "cf": _t(256, _f),
-    "na": _t(16, _f), "cov": _t(16, _f), "ncd": _t(16, _f), "s1": _t(8 * NP, _f), "s1u": _t(16, _u), "gl": _t(256, _f), "eq2": _t(256, _f), "dsum": _t(256, _f),
-    "dd": _t(16, _f), "s2": _t(16, _f), "s2u": _t(32, _u), "pn": _t(16, _f), "dn": _t(16, _f), "dn2": _t(16, _f),
-    "cs": _t(1, _f), "csi": _t(1, _i), "csa": _t(1, _i), "limA": _t(1, _f), "th": _t(16, _f),
-    "outF": _t(256, _f), "inF": _t(256, _f), "ymo": _t(256, _f), "acc": _t(512, _f),
-    "outC": _t(STEPS * NP * CS, _u), "inC": _t(STEPS * NP * CS, _u), "DW": _t(256, _b), "outW": _t(STEPS * 256, _b), "inW": _t(STEPS * 256, _b),
-    "pv0": ("psum", [128, 16, 32], _f), "pv1": ("psum", [128, 16, 32], _f), "pL": ("psum", [128, 16, 32], _f), "pS": ("psum", [128, 16, 32], _f),
-    "pX0": ("psum", [128, 512], _f), "pX1": ("psum", [128, 512], _f), "pX2": ("psum", [128, 512], _f), "pX3": ("psum", [128, 512], _f),
+    "M": ("sbuf", [128, 8, 32], _f), "Lp": _t(272, _f), "vI": _t(272, _i), "yy": _t(16, _i), "KG": _t(256, _b), "KT": ("sbuf", [128, 8, 32], _b), "AB": _t(256, _f), "es": _t(256, _i),
+    "x2": _t(32, _i), "l2": _t(32, _i), "u2": _t(32, _u), "top": _t(256, _f), "cf": _t(256, _f),
+    "na": _t(16, _f), "cov": _t(16, _f), "ncd": _t(16, _f), "xo": ("sbuf", [128, 8, 3], _h), "xx": ("sbuf", [128, 8, 3], _h), "wa": _t(416, _f), "wr": _t(416, _f),
+    "s2u": _t(16, _u), "pn": _t(16, _f), "dn": _t(16, _f), "dn2": _t(16, _f),
+    "cs": _t(1, _f), "csi": _t(1, _i), "csa": _t(1, _i), "limA": _t(1, _f),
+    "inF": _t(256, _f), "ymo": _t(256, _f), "acc": _t(512, _f),
+    "outC": _t(STEPS * CT, _u), "outD": ("sbuf", [128, STEPS, CT], _u), "inC": _t((STEPS + 1) * CT, _u), "outW": _t(STEPS * 256, _b), "inW": _t(STEPS * 256, _b),
+    "pv0": ("psum", [128, 512], _f), "pv1": ("psum", [128, 512], _f), "pT": ("psum", [128, 9, 52], _f), "pL": ("psum", [128, 30, 17], _f),
+    "pS": ("psum", [128, 16, 32], _f), "pX0": ("psum", [128, 512], _f), "pX1": ("psum", [128, 512], _f), "pX2": ("psum", [128, 512], _f),
 }
-DMAS = ["cand", "want", "wts", "last", "mkey", "mobj", "feat0", "feat", "ymu", "yd0", "yd1"] + ["k%d" % q for q in range(8)] + ["yn%d" % h for h in range(NP)]
+DMAS = ["cand", "want", "wts", "last", "mkey", "mobj", "feat0", "feat", "ymu", "yd0", "yd1", "yd2", "yd3"] + ["k%d" % q for q in range(8)] + ["yn%d" % h for h in range(NP)]
 SEMAPHORES = ["sv", "st", "ss", "sg", "ls"] + ["d_" + n for n in DMAS] + [x + "%d_%d" % (t, h) for x in "cw" for t in range(1, STEPS + 1) for h in range(NP)]
 OWN = {"v": "sv", "t": "st", "s": "ss", "g": "sg"}
 
 
 def make():
-    ops, tags, lag = [], {}, [0.0]
+    ops, tags, lag, seen = [], {}, [0.0, -1], {}
 
     def tag(n):
         if n not in tags:
             tags[n] = {"w": [], "r": [], "base": [], "full": False, "mm": None}
         return tags[n]
 
-    def add(q, call, ns, r=(), w=(), p=(), acc=False, sem=None, lat=0.0, after=()):
+    def add(q, call, ns, r=(), w=(), p=(), acc=False, sem=None, lat=0.0, after=(), nm=None):
         i, pre = len(ops), {}
+        if nm is None:
+            nm = (tuple(w) + tuple(p))[0]
+            nm = nm[:-3] + nm[-1] if nm[:2] in ("in", "ou") else "Wx" + nm[-1] + "abcdefgh"[int(nm[2:-2]) // (2 if q == "g" else 4)] if nm[:2] == "Wx" else nm
+            seen[lag[1], q, nm] = seen.get((lag[1], q, nm), -1) + 1
+            nm += "'" * seen[lag[1], q, nm] if nm[:2] not in ("Wx", "wa") else ""
         for n in r:
             d = tag(n)
             pre.update({j: True for j in d["w"]})
@@ -88,7 +167,7 @@ def make():
         if q == "t":
             for n in tuple(w) + tuple(p):
                 tag(n)["mm"] = i
-        ops.append({"lag": lag[0], "q": q, "call": call, "ns": ns, "pre": pre, "sem": sem, "lat": lat})
+        ops.append({"nm": nm, "step": lag[1], "lag": lag[0], "q": q, "call": call, "ns": ns, "pre": pre, "sem": sem, "lat": lat})
         return i
     return ops, add, lag
 
@@ -99,38 +178,45 @@ def order(ops):
     for i, o in enumerate(ops):
         for j, sem in o["pre"].items():
             post[j].append((i, ops[j]["lat"] + HOP if sem else 0.0))
-    way0 = [0.0] * n
+    when = {(q, w.split("@")[0]): float(w.split("@")[1]) for q in ROUND for w in ROUND[q].split()}
+    due, way, row, row_end = [None] * n, [0.0] * n, set(), {}
     for i in range(n - 1, -1, -1):
-        way0[i] = ns[i] + max([d + way0[k] for k, d in post[i]] + [ops[i]["lat"]])
-
-    def run(lag, look):
-        way = [way0[i] - lag * ops[i]["lag"] for i in range(n)]
-        left, ready, end = [len(o["pre"]) for o in ops], [0.0] * n, 0.0
-        free, cand, seq = {o["q"]: 0.0 for o in ops}, {o["q"]: [] for o in ops}, []
-        for i, o in enumerate(ops):
-            if not left[i]:
-                cand[o["q"]].append(i)
-        while len(seq) < n:
-            now, q = min((max(free[q], min(ready[i] for i in c)), q) for q, c in cand.items() if c)
-            worth = lambda i: way[i] - look * max(0.0, ready[i] - now)
-            i = max(cand[q], key=worth)
-            if ready[i] > now:
-                i = max([k for k in cand[q] if max(now, ready[k]) + ns[k] <= ready[i] + 40.0] or [i], key=worth)
-            cand[q].remove(i)
-            seq.append(i)
-            done = max(now, ready[i]) + ns[i]
-            end = max(end, done + ops[i]["lat"])
-            if q != "x":
-                free[q] = done
-            for k, d in post[i]:
-                ready[k] = max(ready[k], done + d)
-                left[k] -= 1
-                if not left[k]:
-                    cand[ops[k]["q"]].append(k)
-        return end, seq
-    if n not in ORDER:
-        ORDER[n] = min(run(lag, look) for lag in LAGS for look in LOOKS)
-    return ORDER[n][1]
+        o = ops[i]
+        way[i] = ns[i] + max([d + way[k] for k, d in post[i]] + [o["lat"]])
+        edge = (o["q"], {-1: "-", 0: "<", STEPS - 1: ">", STEPS: "+"}.get(o["step"], "") + o["nm"])
+        if edge in when or (0 <= o["step"] < STEPS and (o["q"], o["nm"]) in when):
+            due[i] = PERIOD * min(max(o["step"], 0), STEPS - 1) + when.get(edge, when.get((o["q"], o["nm"])))
+            if 0 < o["step"] < STEPS - 1:
+                row.add(i)
+        elif any(due[k] is not None for k, d in post[i]):
+            due[i] = min(due[k] - d for k, d in post[i] if due[k] is not None) - ns[i]
+    due = [PERIOD * STEPS + END - way[i] if due[i] is None else due[i] for i in range(n)]
+    left, ready, start = [len(o["pre"]) for o in ops], [0.0] * n, [0.0] * n
+    busy, cand = {o["q"]: [] for o in ops}, [(due[i], i) for i in range(n) if not left[i]]
+    while cand:
+        c = min(cand)
+        cand.remove(c)
+        i = c[1]
+        at, b = ready[i], busy[ops[i]["q"]]
+        if i in row:
+            at = max(at, row_end.get(ops[i]["q"], 0.0))
+        if ops[i]["q"] != "x":
+            k = len(b)
+            while k and b[k - 1][1] > at:
+                k -= 1
+            while k < len(b) and b[k][0] < at + ns[i] - 1e-6:
+                at = max(at, b[k][1])
+                k += 1
+            b.insert(k, (at, at + ns[i]))
+        start[i] = at
+        if i in row:
+            row_end[ops[i]["q"]] = at + ns[i]
+        for k, d in post[i]:
+            ready[k] = max(ready[k], at + ns[i] + d)
+            left[k] -= 1
+            if not left[k]:
+                cand.append((due[k], k))
+    return sorted(range(n), key=lambda i: (start[i], i))
 
 
 def emit(g, T, ops, seq):
@@ -167,28 +253,15 @@ def emit(g, T, ops, seq):
 
 def rank_program(g, core, T, topo):
     rank, n = T.rank_of(core), len(T.cores)
-    wants = lambda b, t, h: b[:, 256 * t + 16 * PARTS[h][0]:256 * t + 16 * PARTS[h][1]]
-
-    def helper(a, b):
-        free = [c for c in topo.cores_of(a) if c not in T.cores and topo.may_write(c, b) and topo.die(c) != topo.die(a)]
-        return free[0] if RELAY and free and topo.chip(a) != topo.chip(b) else None
     if rank is None:
-        for a, b in zip(T.cores, T.cores[1:] + T.cores[:1]):
-            if helper(a, b) == core:
-                k = len(topo.engines(a, core)) - len(topo.engines(a, b))
-                for t in range(1, STEPS):
-                    for h in range(NP):
-                        sem = T.sem["w%d_%d" % (t, h)]
-                        g.wait_ge(sem, k)
-                        g.remote_dma(wants(T.inW, t, h), wants(T.inW, t, h), sem, T.sem.ls, topo.addr(b)[1], topo.addr(b)[0], topo.mask(core, b))
-                g.wait_ge(T.sem.ls, (STEPS - 1) * NP * len(topo.engines(core, b)))
         return
     ops, add, lag = make()
     v, te, sc = g.vector, g.tensor, g.scalar
     nxt, prv = T.cores[(rank + 1) % n], T.cores[(rank - 1) % n]
-    hlp, nin = helper(core, nxt), len(topo.engines(prv, core))
+    nin = len(topo.engines(prv, core))
     cy = lambda k: max(64.0, k) * CY
     ga = lambda k: (60.0 + GA * k) * CY
+    NP = len(PARTS)
 
     def ts(ns, out, in0, s1, s2, o0, o1, r, w=(), p=()):
         args = (out, in0, s1, s2, o0) if o1 is None else (out, in0, s1, s2, o0, o1)
@@ -209,19 +282,20 @@ def rank_program(g, core, T, topo):
     def act(ns, out, a, f, r, w=(), p=(), **kw):
         add("s", lambda: sc.activation(out, a, f, **kw), ns, r, w, p)
 
-    def copy(e, k, out, a, r, w=(), p=(), fast=1.0):
+    def copy(e, dims, out, a, r, w=(), p=(), fast=1.0):
+        k = dims[0] * dims[1]
         if e == "v":
             cp(cy(k * fast), out, a, r, w, p)
         elif e == "s":
             act(cy(k), out, a, AF.Copy, r, w, p)
         else:
-            add("g", lambda: g.affine_select(out, a, [[0, k]], ALU.is_equal, 0.0, 0, 0), 180 + 2 * k * CY, r, w, p)
+            add("g", lambda: g.affine_select(out, a, [[0, x] for x in dims if x > 1], ALU.is_equal, 0.0, 0, 0), 180 + 2 * k * CY, r, w, p)
 
-    def mm(k, out, l, rh, st, sp, r, w, part=False):
+    def mm(k, out, l, rh, st, sp, r, w, part=False, nm=None):
         if part:
-            add("t", lambda: te.matmul(out, l, rh, st, sp), max(64, k) * PE, r, p=(w,))
+            add("t", lambda: te.matmul(out, l, rh, st, sp), max(64, k) * PE, r, p=(w,), nm=nm)
         else:
-            add("t", lambda: te.matmul(out, l, rh, st, sp), max(64, k) * PE, r, (w,), acc=not st)
+            add("t", lambda: te.matmul(out, l, rh, st, sp), max(64, k) * PE, r, (w,), acc=not st, nm=nm)
 
     def fill(ns, ap, x, w=(), p=()):
         add("v", lambda: v.memset(ap, x), ns, (), w, p)
@@ -232,20 +306,29 @@ def rank_program(g, core, T, topo):
 
     def dma(q, out, in_, name, nbytes, r=(), w=()):
         last["bytes"][0] = nbytes + ROWS + (0.0 if r else last["bytes"][0])
-        last[q] = [add(q, lambda: (sc if q == "s" else g.sync).dma_start(out, in_), 60.0, r, w, sem=("d_" + name, 16), lat=LOAD + last["bytes"][0] / RATE, after=() if r else last[q])]
+        last[q] = [add(q, lambda: (sc if q == "s" else g.sync).dma_start(out, in_), 60.0, r, w, sem=("d_" + name, 16), lat=LOAD + last["bytes"][0] / RATE, after=() if r else last[q], nm=name)]
 
-    def send(out, in_, sem, r, w, via=None, fly=FLY):
-        rid, pid, _se = topo.addr(via or nxt)
-        mask = topo.mask(core, via) & ~topo.mask(core, nxt) if via else topo.mask(core, nxt)
-        i = add("g", lambda: g.remote_dma(out, in_, T.sem[sem], T.sem.ls, pid, rid, mask), 400.0, r, sem=("ls", bin(mask).count("1")))
+    def send(out, in_, sem, r, w, fly=FLY):
+        rid, pid, _se = topo.addr(nxt)
+        mask = topo.mask(core, nxt)
+        if isinstance(in_, list):
+            call = lambda: g.remote_dma_fused([RemoteDMATransfer(dst_ids=[DstId(rid=rid, pnc=pid)], dma_engine_mask=mask, remote_sem=T.sem[sem], srcs=in_, dsts=[out], alu_op=2)], local_sem=T.sem.ls)
+        else:
+            call = lambda: g.remote_dma(out, in_, T.sem[sem], T.sem.ls, pid, rid, mask)
+        i = add("g", call, 400.0, r, sem=("ls", bin(mask).count("1")), nm="send" + sem[0] + sem[-1])
         add("x", None, fly, (), w, sem=(sem, nin), after=(i,))
+
+    def bank(ps, k):
+        return T[ps][:, 0:k] if ps[1] in "Xv" else T[ps][:, 0:k // 32, :] if ps == "pS" else T[ps][:, 0:k // 16, 0:16]
     C = lambda j: T.col[:, j:j + 1]
-    M1, M0, SCT, BIT, DUMP, THR, OFF, K0, K1, YC = range(10)
+    M1, M0, SCT, BIT, DUMP, OFF, K0, K1, DU0 = range(9)
     S = cy(16)
-    at = lambda t, c: 2 * CS * t + 16 * c + (16 if c >= NC else 0)
+    at = lambda t, h: CT * t + (0 if h else 144)
+    own = lambda h, c: W + L - 16 * PARTS[h][1] + 16 * (c - PARTS[h][0])
+    tag_all = lambda s: [s + "%d" % h for h in range(NP)]
 
     loads = {"wts": (T.wti[:], T.wts[:], 512, ("wti",)), "feat0": (T.featW[:, 0:W // 2], T.feat[:, 0:W // 2], 524288, ("feat0",)),
-             "cand": (T.ci[:], T.cand[:], 131072, ("ci",)), "want": (T.inW[:, 0:256], T.want[:], 65536, ["inW0_%d" % h for h in range(NP)]),
+             "cand": (T.ci[:], T.cand[:], 131072, ("ci",)), "want": (T.inW[:, 0:256], T.want[:], 65536, tag_all("inW0_")),
              "feat": (T.featW[:, W // 2:W], T.feat[:, W // 2:W], 524288, ("feat",)), "mkey": (T.mkb[:], T.mkey[:], 65536, ("mkb",)),
              "mobj": (T.moi[:], T.mobj[:], 131072, ("moi",)), "last": (T.lai[:], T.last[:], 8192, ("lai",))}
     for nm in LOADS:
@@ -257,12 +340,14 @@ def rank_program(g, core, T, topo):
     iota(16, T.i5[:], [[0, 16]], 0, 1, "i5")
     iota(16, T.i2[:], [[1, 16]], 128, -1, "i2")
     iota(128, T.i1[:], [[16, 8], [0, 16]], 15, -1, "i1")
-    iota(16, T.i4[:], [[1, 16]], 0, 0, "i4")
     iota(16, T.i3[:], [[1, 16]], 0, 1, "i3")
-    fill(S, T.Kc[:], 0.0, w=("Kc",))
-    fill(S, T.Kc[32:33, :], -RC * RS, w=("Kc",))
-    iota(128, T.Kc[0:1, :], [[0, 8], [8192, 16]], 6144, 0, "Kc", **small)
-    iota(W + 16, T.idW[:], [[1, W + 16]], W, 0, "idW", **small)
+    fill(cy(68), T.Kc[:], 0.0, w=("Kc",))
+    fill(S, T.Kc[32:33, :, 0:16], -RC * RS, w=("Kc",))
+    fill(S, T.Kc[32:33, :, 16], BIG, w=("Kc",))
+    iota(136, T.Kc[0:1, :, :], [[0, 8], [8192, 17]], 6144, 0, "Kc", **small)
+    for h, (c0, c1) in enumerate(PARTS):
+        iota(16, T.i6[:, 2 * c0:2 * c1], [[0, 2], [16, c1 - c0]], own(h, c0), 0, "i6")
+    iota(128, T.i4[:], [[0, 8], [1, 16]], 0, 0, "i4")
     fill(cy(128), T.LH[:], 0.0, w=("LH",))
     ts(S, T.i2b[:], T.i2[:], 15, None, ALU.bitwise_and, None, ("i2",), ("i2b",))
     ts(S, T.bi[:], T.i5[:], 15, None, ALU.bitwise_and, None, ("i5",), ("bi",))
@@ -276,33 +361,43 @@ def rank_program(g, core, T, topo):
     ts(S, T.LH[:, 15:143:16], T.blk[:, 0::16], RS, None, ALU.mult, None, ("blk",), ("LH",))
     cp(S, C(M1), T.ib[:, 0:1], ("ib0",), ("m1",))
     ts(S, C(M0), T.ib[:, 0:1], -1.0, 1.0, ALU.mult, ALU.add, ("ib0",), ("m0",))
-    ts(S, C(SCT), T.ib[:, 1:2], -1.0, 1.0, ALU.mult, ALU.add, ("ib1",), ("sct",))
-    ts(S, C(DUMP), T.bi[:, 0:1], 2.0 * W, None, ALU.add, None, ("bi",), ("dump",))
-    ts(S, C(YC), T.bi[:, 0:1], W + 16.0, None, ALU.add, None, ("bi",), ("ycc",))
-    ts(S, T.yc[:], T.i4[:, 0:8], 16.0, C(YC), ALU.mult, ALU.add, ("i4", "ycc"), ("yc",))
-    fill(S, T.kid[:, W:W + 16], 0.0, p=("kid",))
+    ts(S, C(SCT), T.ib[:, 1:2], -1.0, 1.0, ALU.mult, ALU.add, ("ib1",), p=("sct",))
+    cp(S, C(SCT + 1), T.ib[:, 1:2], ("ib1",), p=("sct",))
+    cp(S, C(DUMP), T.bi[:, 0:1], ("bi",), ("dump",))
+    ts(S, T.yc[:], T.i6[:], C(DUMP), None, ALU.add, None, ("i6", "dump"), ("yc",))
+    fill(S, T.kid[:, 0:D], 0.0, p=("kid",))
     tt(cy(256), T.IB[:], T.blk[:], T.diag[:], ALU.mult, ("blk", "diag"), ("IB",))
     cp(S, T.I16[:], T.IB[:], ("IB",), ("I16",))
-    for nm, x in (("IN", -1.0), ("IN16", -1.0), ("INf", -1.0), ("IK", KS)):
+    for nm, x in (("IN", -1.0), ("INf", -1.0), ("T1", 1.0 / DB)):
         ts(cy(128 if nm == "INf" else 64), T[nm][:], T.IB[:], x, None, ALU.mult, None, ("IB",), (nm,))
 
     for h, (c0, c1) in enumerate(PARTS):
-        cp(cy(16 * NC), T.inC[:, at(0, c0):at(0, c0) + 16 * NC], T.ci[:, 16 * c0:16 * c1], ("ci",), ("inC0_%d" % h,))
+        cp(cy(16 * (c1 - c0)), T.inC[:, at(0, h):at(0, h) + 16 * (c1 - c0)], T.ci[:, 16 * c0:16 * c1], ("ci",), ("inC0_%d" % h,))
     ts(S, T.wtf[:], T.wti[:], 1.0 / RS, None, ALU.mult, None, ("wti",), ("wtf",))
-    fill(cy(256), T.R2[:], 2.0, w=("R2",))
-    fill(S, T.R2[:, 0::16], 0.0, p=("R2",))
-    act(cy(256), T.RN[:], T.R2[:], AF.Copy, ("R2",), ("RN",), scale=-NONE / 2, bias=float(NONE))
-    act(cy(256), T.RST[:], T.R2[:], AF.Copy, ("R2",), ("RST",), scale=-BIG, bias=BIG)
-    ts(S, C(BIT), C(SCT), 4097.0, -1.0, ALU.mult, ALU.add, ("sct",), ("bit",))
-    ts(S, C(OFF), C(SCT), 4096.0, None, ALU.mult, None, ("sct",), ("off",))
-    cp(S, T.expl[:], T.i4[:], ("i4",), ("expl",))
-    ts(S, C(K0), C(M0), 1.0 / 64, None, ALU.mult, None, ("m0",), ("k0",))
-    ts(S, C(K1), C(M1), 1.0 / 64, None, ALU.mult, None, ("m1",), ("k1",))
-    for i in range(8 - YP, 8):
-        act(cy(128), T["F%d" % (i + 1)][:], T.IB[:], AF.Copy, ("IB",), p=("F",), scale=float(i + 1))
+    fill(cy(128), T.RN[:], 0.0, w=("RN",))
+    fill(S, T.RN[:, 0::16], float(NONE), w=("RN",))
+    for e in range(2):
+        ts(S, C(DU0 + e), T.bi[:, 0:1], 16.0 * e, 1.0 / DB, ALU.add, ALU.mult, ("bi",), p=("dmp",))
+    fill(S, T.outD[:, :, 128:144], 0, w=("nought",))
+    for i in range(8 - max(YP), 8):
+        act(cy(128), T.FF[:, 128 * (7 - i):128 * (8 - i)], T.IB[:], AF.Copy, ("IB",), p=("F",), scale=float(i + 1))
+    act(cy(128), T.If[:], T.IB[:], AF.Copy, ("IB",), ("If",))
     fill(S, T.limA[:], RS * (LIM - 1), w=("limA",))
     fill(S, T.ob[:], 1.0, w=("ob",))
-    fill(cy(128), T.ones[:], 1.0, w=("ones",))
+    fill(cy(128), T.half[:], 0.5, w=("half",))
+    ts(S, T.dgn[:], T.dg[:], -1.0, None, ALU.mult, None, ("dg",), ("dgd",))
+    for b in range(16):
+        act(cy(128), T.EX[:, 128 * b:128 * b + 128], T.blk[:], AF.Copy, ("blk", "dgd"), ("EX%d" % b,), scale=T.dgn[:, b:b + 1])
+    fill(cy(104), T.CW[:], 0.0, w=("CW",))
+    for a in (2, 36):
+        ts(S, T.CW[:, :, a:a + 16], T.i4[:, 0:64], C(DUMP), BIG, ALU.is_ge, ALU.mult, ("i4", "dump"), p=("CW",))
+    fill(S, T.CW[:, :, 1:36:34], (2048.0 + D) / DB, p=("CW",))
+    for e, (a, x) in enumerate(((0, 18), (18, 52))):
+        act(cy(4 * (x - a)), T.RS3[:, :, a:x], T.CW[:, :, a:x], AF.Identity, ("CW", "dmp"), p=("RS3",), scale=0.0, bias=C(DU0 + e))
+    fill(S, T.RS3[:, :, 0:19:18], BIG, w=("RS3",))
+    act(cy(208), T.RST[:], T.RS3[:], AF.Copy, ("RS3",), ("RST",))
+    fill(cy(136), T.A[:, :, 16], 0.0, w=["A%d" % c for c in range(16)])
+    fill(cy(68), T.limT[:], RS * (LIM - 1), w=("limT",))
     ts(S, T.i3b[:], T.i3[:], 15, None, ALU.bitwise_and, None, ("i3",), ("i3b",))
     ts(S, T.a0[:], T.i3[:], 14, None, ALU.bitwise_and, None, ("i3",), ("a0",))
     ts(S, T.a2[:], T.i3b[:], 4.0, -2.0, ALU.is_ge, ALU.mult, ("i3b",), ("a2",))
@@ -315,258 +410,229 @@ def rank_program(g, core, T, topo):
     cp(S, T.R16[:, :, 0:16], T.IB[:], ("IB",), p=("R16",))
     cp(S, T.R16[:, :, 16:32], T.IB[:], ("IB",), p=("R16",))
     for b in range(16):
-        if SHQ[b] == "v":
-            cp(S, T.SH[:, 128 * b:128 * b + 128], T.R16[:, :, b:b + 16], ("R16",), p=("SH",))
-        else:
-            act(cy(128), T.SH[:, 128 * b:128 * b + 128], T.R16[:, :, b:b + 16], AF.Copy, ("R16",), p=("SH",))
+        copy(SHQ[b], (8, 16), T.SH[:, 128 * b:128 * b + 128], T.R16[:, :, b:b + 16], ("R16",), p=("SH",), fast=0.5)
     for s in range(2):
         cp(S, T.S4[:, :, s, :], T.R16[:, 1 - s::2, 0:16], ("R16",), p=("S4",))
     for e, m, nm in ((0, M0, "m0"), (1, M1, "m1")):
         ts(S, T.PM[:, 384 * e:384 * e + 128], T.I16[:], C(m), None, ALU.mult, None, ("I16", nm), p=("PM",))
         ts(S, T.PM[:, 128 + 128 * e:256 + 128 * e], T.S4[:], C(m), None, ALU.mult, None, ("S4", nm), p=("PM",))
     ts(cy(256), T.PK[:], T.PM[:], KS, None, ALU.mult, None, ("PM",), ("PK",))
+    act(cy(512), T.PF[:], T.PK[:], AF.Copy, ("PK",), ("PF",), scale=-1.0 / KS)
 
-    def flip(src, ns, X, XT, nx, c0=0, c1=16, sub=0.0):
-        k = 16 * (c1 - c0)
-        ts(cy(k), X[:, c0:c1, 0:16], src, sub, C(M0), ALU.subtract, ALU.mult, (ns, "m0"), p=(nx,))
-        ts(cy(k), X[:, c0:c1, 16:32], src, sub, C(M1), ALU.subtract, ALU.mult, (ns, "m1"), p=(nx,))
-        tr(cy(k), XT[:, c0:c1, :], X[:, c0:c1, :], (nx,), (nx + "T",))
-    cp(cy(128), T.mk16[:], T.mkb[:], ("mkb",), ("mk16",))
-    ts(cy(256), T.mo16[:], T.moi[:], 2048.0, None, ALU.subtract, None, ("moi",), ("mo16",))
-    for ps, src in (("pv1", "mk16"), ("pL", "mo16")):
-        for b in range(16):
-            mm(16, T[ps][:, 0:8, b::16], T.SH[:, 128 * b:128 * b + 128], T[src][:, b::16], True, True, ("SH", src), ps, part=True)
-    flip(T.pv1[:, 0:8, :], "pv1", T.X, T.XT, "X")
-    flip(T.pL[:, 0:8, :], "pL", T.Y, T.YT, "Y")
-    for e, (l, nl, XT, nx) in enumerate((T.IK, "IK", T.XT, "XT") if x < 2 else (T.IN16, "IN16", T.YT, "YT") for x in range(4)):
-        mm(256, T.pv1[:, 0:8, :], l[:], XT[:, :, 16 * (e % 2):16 * (e % 2) + 16], e == 0, e == 3, (nl, nx), "pv1")
-    tt(cy(256), T.M[:], T.pv1[:, 0:8, :], T.CJ2[:], ALU.subtract, ("pv1", "CJ2"), ["M%d" % h for h in range(NP)])
+    act(cy(256), T.mk16[:], T.mkb[:], AF.Copy, ("mkb",), ("mk16",), scale=KS)
+    ts(cy(256), T.mo16[:], T.moi[:], -1.0, 2048.0, ALU.mult, ALU.add, ("moi",), ("mo16",))
+    for b in range(16):
+        for e, src in enumerate(("mk16", "mo16")):
+            mm(16, T[MB][:, b:256:16], T.SH[:, 128 * b:128 * b + 128], T[src][:, b::16], e == 0, e == 1, ("SH", "mk16", "mo16"), MB, part=True, nm="rot")
+    for e in range(2):
+        act(cy(256), T.XF[:, :, 16 * e:16 * e + 16], T[MB][:, 0:256], AF.Copy, (MB, "m0", "m1"), p=("XF",), scale=C((M0, M1)[e]))
+    tr(cy(512), T.XG[:], T.XF[:], ("XF",), ("XG",))
+    mm(1024, T[MB][:, 0:256], T.INf[:], T.CJ2[:], True, False, ("INf", "CJ2"), MB, nm="code")
+    for e in range(2):
+        mm(1024, T[MB][:, 0:256], T.If[:], T.XG[:, :, 16 * e:16 * e + 16], False, e == 1, ("If", "XG"), MB, nm="join")
+    act(cy(256), T.M[:], T[MB][:, 0:256], AF.Copy, (MB,), tag_all("M"))
     ts(S, T.LX[:, 0:16], T.lai[:], C(M0), None, ALU.mult, None, ("lai", "m0"), p=("LX",))
     ts(S, T.LX[:, 16:32], T.lai[:], C(M1), None, ALU.mult, None, ("lai", "m1"), p=("LX",))
     tr(S, T.LT[:], T.LX[:], ("LX",), ("LT",))
     tt(S, T.prev0[:], T.LT[:, 0:16], T.LT[:, 16:32], ALU.add, ("LT",), ("prev0",))
-    scan(S, T.th[:], T.R2[:, 0:16], T.dg[:], ALU.mult, ALU.add, ("R2", "dg"), ("th",))
-    ts(S, C(THR), T.th[:, 15:16], 2.0, None, ALU.mult, None, ("th",), ("thr",))
     ts(cy(128), T.LW[:], T.LH[:], T.wtf[:], None, ALU.mult, None, ("LH", "wtf"), ("LW",))
-    for b in range(16):
-        act(cy(128), T.EX[:, 128 * b:128 * b + 128], T.blk[:], AF.Copy, ("blk", "dg"), p=("EX",), scale=T.dg[:, b:b + 1])
-    for b in range(16):
-        mm(256, T.pS[:, 0:8, :], T.LW[:, 15 - b:143 - b], T.featW[:, 256 * b:256 * b + 256], b == 0, b == 15, ("LW", "feat" if b > 7 else "feat0"), "pS")
-    tag_all = lambda s: [s + "%d" % h for h in range(NP)]
-    cp(cy(256), T.mi[:], T.pS[:, 0:8, :], ("pS",), tag_all("mi"))
-    ts(cy(256), T.mj[:], T.mi[:], 63, None, ALU.bitwise_and, None, tag_all("mi"), tag_all("mj"))
-    cp(cy(256), T.klb[:], T.mj[:], tag_all("mj"), ("klb",))
 
-    def keys():
-        for i in range(8):
-            ps = KB[i % len(KB)]
+    def keys(x):
+        for b in range(8 * x, 8 * x + 8):
+            mm(256, T.pS[:, 0:8, :], T.LW[:, 15 - b:143 - b], T.featW[:, 256 * b:256 * b + 256], b % 8 == 0, b % 8 == 7, ("LW", "feat" if x else "feat0"), "pS", nm="ksum%d" % x)
+        cp(cy(256), T.mi[:], T.pS[:, 0:8, :], ("pS",), ("mi",))
+        ts(cy(256), T.mj[:], T.mi[:], 63, None, ALU.bitwise_and, None, ("mi",), ("mj",))
+        ts(cy(256), T.klb[:], T.mj[:], -1.0, None, ALU.mult, None, ("mj",), ("klb",))
+        for i in range(4 * x, 4 * x + 4):
+            ps = KB[i]
             for e in range(2):
                 b = 2 * i + e
-                mm(256, T[ps][:, 256 * e:256 * e + 256] if ps[1] == "X" else T[ps][:, 8 * e:8 * e + 8, :], T.EX[:, 128 * b:128 * b + 128], T.klb[:], True, True, ("EX", "klb"), ps, part=True)
-            if KEYQ[i] == "s":
-                act(cy(512), T.keyW[:, 512 * i:512 * i + 512], T[ps][:], AF.Copy, (ps,), p=("keyW",))
-            else:
-                cp(cy(512), T.keyW[:, 512 * i:512 * i + 512], T[ps][:], (ps,), p=("keyW",))
+                mm(256, T[ps][:, 256 * e:256 * e + 256] if ps != "pS" else T[ps][:, 8 * e:8 * e + 8, :], T.EX[:, 128 * b:128 * b + 128], T.klb[:], True, True, ("EX%d" % b, "klb"), ps, part=True, nm="rows%d" % i)
+            copy(KEYQ[i], (512, 1), T.keyW[:, 512 * i:512 * i + 512], T[ps][:], (ps,), p=("keyW",))
+    keys(0)
     for q, (a, e) in enumerate(zip(KQ, KQ[1:])):
         for x in range(a, e, 512):
-            if KIDQ[x // 512] == "v":
-                cp(cy(512), T.kid[:, x:x + 512], T.kidi[:, x:x + 512], ("kidi%d" % q,), p=("kid",))
-            elif KIDQ[x // 512] == "s":
-                act(cy(512), T.kid[:, x:x + 512], T.kidi[:, x:x + 512], AF.Copy, ("kidi%d" % q,), p=("kid",))
-            else:
-                add("g", lambda x=x: g.affine_select(T.kid[:, x:x + 512], T.kidi[:, x:x + 512], [[0, 512]], ALU.is_equal, 0.0, 0, 0), 180 + 1024 * CY, ("kidi%d" % q,), p=("kid",))
+            copy(KIDQ[x // 512], (512, 1), T.kid[:, D + x:D + x + 512], T.kidi[:, x:x + 512], ("kidi%d" % q,), p=("kid",))
 
-    def mounts(t, c0, c1, hs):
-        N, lb, q = lambda *s: [x + "%d" % h for x in s for h in hs], slice(c0, c1), 5 * t % 16
-        prev, prn = (T.inC[:, 2 * CS * t + 128 + c0:2 * CS * t + 128 + c1], N("inC%d_" % t)) if t else (T.prev0[:, lb], ["prev0"])
-        ts(S, T.pn[:, lb], prev, T.CJ[:, q:q + 1], None, ALU.add, None, prn + ["CJ"], N("pn"))
-        ts(S, T.na[:, lb], T.vI[:, 16 * c0 + 15:16 * c1:16], T.limA[:], (1 - RC) * RS, ALU.subtract, ALU.is_ge, N("vI") + ["limA"], N("na"))
-        tt(S, T.dn[:, lb], T.pS[:, c0 // 2:c1 // 2, q::16], T.pn[:, lb], ALU.subtract, ["pS"] + N("pn"), N("dn"))
-        tt(S, T.dn2[:, lb], T.dn[:, lb], T.na[:, lb], ALU.mult, N("dn", "na"), N("dm"))
-        tt(S, T.M[:, 16 * c0 + q:16 * c1:16], T.M[:, 16 * c0 + q:16 * c1:16], T.dn2[:, lb], ALU.add, N("dm", "M"), N("M"))
+    def mounts(t):
+        N, q = lambda *s: [y for x in s for y in tag_all(x)], 5 * t % 16
+        prev, prn = (T.inC[:, CT * t + 128:CT * t + 144], N("inC%d_" % t)) if t else (T.prev0[:], ["prev0"])
+        ts(S, T.pn[:], prev, T.CJ[:, q:q + 1], None, ALU.add, None, prn + ["CJ"], ("pn",))
+        ts(S, T.na[:], T.vI[:, 0::17], T.limA[:], (1 - RC) * RS, ALU.subtract, ALU.is_ge, N("vI") + ["limA"], ("na",))
+        tt(S, T.dn[:], T.pS[:, 0:8, q::16], T.pn[:], ALU.subtract, ("pS", "pn"), ("dn",))
+        tt(S, T.dn2[:], T.dn[:], T.na[:], ALU.mult, ("dn", "na"), ("dm",))
+        tt(S, T.M[:, :, q::16], T.M[:, :, q::16], T.dn2[:], ALU.add, ["dm"] + N("M"), N("M"))
 
-    def writers(c0, c1, hs):
-        N, lb, ls, nl = lambda *s: [x + "%d" % h for x in s for h in hs], slice(c0, c1), slice(16 * c0, 16 * c1), 16 * (c1 - c0)
-        s1, last16 = T.s1[:, lb], lambda b: b[:, 16 * c0 + 15:16 * c1:16]
-        ts(S, T.ncd[:, lb], last16(T.es), float(NONE), C(DUMP), ALU.is_ge, ALU.mult, N("es") + ["dump"], N("ncd"))
-        tt(S, s1, T.yy[:, lb], T.ncd[:, lb], ALU.max, N("yy", "ncd"), N("s1_"))
-        ts(S, T.s1u[:, lb], s1, 4096.0, None, ALU.subtract, None, N("s1_"), N("s1u"))
-        act(ga(nl), T.gl[:, ls], T.idW[:].indirect(T.s1u[:, lb]), AF.Copy, ["idW"] + N("s1u"), N("gl"))
-        tt(ga(nl), T.eq2[:, ls], s1.indirect(T.expl[:, 0:c1 - c0]), T.gl[:, ls], ALU.is_equal, N("s1_", "gl") + ["expl"], N("eq2_"))
-        scan(cy(nl), T.dsum[:, ls], T.R2[:, 0:nl], T.eq2[:, ls], ALU.mult, ALU.add, ["R2"] + N("eq2_"), N("dsum"))
-        ts(S, T.dd[:, lb], last16(T.dsum), C(THR), C(DUMP), ALU.is_ge, ALU.mult, N("dsum") + ["thr", "dump"], N("dd"))
-        tt(S, T.s2[:, lb], s1, T.dd[:, lb], ALU.max, N("s1_", "dd"), N("s2_"))
-        ts(S, T.s2u[:, 2 * c0:2 * c1:2], T.s2[:, lb], 4096.0, None, ALU.subtract, None, N("s2_"), N("s2u"))
-    nx = [0]
+    def writers(c0, c1, hs, ps):
+        N, lb, nc = lambda *s: [x + "%d" % h for x in s for h in hs], slice(c0, c1), c1 - c0
+        k, pr, ws = nc // 2, slice(c0 // 2, c1 // 2), slice(26 * c0, 26 * c1)
+        ts(S, T.xo[:, pr, 0:2], T.yy[:, lb], 2048.0, None, ALU.subtract, None, N("yy"), p=N("xo"))
+        ts(S, T.xo[:, pr, 2], T.yy[:, c0 + 1:c1:2], 2048.0, None, ALU.subtract, None, N("yy"), p=N("xo"))
+        ts(S, T.ncd[:, lb], T.es[:, 16 * c0 + 15:16 * c1:16], -1.0, NONE - 2048.0 - D, ALU.mult, ALU.add, N("es"), N("ncd"))
+        tt(S, T.xx[:, pr, 1:3], T.xo[:, pr, 0:2], T.ncd[:, lb], ALU.min, N("xo", "ncd"), p=N("xx"))
+        tt(S, T.xx[:, pr, 0], T.xo[:, pr, 0], T.ncd[:, c0:c1:2], ALU.min, N("xo", "ncd"), p=N("xx"))
+        mm(52 * k, T[ps][:, 0:k, :], T.IB[:], T.CW[:, 0:k, :], True, False, ("IB", "CW"), ps, nm=N("cw")[0])
+        for b in range(16):
+            mm(3 * k, T[ps][:, 0:k, 2 + b:52:17], T.IB[:], T.xo[:, pr, :], False, False, N("xo"), ps, nm=N("own")[0])
+        mm(nc, T[ps][:, 0:k, 1:36:34], T.T1[:], T.xx[:, pr, 1:3], False, False, ["T1"] + N("xx"), ps, nm=N("eq")[0])
+        for b in range(16):
+            mm(3 * k, T[ps][:, 0:k, 2 + b:52:17], T.EX[:, 128 * b:128 * b + 128], T.xx[:, pr, :], False, b == 15, N("xx"), ps, nm=N("eq")[0])
+        act(cy(52 * k), T.wa[:, ws], T[ps][:, 0:k, :], AF.Abs, (ps,), N("wa"))
+        scan(cy(52 * k), T.wr[:, ws], T.wa[:, ws], T.RST[:, 0:52 * k], ALU.min, ALU.max, ["RST"] + N("wa"), N("wr"))
+        for e in range(2):
+            ts(S, T.s2u[:, c0 + e:c1:2], T.wr[:, 26 * c0 + 17 + 34 * e:26 * c1:52], DB, None, ALU.mult, None, N("wr"), p=N("s2u"))
+
     for t in range(STEPS):
-        final, q = t == STEPS - 1, 5 * t % 16
+        final = t == STEPS - 1
+        lag[1] = t
         for h, (c0, c1) in enumerate(PARTS):
             N = lambda s: s + "%d" % h
             lag[0] = LAG * h
-            l0, l1, nl, o, ob, hc = 16 * c0, 16 * c1, 16 * NC, at(t, c0), 2 * CS * t + 128 + c0, NC // 2
+            NC, o = c1 - c0, at(t, h)
+            l0, l1, nl, ob = 16 * c0, 16 * c1, 16 * NC, CT * t + 128 + c0
             ls, lb, pr = slice(l0, l1), slice(c0, c1), slice(c0 // 2, c1 // 2)
-            iw, ic, pv = "inW%d_%d" % (t, h), "inC%d_%d" % (t, h), "pv%d" % (h % 2)
-            last16 = lambda b: b[:, l0 + 15:l1:16]
-            Wa = T.inW[:, 256 * t + l0:256 * t + l1]
-            for k in range(16 if NX else 0):
-                out, src = T.Wx[:, 16 * l0 + k:16 * (l0 + NX):16], T.inW[:, 256 * t + l0:256 * t + l0 + NX]
-                if WXQ[k] == "v" or t == 0:
-                    cp(cy(NX / 2), out, src, (iw,), p=(N("Wx"),))
-                elif WXQ[k] == "s":
-                    act(cy(NX), out, src, AF.Copy, (iw,), p=(N("Wx"),))
+            iw, ic, pv = "inW%d_%d" % (t, h), "inC%d_%d" % (t, h), "pv%d" % h
+            nf = 16 * sum(m for e, m in CH[h] if e == "f")
+            wx = lambda a, k: [N("Wx%d_" % y) for y in range(a, a + k)]
+            Wk = lambda e, a, m: T.Wx[:, 16 * a + e:16 * (a + m):16]
+            for e, qu in enumerate(WXQ[h] if t else WX0[h]):
+                m = nf if e else nl
+                if qu == "s":
+                    act(cy(m), Wk(e, l0, m), T.inW[:, 256 * t + l0:256 * t + l0 + m], AF.Abs, (iw,), wx(e, 1))
+                elif t:
+                    copy(qu, (m, 1), Wk(e, l0, m), Wk(0, l0, m), wx(0, 1), wx(e, 1), fast=0.5)
                 else:
-                    add("g", lambda out=out, src=src: g.affine_select(out, src, [[0, NX]], ALU.is_equal, 0.0, 0, 0), 180 + 2 * NX * CY, (iw,), p=(N("Wx"),))
+                    copy(qu, (m, 1), Wk(e, l0, m), T.inW[:, l0:l0 + m], (iw,), wx(e, 1), fast=0.5)
             c = c0
-            for calls in CH:
-                a, k, x = 16 * (c - c0), sum(m for e, m in calls), 0
-                if calls[0][0] == "f":
-                    for e, m in calls:
-                        tt(ga(256 * m), T.raw[:, 256 * (c + x):256 * (c + x + m)], T.featW[:].indirect(T.inC[:, o + a + 16 * x:o + a + 16 * (x + m)]),
-                           T.Wx[:, 256 * (c + x):256 * (c + x + m)], ALU.subtract, ("feat", "feat0", ic, N("Wx")), ("raw%d" % (c + x),))
-                        x += m
-                    act(cy(256 * k), T.A[:, c:c + k, :], T.raw[:, 256 * c:256 * (c + k)], AF.Abs, ["raw%d" % y for y in range(c, c + k)], ["A%d" % y for y in range(c, c + k)])
-                    c += k
-                    continue
-                px = "pX%d" % (nx[0] % 4)
-                nx[0] += 1
-                mm(256 * k, T[px][:, 0:256 * k], T.IN[:], T.Wx[:, 256 * c:256 * (c + k)], True, False, ("IN", N("Wx")), px)
-                for e, m in calls:
-                    raw, src = T.raw[:, 256 * (c + x):256 * (c + x + m)], T.featW[:].indirect(T.inC[:, o + a + 16 * x:o + a + 16 * (x + m)])
-                    if e == "v":
-                        cp(ga(256 * m), raw, src, ("feat", "feat0", ic), ("raw%d" % (c + x),))
+            for u, (e, k) in enumerate(CH[h]):
+                a, raw, rn, an = o + 16 * (c - c0), T.raw[:, 256 * c:256 * (c + k)], ["raw%d" % y for y in range(c, c + k)], ["A%d" % y for y in range(c, c + k)]
+                src = T.featW[:].indirect(T.inC[:, a:a + 16 * k])
+                if e == "f":
+                    tt(ga(256 * k), raw, src, T.Wx[:, 256 * c:256 * (c + k)], ALU.subtract, ["feat", "feat0", ic] + wx(0, 16), rn)
+                    act(cy(256 * k), T.A[:, 16 * c:16 * (c + k), 0:16], raw, AF.Abs, rn, an)
+                else:
+                    px = "pX%d" % ([(x, y) for x in range(NP) for y, z in enumerate(CH[x]) if z[0] != "f"].index((h, CH[h].index((e, k), u))) % 3)
+                    for y in range(16):
+                        mm(16 * k, T[px][:, y:256 * k:16], T.IN[:], Wk(0, 16 * c, 16 * k), y == 0, False, ["IN"] + wx(0, 1), px, nm="sub%d" % c)
+                    if e == "p":
+                        cp(ga(256 * k), raw, src, ("feat", "feat0", ic), rn)
                     else:
-                        act(ga(256 * m), raw, src, AF.Copy, ("feat", "feat0", ic), ("raw%d" % (c + x),))
-                    mm(256 * m, T[px][:, 256 * x:256 * (x + m)], T.IB[:], raw, False, x + m == k, ("IB", "raw%d" % (c + x)), px)
-                    x += m
-                act(cy(256 * k), T.A[:, c:c + k, :], T[px][:, 0:256 * k], AF.Abs, (px,), ["A%d" % y for y in range(c, c + k)])
+                        act(ga(256 * k), raw, src, AF.Copy, ("feat", "feat0", ic), rn)
+                    mm(256 * k, T[px][:, 0:256 * k], T.IB[:], raw, False, True, ["IB"] + rn, px, nm="add%d" % c)
+                    act(cy(256 * k), T.A[:, 16 * c:16 * (c + k), 0:16], T[px][:, 0:256 * k], AF.Abs, (px,), an)
                 c += k
             if t == h == 0:
-                keys()
+                keys(1)
             ts(cy(nl / 2), T.G[:, pr, :], T.inC[:, o:o + nl], 2048.0, None, ALU.subtract, None, (ic,), (N("G"),))
             tr(cy(nl / 2), T.GT[:, pr, :], T.G[:, pr, :], (N("G"),), (N("GT"),))
 
             def turned(ps, PM, nm, XT, nxt_, stop):
                 for e in range(2):
                     for s in range(2):
-                        mm(8 * NC, T[ps][:, pr if ps == "pS" else slice(0, hc), 16 * e:16 * e + 16], PM[:, 256 * e + 128 * s:256 * e + 128 * s + 128], XT[:, pr, 16 * s:16 * s + 16], False, stop and e + s == 2, (nm, nxt_), ps)
-            for ps in (pv, "pL"):
-                mm(nl, T[ps][:, 0:hc, :], T.ob[0:33, :], T.Kc[0:33, 0:nl], True, False, ("ob", "Kc"), ps)
-                turned(ps, T.PM, "PM", T.GT, N("GT"), ps == "pL")
-            act(cy(nl), T.Lp[:, ls], T.pL[:, 0:hc, :], AF.Identity, ("pL", "limA"), (N("Lp"),), bias=T.limA[:])
-            for a, e in zip([0] + BATCH, BATCH):
+                        out = T.pS[:, pr, 16 * e:16 * e + 16] if ps == "pS" else T[ps][:, e:NC:2, 0:16]
+                        mm(8 * NC, out, PM[:, 256 * e + 128 * s:256 * e + 128 * s + 128], XT[:, pr, 16 * s:16 * s + 16], False, stop and e + s == 2, (nm, nxt_), ps, nm=N("t" + ps[1]))
+            mm(17 * NC, T.pL[:, 0:NC, :], T.ob[0:33, 0:128], T.Kc[0:33, 0:NC, :], True, False, ("ob", "Kc"), "pL", nm=N("kL"))
+            turned("pL", T.PM, "PM", T.GT, N("GT"), True)
+            l17, back = slice(17 * c0, 17 * c1), lambda a, e: slice(17 * e - 1, 17 * a - 1 if a else None, -1)
+            if LPQ[h] == "v":
+                ts(cy(17 * NC), T.Lp[:, l17], T.pL[:, 0:NC, :], T.limA[:], None, ALU.add, None, ("pL", "limA"), (N("Lp"),))
+            else:
+                act(cy(17 * NC), T.Lp[:, l17], T.pL[:, 0:NC, :], AF.Identity, ("pL", "limA"), (N("Lp"),), bias=T.limA[:])
+            mm(17 * NC, T[pv][:, 0:17 * NC], T.IN[:], T.limT[:, 0:17 * NC], True, False, ("IN", "limT"), pv, nm=N("kv"))
+            for a, e in BATCH[h]:
+                if (a, e) == BATCH[h][TV[h]]:
+                    mm(68 * NC, T[pv][:, 0:17 * NC], T.If[:], T.Lp[:, l17], False, False, ("If", N("Lp")), pv, nm=N("tv"))
                 for b in range(16):
-                    mm(16 * (e - a), T[pv][:, a // 2:e // 2, :], T.LH[:, 15 - b:143 - b], T.A[:, c0 + a:c0 + e, 16 * b:16 * b + 16], False, b == 15 and e == NC,
-                       ["LH"] + ["A%d" % y for y in range(c0 + a, c0 + e)], pv)
-            tt(cy(nl), T.vm[:, ls], T[pv][:, 0:hc, :], T.Lp[:, ls], ALU.max, (pv, N("Lp")), (N("vm"),))
-            scan(cy(nl), T.vI[:, ls], T.RST[:, 0:nl], T.vm[:, ls], ALU.max, ALU.min, ("RST", N("vm")), (N("vI"),))
-            ts(S, T.yy[:, lb], last16(T.vI), 8191, None, ALU.bitwise_and, None, (N("vI"),), (N("yy"),))
+                    mm(17 * (e - a), T[pv][:, 17 * a:17 * e], T.LH[:, 15 - b:143 - b], T.A[:, 16 * (c0 + a) + b:16 * (c0 + e):16, :], False, b == 15 and (a, e) == BATCH[h][-1],
+                       ["LH"] + ["A%d" % y for y in range(c0 + a, c0 + e)], pv, nm="sum%d" % (c0 + a))
+            scan(cy(17 * NC), T.vI[:, back(c0, c1)], T[pv][:, back(0, NC)], T.Lp[:, back(c0, c1)], ALU.min, ALU.max, (pv, N("Lp")), (N("vI"),))
+            ts(S, T.yy[:, lb], T.vI[:, 17 * c0:17 * c1:17], 4095, None, ALU.bitwise_and, None, (N("vI"),), (N("yy"),))
             ou, oo = T.outC[:, ob:ob + NC], "outO%d_%d" % (t, h)
-            ts(S, ou, T.yy[:, lb], 4096.0, None, ALU.subtract, None, (N("yy"),), (oo,))
-            if KGQ == "v":
+            cp(S, ou, T.yy[:, lb], (N("yy"),), (oo,))
+            if KGQ[h] == "v":
                 cp(ga(nl), T.KG[:, ls], T.keyW[:].indirect(ou), ("keyW", oo), (N("KG"),))
             else:
                 act(ga(nl), T.KG[:, ls], T.keyW[:].indirect(ou), AF.Copy, ("keyW", oo), (N("KG"),))
             if not final:
                 ow = T.outW[:, 256 * t + l0:256 * t + l1]
-                if DWQ == "v":
-                    tt(ga(nl), T.DW[:, ls], T.featW[:].indirect(ou), Wa, ALU.subtract, ("feat", "feat0", oo, iw), (N("DW"),))
-                    act(cy(nl), ow, T.DW[:, ls], AF.Abs, (N("DW"),), ("outW%d_%d" % (t, h),))
-                else:
-                    act(ga(nl), T.DW[:, ls], T.featW[:].indirect(ou), AF.Copy, ("feat", "feat0", oo), (N("DW"),))
-                    mm(nl, T[pv][:, 0:hc, :], T.IN[:], Wa, True, False, ("IN", iw), pv)
-                    mm(nl, T[pv][:, 0:hc, :], T.IB[:], T.DW[:, ls], False, True, ("IB", N("DW")), pv)
-                    act(cy(nl), ow, T[pv][:, 0:hc, :], AF.Abs, (pv,), ("outW%d_%d" % (t, h),))
-                send(T.inW[:, 256 * (t + 1) + l0:256 * (t + 1) + l1], ow, "w%d_%d" % (t + 1, h), ("outW%d_%d" % (t, h),), ("inW%d_%d" % (t + 1, h),), hlp, FLYW)
+                tt(ga(nl), ow, T.featW[:].indirect(ou), Wk(0, l0, nl), ALU.subtract, ["feat", "feat0", oo] + wx(0, 1), ("outW%d_%d" % (t, h),))
+                send(T.inW[:, 256 * (t + 1) + l0:256 * (t + 1) + l1], ow, "w%d_%d" % (t + 1, h), ("outW%d_%d" % (t, h),), ("inW%d_%d" % (t + 1, h),), FLYW)
             tr(cy(nl / 2), T.KT[:, pr, :], T.KG[:, ls], (N("KG"),), (N("KT"),))
-            mm(4 * nl, T.pS[:, pr, :], T.INf[:], T.M[:, ls], True, False, ("INf", N("M")), "pS")
+            mm(4 * nl, T.pS[:, pr, :], T.INf[:], T.M[:, pr, :], True, False, ("INf", N("M")), "pS", nm=N("kS"))
             turned("pS", T.PK, "PK", T.KT, N("KT"), True)
             act(cy(nl), T.AB[:, ls], T.pS[:, pr, :], AF.Abs, ("pS",), (N("AB"),))
             scan(cy(nl), T.es[:, ls], T.RN[:, 0:nl], T.AB[:, ls], ALU.max, ALU.min, ("RN", N("AB")), (N("es"),))
-            ev = last16(T.es)
             two = lambda b, e: b[:, 2 * c0 + NC * e:2 * c0 + NC * e + NC]
             both = lambda b: b[:, 2 * c0:2 * c1]
             for e, bit in enumerate((16, 2)):
-                ts(S, two(T.x2, e), ev, 4095 + 4096 * bit + NONE, None, ALU.bitwise_and, None, (N("es"),), (N("x2%d_" % e),))
-            for e in range(2):
-                tt(S, two(T.l2, e), two(T.x2, e), T.yc[:] if STG else T.yy[:, lb], ALU.min, (N("x2%d_" % e), "yc" if STG else N("yy")), p=(N("l2"),))
-            if STG:
-                act(ga(nl), T.kid[:, W + 16:W + 16 + nl], T.kid[:, 0:W].indirect(ou), AF.Copy, ("kid", oo), ("stg",))
-                cp(S, both(T.u2), both(T.l2), (N("l2"),), (N("u2"),))
-            else:
-                ts(S, both(T.l3), both(T.l2), 4095, None, ALU.bitwise_and, None, (N("l2"),), (N("l3"),))
-                cp(S, both(T.u2), both(T.l3), (N("l3"),), (N("u2"),))
-            win = T.kid[:] if STG else T.kid[:, 0:W]
-            if TOPQ == "v":
-                ts(ga(nl), T.top[:, ls], win.indirect(two(T.u2, 0)), C(SCT), C(BIT), ALU.mult, ALU.add, ("kid", "stg", N("u2"), "sct", "bit"), (N("top"),))
-            else:
-                act(ga(nl), T.top[:, ls], win.indirect(two(T.u2, 0)), AF.Identity, ("kid", "stg", N("u2"), "sct", "bit"), (N("top"),), bias=C(BIT), scale=C(SCT))
-            tt(ga(nl), T.cf[:, ls], win.indirect(two(T.u2, 1)), T.top[:, ls], ALU.max, ("kid", "stg", N("u2"), N("top")), (N("cf"),))
-            oc = "outC%d_%d" % (t, h)
-            if final:
-                ts(cy(nl), T.outF[:, ls], T.cf[:, ls], C(OFF), None, ALU.subtract, None, (N("cf"), "off"), (oc,))
-                send(T.inF[:, ls], T.outF[:, ls], "c%d_%d" % (t + 1, h), (oc,), (N("inF"),))
-                dma("y", T.yn[:, ls], T.inF[:, ls], N("yn"), 512 * nl, r=(N("inF"),))
-            else:
-                ts(cy(nl), T.outC[:, o:o + nl], T.cf[:, ls], C(OFF), None, ALU.subtract, None, (N("cf"), "off"), (oc,))
+                ts(S, two(T.x2, e), T.es[:, l0 + 15:l1:16], 4095 + 4096 * bit + NONE, None, ALU.bitwise_and, None, (N("es"),), p=(N("x2"),))
+            tt(S, both(T.l2), both(T.x2), both(T.yc), ALU.min, (N("x2"), "yc"), (N("l2"),))
+            stg, win, wn = T.kid[:, D + own(h, c0):D + own(h, c1)], T.kid[:, D:D + own(h, c1)], ["kid"] + tag_all("stg")[:h + 1]
+            act(ga(nl), stg, T.kid[:, D:D + W].indirect(ou), AF.Copy, ("kid", oo), (N("stg"),))
+            cp(S, both(T.u2), both(T.l2), (N("l2"),), (N("u2"),))
+            oc, od = "outC%d_%d" % (t, h), "outD%d_%d" % (t, h)
+            if True:
+                for e, (out, nm) in enumerate(((T.outC[:, o:o + nl], oc), (T.outD[:, t, o % CT:o % CT + nl], od))):
+                    ts(ga(nl), out, win.indirect(two(T.u2, e)), C(SCT + e), None, ALU.mult, None, wn + [N("u2"), "sct"], (nm,))
                 a = min(o, ob)
-                send(T.inC[:, a + 2 * CS:a + 3 * CS], T.outC[:, a:a + CS], "c%d_%d" % (t + 1, h), (oc, oo), ("inC%d_%d" % (t + 1, h),))
-            if t not in JM:
-                mounts(t, c0, c1, [h])
+                send(T.inC[:, a + CT:a + CT + CT // 2], [T.outC[:, a:a + CT // 2], T.outD[:, t, a % CT:a % CT + CT // 2]], "c%d_%d" % (t + 1, h), (oc, od, oo, "nought"), ("inC%d_%d" % (t + 1, h),))
+            for e, nm in enumerate(("top", "cf")):
+                act(ga(nl), T[nm][:, ls], win.indirect(two(T.u2, e)), AF.Copy, wn + [N("u2"), "sct"], (N(nm),), scale=C(SCT + e))
+            if final:
+                cp(cy(nl), T.inF[:, ls], T.inC[:, o + CT:o + CT + nl], ("inC%d_%d" % (t + 1, h),), (N("yf"),))
+                dma("y", T.yn[:, ls], T.inF[:, ls], N("yn"), 512 * nl, r=(N("yf"),))
             lag[0] = LAGW * h
-            if t not in JW:
-                writers(c0, c1, [h])
+            if not JW:
+                writers(c0, c1, [h], "pT")
         lag[0] = LAGJ
-        if t in JM:
-            mounts(t, 0, 16, range(NP))
-        if t in JW:
-            writers(0, 16, range(NP))
+        if JW:
+            writers(0, 16, range(NP), "pT")
+        mounts(t)
         lag[0] = 0.0
         if not final:
-            act(S, T.cov[:], T.ncd[:], AF.Sign, ["ncd%d" % h for h in range(NP)], ("cov", "cs"), scale=-1.0, accum_out=T.cs[:])
-            mm(256, T.pL[:, 0, 0:1], T.ones[:], T.cs[:], True, True, ("ones", "cs"), "pL")
+            act(S, T.cov[:], T.ncd[:], AF.Sign, tag_all("ncd"), ("cov", "cs"), accum_out=T.cs[:])
+            mm(256, T.pL[:, 0, 0:1], T.half[:], T.cs[:], True, True, ("half", "cs"), "pL", nm="cnt")
             cp(S, T.csi[:], T.pL[:, 0, 0:1], ("pL",), ("csi",))
             ts(S, T.csa[:], T.csi[:], 15, None, ALU.bitwise_and, None, ("csi",), ("csa",))
             ts(S, T.limA[:], T.csa[:], RS, RS * (LIM - 1), ALU.mult, ALU.add, ("csa",), ("limA",))
+            ts(cy(68), T.limT[:], T.ob[:], T.limA[:], None, ALU.mult, None, ("ob", "limA"), ("limT",))
         for h, (c0, c1) in enumerate(PARTS):
-            for c in range(c1 - 1, c0 - 1, -1):
-                a = at(t, c)
-                src = T.outF[:, 16 * c:16 * c + 16] if final else T.outC[:, a:a + 16]
-                kid = "end" if final and ENDQ else "kid"
-                cp((60 + 16 * SCAT) * CY, T[kid][:, 0:W + 16].indirect(T.s2u[:, 2 * c:2 * c + 1]), src, ("s2u%d" % h, "outC%d_%d" % (t, h)), (kid,))
-        if t == STEPS - 2:
-            for x, e in enumerate(ENDQ):
-                copy(e, 256, T.end[:, 256 * x:256 * x + 256], T.kid[:, 256 * x:256 * x + 256], ("kid",), p=("end",))
-    for h, (c0, c1) in enumerate(PARTS):
-        N = lambda s: s + "%d" % h
-        ls, nl = slice(16 * c0, 16 * c1), 16 * NC
-        ts(cy(nl), T.mi[:, ls], T.M[:, ls], 1.0 / KS, 0.25, ALU.mult, ALU.add, (N("M"),), (N("mi"),))
-        ts(cy(nl), T.mn[:, ls], T.M[:, ls], -1.0, None, ALU.mult, None, (N("M"),), (N("mn"),))
-        ts(cy(nl), T.mj[:, ls], T.mn[:, ls], 4095, None, ALU.bitwise_and, None, (N("mn"),), (N("mj"),))
-        for src, ns, X, XT, nm, sub, ms in ((T.mj, "mj", T.X, T.XT, "X", 2048.0, (M0, M1)), (T.mi, "mi", T.Y, T.YT, "Y", 0.0, (K0, K1))):
-            for e, m in enumerate(ms):
-                ts(cy(nl), X[:, c0:c1, 16 * e:16 * e + 16], src[:, ls], sub, C(m), ALU.subtract, ALU.mult, (N(ns), "m0", "m1", "k0", "k1", nm + "T"), (N(nm + "%d_" % e),))
-            tr(cy(nl), XT[:, c0:c1, :], X[:, c0:c1, :], (N(nm + "0_"), N(nm + "1_")), (N(nm + "T"),))
+            for c in range(c1 - 2, c0 - 2, -2):
+                ns, off, r = (60 + 32 * SCAT) * CY, T.s2u[:, c:c + 2], ["s2u%d" % h, "top%d" % h, "cf%d" % h]
+                tt(ns, T.kid[:, 0:D + W].indirect(off), T.top[:, 16 * c:16 * c + 32], T.cf[:, 16 * c:16 * c + 32], ALU.add, r, ("kid",))
+    lag[1] = STEPS
+    act(cy(256), T.mk16[:], T.M[:], AF.Copy, tag_all("M"), ("mk16",), scale=1.0 / KS, bias=192.0)
+    ts(cy(128), T.klb[:], T.mk16[:], 192.0, None, ALU.subtract, None, ("mk16",), ("klb",))
+    ts(cy(128), T.Y[:], T.mk16[:], 192.0, 1.0 / 64, ALU.subtract, ALU.mult, ("mk16",), ("Y",))
+    mm(1024, T.pS[:, 0:8, :], T.INf[:], T.CJ2[:], True, False, ("INf", "CJ2"), "pS", nm="code")
+    for x, (k, PM, src, r) in enumerate(((512, T.PF, T.M, ["PF"] + tag_all("M")), (128, T.PK, T.klb, ["PK", "klb"]), (128, T.PM, T.Y, ["PM", "Y"]))):
+        for e in range(2):
+            for s in range(2):
+                out = T.pS[:, 8 * (x // 2):8 * (x // 2) + 8, 16 * s:16 * s + 16]
+                mm(k, out, PM[:, 256 * s + 128 * e:256 * s + 128 * e + 128], src[:, :, 16 * e:16 * e + 16], False, x == 2 and e + s == 2, r, "pS", nm="turn%d" % x)
+    for e in range(2):
+        cp(cy(256), T.X[:, 8 * e:8 * e + 8, :], T.pS[:, 8 * e:8 * e + 8, :], ("pS",), ("X%d" % e,))
+        tr(cy(128), T.XT[:, 8 * e:8 * e + 8, :], T.X[:, 8 * e:8 * e + 8, :], ("X%d" % e,), ("XT%d" % e,))
     for b in range(16):
-        sh = T.SH[:, 128 * (-b % 16):128 * (-b % 16) + 128]
-        for e, (XT, nm) in enumerate(((T.XT, "XT"), (T.XT, "XT"), (T.YT, "YT"), (T.YT, "YT"))):
-            mm(16, T.pX0[:, b:256:16], sh, XT[:, :, 16 * (e % 2) + b], e == 0, e == 3, ["SH"] + tag_all(nm), "pX0", part=True)
-    act(cy(256), T.ymo[:], T.pX0[:, 0:256], AF.Copy, ("pX0",), ("ymo",), scale=64.0, bias=131072.0)
+        for e in range(2):
+            mm(16, T.pS[:, 0:8, b::16], T.SH[:, 128 * (-b % 16):128 * (-b % 16) + 128], T.XT[:, 8 * e:8 * e + 8, b::16], e == 0, e == 1, ("SH", "XT0", "XT1"), "pS", part=True, nm="back")
+    act(cy(256), T.ymo[:], T.pS[:, 0:8, :], AF.Copy, ("pS",), ("ymo",), scale=64.0, bias=131072.0)
     dma("s", T.ymu[:], T.ymo[:], "ymu", 131072, r=("ymo",))
-    yb = ["pX1", "pX2", "pX3", "pL"]
-    kid = "end" if ENDQ else "kid"
-    col = lambda i, x: T[kid][:, 512 * i + 256 * x:512 * i + 256 * x + 256]
-    acc = lambda x: T.acc[:, 256 * x:256 * x + 256]
-    for x in range(2):
-        for i in range(8 - YP, 8):
-            mm(1024, T["pv%d" % x][:, 0:8, :], T["F%d" % (i + 1)][:], col(i, x), i == 8 - YP, i == 7, ("F", kid), "pv%d" % x)
-    for i in range(1, 8 - YP):
-        for x in range(2):
-            ps = yb[nx[0] % 4]
-            nx[0] += 1
-            out = T[ps][:, 0:256] if ps[1] == "X" else T[ps][:, 0:8, :]
-            act(cy(256), out, col(i, x), AF.Copy, (kid,), (ps,), scale=float(i + 1))
-            tt(cy(256), acc(x), col(0, x) if i == 1 else acc(x), out, ALU.add, (kid if i == 1 else "acc%d" % x, ps), ("acc%d" % x,))
-    for x in range(2):
-        tt(cy(256), acc(x), acc(x), T["pv%d" % x][:, 0:8, :], ALU.add, ("acc%d" % x, "pv%d" % x), ("acc%d" % x,))
-        dma("ys"[x], T.yd[:, 256 * x:256 * x + 256], acc(x), "yd%d" % x, 131072, r=("acc%d" % x,))
+    yb, n = ["pX0", "pX1", "pL", "pv0", "pv1", "pX2"], 0
+    col = lambda i, x: T.kid[:, D + 512 * i + YQ[x]:D + 512 * i + YQ[x + 1]]
+    acc = lambda x: T.acc[:, YQ[x]:YQ[x + 1]]
+    for two in range(0, len(YQ) - 1, 2):
+        for x in (two, two + 1):
+            k = YQ[x + 1] - YQ[x]
+            for i in range(8 - YP[x], 8):
+                mm(4 * k, bank(yb[x % 2], k), T.FF[:, 128 * (7 - i):128 * (8 - i)], col(i, x), i == 8 - YP[x], i == 7, ("F", "kid"), yb[x % 2], nm="yd%d" % x)
+        for i in range(1, 9):
+            for x in [x for x in (two + 1, two) if i <= 8 - YP[x]]:
+                k, ps = YQ[x + 1] - YQ[x], yb[2 + n % 4] if i < 8 - YP[x] else yb[x % 2]
+                if i < 8 - YP[x]:
+                    n += 1
+                    act(cy(k), bank(ps, k), col(i, x), AF.Copy, ("kid",), (ps,), scale=float(i + 1))
+                tt(cy(k), acc(x), col(0, x) if i == 1 else acc(x), bank(ps, k), ALU.add, ("kid" if i == 1 else "acc%d" % x, ps), ("acc%d" % x,))
+        for x in (two, two + 1):
+            dma("ys"[x % 2], T.yd[:, YQ[x]:YQ[x + 1]], acc(x), "yd%d" % x, 512 * (YQ[x + 1] - YQ[x]), r=("acc%d" % x,))
     emit(g, T, ops, order(ops))

from concourse.bass import DstId, RemoteDMATransfer
from concourse.mybir import AluOpType as ALU, ActivationFunctionType as AF

STEPS, W, L, LIM = 8, 4096, 256, 60
PARTS = [(8, 16), (0, 8)]
SHQ, KIDQ, KEYQ, KGQ, LPQ, TOPQ = "sg" * 8, "ggggggvv", "svsvsvsv", "ss", "ss", "s"
WXQ, WX0 = ["s" * 11 + "g" * 5, "s" * 10 + "g" * 6], ["vvvvvvvvssssssss", "ssssvvgggggggggg"]
CH = [[("f", 2), ("f", 2), ("f", 2), ("s", 2)], [("f", 2), ("f", 2), ("f", 1), ("f", 1), ("s", 2)]]
BATCH, TV = [[(0, 4), (4, 8)]] * 2, [0, 0]
JW = False
BIG, NONE, RS, KS, RC, DB = float(2 ** 26), 2 ** 17, float(2 ** 17), float(2 ** 18), 120, 8192.0
KB, MB = ["pX2", "pX1", "pv0", "pX2", "pX2", "pX1", "pS", "pX2"], "pv1"
LAG, LAGJ, LAGW = 1.0, 0.0, 0.0
PERIOD, END = 12327.0, 8000.0
ROUND = {
    "v": """G0@25 raw10@621 GT0@990 raw8@2554 raw12@2927 G1@3633 GT1@3923 raw2@3923 ncd0@3994 outO0@4040 raw0@4216 vI0@4346 raw4@4936 yy0@4937 xo0@5306 raw5@5586 KT0@5910 outW0@6102 vI1@7001 es0@7053 xx0@7101 cf0@7383 x20'@7420 x20@7496 outO1@7748 x21'@7978 xo1@8016 yy1@8021 na@8130 l20@8179 cf1@8216 x21@8228 KT1@8264 u20@8482 s2u0'@9200 outW1@9202 dn@9234 kid'@9280 pn'@9304 ncd1@9876 l21@10088 es1@10171 outC0@10171 u21@10270 csi@10291 xx1@10424 pn@10493 s2u0@10577 kid@10610 outC1@11026 csa@11400 dm@11424 M0@11492 wr0@11498 kid''@13264 limT@13444 wr1@13641 limA@14090 s2u1@14882 s2u1'@14974 kid'''@15306 kid''''@17653 kid'''''@18001 kid'''''''@18721 kid''''''@20156""",
    "s": """A8@-1810 Wx0@-248 A14@1132 A10@1166 raw14@1339 A12@2237 Wx1@2311 Lp0@2330 AB0@2370 KG0@2727 A0@3294 A6@3574 raw6@3639 A2@3656 Lp1@4015 A4@6022 A5@6022 stg0@7188 top0@7440 KG1@8414 stg1@9140 cov@9176 AB1@10103 wa0@11528 top1@11806 wa1@14258""",
    "g": """Wx0@-1300 Wx1@643 sendw0@5497 sendw1@7869 sendc0@11164 sendc1@11865""",
    "t": """add14@-1186 kL0@703 sub14@758 sub6@1083 kv0@1264 tL1@1584 tL0@1751 sum8@1803 kL1@2118 cw0@2261 tv0@2387 kv1@2503 sum0@2677 sum12@3090 add6@4662 sum4@4706 tv1@5134 kS0@5232 tS0@5864 own0@6309 eqa0@6428 tS1@6505 kS1@7242 cw1@10528 eqb1@10552 eqa1@11317 cnt@11835 own1@11863 eqb0@12101""",
}
NP = len(PARTS)
YP, YQ = [2, 1], [0, 256, 512]
ROUND = {
    "v": """<klb@-9839 <raw8@-7903 <mo16@-7436 <raw10@-6936 <keyW'@-6779 <mi@-6732 <keyW@-5823 <mj@-5278 <raw4@-4982 <raw12@-3881 <XG@-2816 raw10@-1648 G0@-861 <vI0@747 GT0@2460 G1@2466 <outW0@2831 raw12@3244 raw8@3244 raw0@3299 <raw2@3497 GT1@3497 raw2@3558 <outO0@3590 vI0@3853 <KT0@3855 <raw0@3897 yy0@3917 <yy0@4070 <raw5@4290 pn@4341 <vI1@4571 raw4@4620 outO0@4885 x20'@5019 vI1@5020 KT0@5221 raw5@5236 xo0@5269 x20@5458 outW0@5515 <kid'@5912 u20@5946 xx0@5949 <es0@6051 es0@6070 outO1@6233 xx0'@6427 yy1@7272 es1@7519 l20@7823 outW1@7879 outC0@8037 wr0@8114 u21@8170 ncd0@8305 cf0@8573 l21@8746 csa@8993 ncd1@9087 x21'@9087 x21@9144 KT1@9211 >kid''''@9235 dm@9325 xx1'@9369 na@9452 xo1@9481 dn@9515 s2u0@9613 >kid@10087 >kid'''''@10131 cf1@10238 >kid'''''''@10460 xx1@10662 >kid'@11079 kid@11548 outC1@11548 csi@11614 <kid@11687 kid'@11767 M0@11890 >YT@11992 wr1@11992 >X@12131 >X'@12143 >kid'''@12377 >wr1@12409 kid''@12636 >XT@13241 >kid''@13609 limA@13638 >s2u1@13673 >kid''''''@14541 s2u1@16290 kid'''@16853 kid''''@17825 kid'''''@17843 kid'''''''@18358 kid''''''@19050""",
    "s": """<mk16@-8412 <XF@-5087 <XF'@-4445 <keyW'@-4322 <keyW@-3930 <raw14@-2754 Wx1@-228 KG0@-111 Wx0@563 <A10@642 A6@677 Lp1@890 <M0@948 A12@992 A2@1116 A8@1329 A0@1593 <A14@1657 Lp0@1700 raw14@1779 <A12@1914 A14@2092 <A8@2411 A10@2426 <raw6@3251 raw6@3274 <A6@3745 <KG0@3774 A5@4327 A4@5221 <AB0@5339 <A0@5593 AB0@5988 <A2@6028 stg0@6477 >klb@6487 KG1@6951 <A4@6967 AB1@7669 stg1@7910 top0@7910 <A5@8024 >Y@9088 >mk16@9339 top1@9613 cov@9796 wa0@9884 wa1@10597 >wa1@12354 limT@12568 >Y'@12681""",
    "g": """Wx0@-2056 Wx1@709 sendw0@4223 sendw1@7378 sendc0@8837 sendc1@11636""",
    "t": """<ksum0@-8605 <rot@-8397 <join@-4933 <ksum1@-3625 <rows0@-3337 <rows1@-3335 <code@-2559 sub6@-1873 sub14@-1836 <rows2@-1410 <rows3@-1410 <add14@-32 cw0@145 kv0@268 kL0@473 <rows4@1087 add14@1221 kL1@1521 tv0@1870 kv1@1884 tL0@2324 <kS0@2454 tv1@2454 sum12@2622 <sub6@2722 <rows5@2745 <add6@2762 <sum12@2820 <rows7@3010 <sum8@3197 sum8@3198 <rows6@3360 tL1@3601 kS0@4025 add6@4224 sum4@5644 >pX2'@5783 sum0@5855 >eq1@6019 kS1@6359 tS0@6400 eq0@7202 >pX2@8004 >pX2''@8411 tS1@8672 eq1@9426 cnt@9623 cw1@9634 >back@16219""",
}
PERIOD, WXQ, KIDQ, KEYQ = 12153.0, ["ssssssssssvvgggg", "ssssssssvvgggggg"], "gggggggv", "svsvssss"
ROUND = {
    "v": """-mo16@-11333 -mi@-7653 -klb@-7476 -mj@-5630 -keyW@-3364 -XG@-2323 Wx0c@-1817 <Wx1c@-1573 <Wx1b@-1102 <GT1@-423 <mi@-217 Wx1c@-80 <raw10@-13 <Wx1a@67 G0@210 <mj@255 raw10@264 <raw8@470 GT0@994 raw8@1048 -keyW'@1621 raw12@1778 <vI0@1940 <klb@2094 <raw0@2111 <outO0@2409 <raw12@2415 G1@2500 raw0@2560 GT1@3290 raw2@3340 <raw2@3390 <raw5@3559 vI0@4231 raw4@4347 yy0@4737 <raw4@4822 <outW0@4885 outO0@5001 raw5@5056 <yy0@5243 xo0'@5446 outW0@5501 KT0@5735 xo0@5789 <es0@5868 pn@5998 <KT0@6508 es0@6727 vI1@6968 x20@7083 -kid'@7124 x20'@7138 ncd0@7192 yy1@7293 l20@7402 xx0@7457 outO1@7558 u20@7667 xx0'@7721 outW1@7822 na@8043 xo1@8097 <vI1@8122 outC0@8152 KT1@8372 outD0@8427 xo1'@8648 >kid''@8721 +YT@8723 >xx1@9220 >xx1'@9220 +X@9295 es1@9304 +X'@9376 >kid'''@9397 dn@9413 >wr1@9458 wr0@9467 >outC0@9610 x21'@9644 ncd1@9698 x21@9753 dm@9807 s2u0'@9861 s2u0@9916 l21@10017 xx1@10071 xx1'@10126 >kid@10178 M0@10180 u21@10281 >outC1@10398 outD1@10546 >ncd1@10604 csi@10767 outC1@10821 csa@11042 kid@11252 limA@11406 wr1@11575 >s2u1@11721 >s2u1'@11721 kid'@11751 +XT@11789 limT@11906 s2u1'@11964 s2u1@12018 kid''@12181 >kid'@12533 >kid''''''@12820 >kid'''''''@13132 >kid''''@13392 >kid'''''@14377 kid'''@16230 kid''''@16945 kid'''''@17997 kid''''''@18362 kid'''''''@18726""",
    "s": """-mk16@-7593 -keyW'@-5946 <Lp1@-3635 Wx0a@-3011 Wx0b@-2657 Wx0c@-2331 <Wx1d@-2271 -XF@-2186 -keyW@-1954 <Lp0@-759 Wx1a@-690 Wx1b@-336 -XF'@-149 raw14@210 <Wx1c@1089 A10@1204 <keyW'@1481 A14@1639 <A14@1827 <A8@1885 <raw14@1897 Lp0@2074 A8@2190 A12@2718 <A12@2796 raw6@3153 <keyW''@3310 <A6@3484 <A10@3667 A0@3883 <keyW@3979 <A5@3994 A2@4318 <A0@4725 Lp1@4754 <KG0@4818 A6@4869 KG0@5304 <keyW'''@5500 A4@5525 <raw6@5629 -M0@5687 A5@5743 <A2@5940 <A4@6029 AB0@6348 <AB0@6381 stg0@6937 KG1@7822 top0@8043 cf0@8264 stg1@8484 wa0@8783 AB1@8985 cov@9985 +mk16@10218 >wa1@10430 cf1@10546 +klb@10555 top1@10767 wa1@11188 +Y@11887 +Y'@12163""",
    "g": """Wx0h@-2447 Wx0g@-1761 Wx1f@-126 Wx1g@560 Wx1h@1246 sendw0@5931 sendw1@8253 sendc0@8858 sendc1@11252""",
    "t": """+pX2@-24374 -ksum0@-8853 kL0@-1121 sub14@-1048 kS0@-495 -rot@-8 kv0@20 <kS0@26 <tL0@56 kv1@94 cw0@167 -rows3@178 <ksum1@290 -rows1@579 -rows2@579 <sub14@579 -rows0@616 add14@1149 <add14@1365 tL0@1426 sub6@1564 <kL1@1670 <tv0@1671 -code@1739 kL1@2400 tv0@2473 sum8@2835 <sub6@2888 sum12@3423 <rows4@4057 add6@4093 <rows5@4110 <rows6@4148 tL1@4370 tv1@5079 sum0@5373 <rows7@5753 <sum8@5753 -join@5766 tS0@5999 <tL1@6008 sum4@6170 <sum12@6565 <add6@6755 kS1@6758 own0@7034 eq0@7985 tS1@8637 cw1@9170 own1@9282 +pX2'@9577 cnt@10249 eq1@10390 >own1@11203 +pX2''@11609 >eq1@13289 +back@15657""",
}
PERIOD = 12068.0
ROUND = {
    "v": """s2u1@12196 G0@210 raw10@264 GT0@994 Wx1c@1048 raw8@1157 raw12@1887 raw0@2780 G1@2723 raw2@3567 GT1@3510 kid''@16361 vI0@4446 s2u1'@12250 kid'''@16725 yy0@4811 raw4@4865 outO0@5255 raw5@5310 kid''''@17769 KT0@5951 outW0@6005 kid'''''@18294 kid''''''@18659 xo0'@6744 xo0@6799 pn@6853 es0@6908 kid'''''''@19085 vI1@7183 ncd0@7299 x20@7353 x20'@7408 yy1@7509 xx0'@7563 xx0@7618 l20@7672 outO1@7773 na@7828 u20@7936 outW1@8038 outC0@8258 KT1@8479 outD0@8533 xo1'@8754 xo1@8809 wr0@9087 es1@9411 dn@9519 ncd1@9729 x21@9784 x21'@9838 xx1@9994 xx1'@10048 l21@10103 dm@10157 Wx0c@-1857 u21@10367 s2u0@10421 s2u0'@10476 csi@10833 outC1@10887 outD1@11108 M0@11328 csa@11383 kid@11538 limA@11693 wr1@11807 limT@11984 kid'@12042
        -mo16@-13488 -mi@-12207 -mj@-6926 <Wx1c@-1789 -klb@-1354 <mj@-666 <mi@-151 <raw10@677 -XG@678 <outO0@793 <vI0@1152 <Wx1a@1265 -keyW'@1843 -keyW@1907 <klb@1973 <Wx1b@2102 <raw8@2119 <raw0@2432 <raw12@3456 <raw2@3667 <es0@4045 <yy0@4501 <outW0@4588 <raw5@5022 <GT1@5869 -kid'@6372 <raw4@6522 <KT0@6615 <vI1@7960 >xx1'@9684 >outC1@10092 >s2u1@10200 >s2u1'@10265 >xx1@10430 >kid'''@10687 >wr1@10687 >kid''@10740 >kid@10813 >outC0@11009 >ncd1@11696 +X'@12127 +YT@12269 +X@12338 >kid'''''''@12445 >kid''''@12879 +XT@13129 >kid'@13225 >kid''''''@13474 >kid'''''@14840""",
    "s": """raw14@210 Wx1b@939 A10@1266 A14@1701 Lp0@2136 A8@2252 A12@2827 raw6@3262 A0@3992 A2@4447 Lp1@4883 A6@4998 KG0@5520 A4@5741 A5@5958 AB0@6563 stg0@7381 KG1@8038 cf0@8258 top0@8479 wa0@8700 AB1@9092 Wx0a@-2422 stg1@9999 cov@10220 Wx0c@-1793 Wx0b@-1630 cf1@10764 top1@10985 wa1@11420 Wx1a@-390
        -mk16@-8055 -keyW'@-4551 <Lp1@-3748 -XF'@-1916 -keyW@-1574 -XF@-1099 <Wx1d@-654 <Lp0@-24 <A12@923 <keyW''@1447 -M0@1448 <Wx1c@1524 <keyW@1582 <A14@2078 <keyW'@2127 <A8@2264 <A10@3175 <raw14@3193 <A6@3916 <KG0@4428 <A0@4467 <A5@5187 <keyW'''@5187 <A2@5323 <A4@5370 <raw6@6797 <AB0@6850 +mk16@7909 >wa1@10099 +klb@10837 +Y'@11330 +Y@12350""",
    "g": """Wx1h@173 Wx1g@860 Wx1f@1546 sendw0@6436 sendw1@8468 sendc0@8964 Wx0h@-1859 Wx0g@-1172 sendc1@11582""",
    "t": """kv0@183 sub14@256 kv1@809 add14@1149 kL0@1426 tL0@1499 sub6@1638 kL1@2462 tv0@2535 sum8@2897 sum12@3485 add6@4202 tL1@4502 tv1@5208 sum0@5502 tS0@6215 sum4@6386 kS1@6973 own0@7250 eq0@7882 tS1@8743 cw1@9087 own1@9199 cnt@10484 eq1@10623 cw0@-261 kS0@-149
        +pX2@-27424 -ksum0@-9742 <kL1@-390 -rows3@93 <ksum1@436 <add14@666 -rot@1099 -rows1@1099 <sub14@1761 -rows2@1816 <tL0@2160 -rows0@2375 -code@3001 <tv0@3003 <rows5@4378 <rows4@4465 -join@4482 <rows6@4704 <sum8@4704 <rows7@5271 <add6@6100 <sum12@6859 <sub6@6893 <kS0@6935 <tL1@6943 +pX2'@9350 +pX2''@10881 >own1@11001 >eq1@13348 +back@15960""",
}
KIDQ = "ggggggvv"
ROUND = {
    "v": """s2u1@12196 G0@210 raw10@264 GT0@994 Wx1c@1048 raw8@1157 raw12@1887 raw0@2723 G1@3453 raw2@3507 GT1@4237 kid''@16361 vI0@4446 s2u1'@16631 kid'''@16725 yy0@4811 raw4@4865 outO0@5255 raw5@5310 kid''''@17769 KT0@5951 outW0@6005 kid'''''@18294 kid''''''@18659 xo0'@6744 xo0@6799 pn@6853 es0@6908 kid'''''''@19085 vI1@7183 ncd0@7299 x20@7353 x20'@7408 yy1@7509 xx0'@7563 xx0@7618 l20@7672 outO1@7773 na@7828 u20@7936 outW1@8038 outC0@8258 KT1@8479 outD0@8533 xo1'@8754 xo1@8809 wr0@9087 es1@9411 dn@9519 ncd1@9729 x21@9784 x21'@9838 xx1@9994 xx1'@10048 l21@10103 dm@10157 Wx0c@-1857 u21@10367 s2u0@10421 s2u0'@10476 csi@10833 outC1@10887 outD1@11108 M0@11328 csa@11383 kid@11538 limA@11693 wr1@11807 limT@11984 kid'@12042
        -mi@-12207 -mo16@-12109 -XG@-2523 -keyW@-1815 <vI0@-1710 <Wx1c@-1465 -mj@-1408 <klb@-1346 <raw8@-1202 -klb@-637 <mi@-380 <outO0@319 <Wx1b@578 -keyW'@918 <Wx1a@1977 <raw10@2228 <mj@2317 <raw0@2515 <raw12@3981 <raw2@4028 <raw4@4064 <raw5@4081 <yy0@4172 <outW0@4297 <es0@5824 -kid''@6095 <GT1@6632 <KT0@6938 -kid'@7469 <vI1@8032 >xx1'@8552 >xx1@8614 >kid@8992 >outC0@9087 >dn@9803 >M0@9862 >dm@9962 >kid'@11231 >outC1@11231 +XT@11371 >ncd1@12030 >kid'''''@12754 >kid''''''@12921 >kid''''@13447 +YT@13620 >kid'''''''@13846 +X@13944 +X'@13979 >kid''@14495 >kid'''@14675 >s2u1'@15067 >s2u1@15101 >wr1@15730""",
    "s": """raw14@210 Wx1b@939 A10@1266 A14@1701 Lp0@2136 A8@2252 A12@2827 raw6@3262 A0@3992 A2@4447 Lp1@4883 A6@4998 KG0@5520 A4@5741 A5@5958 AB0@6563 stg0@7381 KG1@8038 cf0@8258 top0@8479 wa0@8700 AB1@9092 Wx0a@-2422 stg1@9999 cov@10220 Wx0c@-1793 Wx0b@-1630 cf1@10764 top1@10985 wa1@11420 Wx1a@-390
        -mk16@-9283 -keyW'@-4485 <Lp1@-2811 <Wx1d@-2166 -XF@-1508 -keyW@-1444 -XF'@-1380 <A8@1021 <Lp0@1043 <Wx1c@1393 <keyW''@1701 -M0@2092 <raw14@2162 <keyW'@2192 <keyW@2425 <A12@2561 <A0@2632 <A14@3305 <A10@3632 <keyW'''@4682 <A4@5175 <raw6@5231 <A2@5404 <A6@5436 <A5@5477 <KG0@5890 <AB0@7145 >top1@7972 >cf1@8011 +Y'@8985 +Y@9025 >wa1@9044 +mk16@10336 +klb@12417 +ymo@18297""",
    "g": """Wx1h@173 Wx1g@860 Wx1f@1546 sendw0@6436 sendw1@8468 sendc0@8964 Wx0h@-1859 Wx0g@-1172 sendc1@11582
        -kid@-1997 -kid''@-1315 -kid'@-858 <sendw0@969 -kid''''@1454 -kid'''@2393 -kid'''''@3225 <sendw1@4315 <sendc0@5852""",
    "t": """kv0@183 sub14@256 kv1@809 add14@1149 kL0@1426 tL0@1499 sub6@1638 kL1@2462 tv0@2535 sum8@2897 sum12@3485 add6@4202 tL1@4502 tv1@5208 sum0@5502 tS0@6215 sum4@6386 kS1@6973 own0@7250 eq0@7882 tS1@8743 cw1@9087 own1@9199 cnt@10484 eq1@10623 cw0@-261 kS0@-149
        -ksum0@-8676 <add14@-1303 <tv0@-1283 -rows3@667 <kS0@991 <ksum1@1110 -rot@1252 <rows4@3006 <sum8@3145 <rows6@3412 -rows2@3523 <tL0@3524 -code@3532 -rows0@3591 <sub14@3628 -rows1@3682 <rows7@3939 <kL1@4289 <rows5@4328 <tL1@5002 <sum12@5097 -join@5663 <add6@5919 <sub6@6107 +pX2''@9418 >own1@9521 +pX2@9766 >eq1@10818 +pX2'@10980 +back2@11638 +back1@13011 +yd0@13254 +back0@13743 +yd1@13800 +back3@14904""",
}
KB = ["pX2", "pX1", "pv0", "pX2", "pX2", "pX1", "pS", "pX0"]
EDGE = {
    "v": """-mi@-8949 -mo16@-6865 -mj@-6710 -inC1@-3723 <Wx0b@-2929 <GT0@-2899 <GT1@-2293 <mj@-2248 <G0@-2166 <raw10@-1928 -klb@-1839 <raw8@-1728 -inC0@-1591 -keyW@-1518 <Wx0a@-1045 <mi@-510 -keyW'@-421 <raw5@-255 <raw0@-236 <klb@289 <raw12@358 <outO0@1029 <vI0@1065 <yy0@2159 -XG@2290 <G1@2777 <raw2@3109 <Wx1b@3222 <vI1@4127 <KT0@4479 -kid'@4661 <x20'@4766 <es0@4947 <outW0@5396 <x20@5616 <raw4@5671 -kid''@5804 <l20@6003 <u20@6648 <outD0@8106 <outC0@9950
        >outC0@8260 >outD0@8530 >x21'@9151 >x21@9208 >xx1@9220 >xx1'@9279 >dm@9328 >dn@9554 >ncd1@9820 >M0@9850 >u21@9904 >kid@10029 >outD1@10064 >l21@10135 +Y@10244 >outC1@10244 >kid''@11270 >kid'@11323 >s2u1@11472 >s2u1'@11855 >kid'''@12150 >wr1@12340 +klb@12366 >kid''''@12413 >yf0@12500 >kid''''''@12560 +X1@12880 >kid'''''@12880 >kid'''''''@12975 +X0@13246 +XT1@13714 +XT0@13839 >yf1@14710""",
    "s": """-mk16@-6111 <raw14@-4083 -keyW'@-3701 <Wx0d@-3399 -XF@-2000 <Wx1a@-1543 <A8@-1460 <Wx0c@-1393 -keyW@-1367 <A14@-1212 <A10@-452 -XF'@-70 <A12@946 <raw6@1637 <Lp0@1696 <keyW''@1783 <keyW@1800 <keyW'@2058 <A0@2231 <A4@2255 <keyW'''@2401 -M0@3456 <KG0@3730 <Lp1@4380 <AB0@4864 <A5@5484 <A2@5607 <A6@5607 <stg0@6483
        >cf1@9761 +mk16@9981 >top1@10201 >wa1@11070 +ymo@16422""",
    "g": """<Wx1d@-3408 <Wx1e@-1089 <Wx1g@-943 <Wx1h@346 <Wx1f@743 -kid'@2852 -kid@3236 -kid''@6158 <sendc0@7603 <sendw0@7712 <sendw1@7823 -kid'''''@8115 -kid'''@8147 -kid''''@8438""",
    "t": """<sub14@-4503 -ksum0@-4189 -rot@-4040 -rows0@-3996 -rows1@-3996 <ksum1@-3463 <add14@-3432 -rows3@-3181 <tL0@-3180 -rows2@-468 <sum0@-356 <tS0@-143 -code@89 <tv1@305 <kL1@604 <tv0@781 <kS0@809 <add6@888 <rows7@903 <sum8@908 <rows6@940 <rows4@959 <rows5@1339 -join@1387 <sum12@1401 <sub6@2651 <tL1@2848 <sum4@6169
        >eq1@8281 +code@9478 >own1@9801 +turn0@10365 +turn1@10912 +turn2@11700 +yd0@13438 +back@14523 +yd1@15815""",
}
PERIOD, LPQ = 12359.0, "sv"
ROUND = {
    "v": """G0@210 raw10@264 s2u1@13354 GT0@1048 raw8@1103 Wx1c@1833 limT@14301 raw12@1999 G1@2937 raw0@2992 GT1@3722 raw2@3776 raw4@4506 vI0@4896 kid''@17372 Lp1@5166 yy0@5282 s2u1'@17696 kid'''@17750 outO0@5546 raw5@5601 kid''''@18351 pn@6145 KT0@6241 kid'''''@18715 outW0@6510 kid''''''@19090 xo0@6885 xo0'@6939 kid'''''''@19455 es0@7249 vI1@7474 ncd0@7590 x20'@7644 x20@7699 yy1@7800 xx0'@7854 xx0@7909 l20@7963 outO1@8064 na@8119 u20@8227 outW1@8329 outD0@8549 KT1@8770 outC0@8824 xo1'@9045 xo1@9100 wr0@9378 es1@9701 dn@9810 ncd1@10020 x21@10075 x21'@10129 dm@10183 xx1@10285 xx1'@10339 l21@10393 Wx0c@-1645 s2u0'@10823 u21@10877 s2u0@10932 csi@11117 outC1@11171 outD1@11392 M0@11613 csa@11667 kid@11823 limA@11977 wr1@12091 kid'@12268""",
    "s": """raw14@210 Wx1b@939 A10@1266 A14@1701 Lp0@2136 A8@2252 A12@2939 raw6@3374 A0@4104 A2@4716 A6@5151 KG0@5811 A4@6031 A5@6249 AB0@6854 stg0@7459 KG1@8329 top0@8549 cf0@8770 wa0@8991 AB1@9383 stg1@9491 Wx0a@-2208 cov@10504 Wx0c@-1800 Wx0b@-1637 top1@11142 cf1@11363 wa1@11704 Wx1a@-390""",
    "g": """Wx1h@173 Wx1f@860 Wx1g@1546 sendw0@6941 sendw1@8759 sendc0@9255 Wx0g@-1645 Wx0h@-958 sendc1@12087""",
    "t": """sub14@194 add14@1149 tL0@1426 sub6@1564 kv0@2209 kv1@2283 kL1@2462 tv0@2535 sum8@2897 sum12@3584 tL1@4172 add6@4314 tv1@5492 sum0@5786 tS0@6506 sum4@6677 own0@7264 kS1@7817 eq0@8173 tS1@9034 cw1@9378 own1@9490 cnt@10769 eq1@10907 cw0@-268 kL0@-155 kS0@-82""",
}
UNUSED2 = {
    "v": """-mj@-9014 -mo16@-7800 -mi@-7258 -inC0@-4174 -inC1@-4030 <Wx0a@-3315 <Wx0b@-3296 <GT0@-3262 <GT1@-2833 -keyW@-2815 -klb@-2637 <raw10@-2490 <G0@-2480 <raw8@-2101 <raw0@-912 <mj@-661 <mi@-503 <raw4@-432 <vI0@71 -keyW'@909 <klb@909 <raw12@1654 <G1@2266 <yy0@2297 -XG@2404 <raw2@2435 <outO0@3447 <outW0@3794 -kid'@3979 <Wx1b@4005 <KT0@4111 <x20'@4385 <x20@4467 <vI1@4479 <l20@5544 -kid''@5756 <raw5@5879 <es0@5928 <u20@7001 >outC1@7914 >outC0@8061 <outC0@8310 >outD0@8522 >outD1@8712 >kid@8830 <outD0@8842 >xx1@9200 >xx1'@9279 >dm@9328 >dn@9570 >x21'@9629 >x21@9650 >M0@9695 >s2u1@9940 >ncd1@10157 >l21@10570 >u21@10660 >kid''@10897 +klb@10957 +Y@11155 >kid'@11798 >kid''''@11832 >wr1@11895 >kid'''@12034 >s2u1'@12243 >yf0@12581 >kid'''''@12700 >kid''''''@12740 +X1@12880 >kid'''''''@13165 +X0@13246 +XT1@13556 +XT0@15471 >yf1@15608""",
    "s": """-mk16@-6100 -keyW'@-4354 <raw14@-4174 <Wx0d@-3078 -XF@-2814 <Wx0c@-2814 <Lp0@-1844 <A8@-1594 <A14@-1211 <Wx1a@-1159 -keyW@-743 -XF'@-741 <A10@478 <raw6@1384 <A4@1566 <A12@1781 <keyW'@1781 <keyW''@1783 <A5@2162 <keyW'''@3035 <A0@3414 -M0@3456 <keyW@3514 <KG0@3830 <Lp1@4025 <A2@5758 <A6@5828 <AB0@5901 <stg0@6946 >top1@8769 >cf1@9073 +mk16@9379 >wa1@11803 +ymo@17767""",
    "g": """<Wx1d@-3917 <Wx1e@-1026 <Wx1g@-943 <Wx1f@309 <Wx1h@847 -kid'@2747 -kid@3974 -kid'''@6113 <sendc0@6392 -kid''@8437 <sendw0@8437 -kid''''@8438 -kid'''''@8509 <sendw1@9947""",
    "t": """<add14@-4519 -ksum0@-4425 -rot@-4043 <ksum1@-4035 <tL0@-3916 -rows3@-2513 <sum0@-1124 -rows1@-581 -rows0@-547 <tS0@-522 -code@-376 -rows2@-330 <sub14@-330 <tv1@-73 <kS0@21 <kL1@240 <sum8@625 <rows4@758 <rows7@758 <tL1@870 <rows5@1201 <rows6@1201 <sum12@1872 <tv0@2175 <add6@2348 -join@2651 <sub6@2651 <sum4@5842 >eq1@8337 >own1@9551 +turn1@10448 +code@10468 +turn0@11687 +turn2@11783 +yd0@12998 +back@14080 +yd1@16391""",
}
UNUSED = {
    "v": """Wx1c@53 G0@210 raw10@264 GT0@994 raw8@1048 raw12@1778 kid''@14619 G1@2662 raw0@2717 raw2@3447 GT1@4177 vI0@4282 s2u1@16508 kid'''@16563 yy0@4608 raw4@4662 outO0@5053 s2u1'@17218 raw5@5161 outW0@5552 KT0@5803 kid''''@17969 xo0@6012 kid'''''@18333 pn@6376 xo0'@6431 kid''''''@18697 es0@6741 kid'''''''@19062 vI1@7105 ncd0@7221 x20@7275 x20'@7330 yy1@7431 xx0@7485 xx0'@7540 l20@7594 outO1@7695 u20@7858 outW1@7960 outC0@8180 KT1@8401 xo1@8455 outD0@8510 na@8731 xo1'@8785 wr0@9009 es1@9332 dn@9441 s2u0@9496 ncd1@9651 x21@9706 x21'@9760 xx1@9916 dm@9970 l21@10024 xx1'@10079 M0@10234 u21@10289 outC1@10553 outD1@10774 csi@10995 s2u0'@11049 Wx0d@-1006 csa@11259 kid@11314 limA@11524 wr1@11578 kid'@11755 limT@11909""",
    "s": """raw14@210 Wx1b@939 A10@1266 A14@1701 Lp0@2136 A8@2252 A12@2718 raw6@3153 A0@3883 A2@4387 Lp1@4822 A6@4937 KG0@5373 A4@5593 A5@5811 AB0@6416 stg0@7315 KG1@7960 top0@8180 cf0@8401 wa0@8622 AB1@9014 stg1@9122 Wx0a@-2767 cov@9916 Wx0b@-2140 Wx0c@-1813 cf1@10623 top1@10844 wa1@11141 Wx1a@-510""",
    "g": """Wx1f@53 Wx1g@740 Wx1h@1426 sendw0@5982 sendw1@8390 sendc0@8941 Wx0h@-2203 sendc1@11205""",
    "t": """kS0@82 kv1@359 add14@1149 kL0@1426 tL0@1499 sub6@1638 kv0@2191 tv0@2462 kL1@2756 sum8@2897 sum12@3485 add6@4093 tL1@4441 tv1@5147 sum0@5441 tS0@6068 sum4@6239 kS1@6826 own0@7103 eq0@7804 tS1@8665 cw1@9009 own1@9121 cnt@10180 eq1@10343 cw0@-582 sub14@-470""",
}
ROUND = {q: " ".join([w for w in ROUND[q].split() if w[0] not in "<>-+"] + EDGE[q].split()) for q in ROUND}
KQ = [0, 512, 1536, 2560, 3584, 4096]
LOADS = ["wts", "feat0", "mkey", "mobj", "cand", "want", "feat", "last"]
CT = 272
D = 32
CY, PE, GA, SCAT, HOP, FLY, FLYW, LOAD, RATE, ROWS = 0.85, 0.54, 1.56, 3.8, 210.0, 2600.0, 2600.0, 1600.0, 300.0, 80000.0

_f, _b, _h, _i, _u = "float32", "bfloat16", "float16", "int32", "uint16"
_t = lambda n, d: ("sbuf", [128, n], d)
_l = lambda n, d: ("sbuf", [128, n, 17], d)
SCRATCH = {
    "featW": _t(W, _b), "kidi": _t(W, _i), "kid": _t(D + W + L, _f), "yc": _t(32, _f), "keyW": _t(W, _b),
    "A": _l(256, _b), "limT": _t(136, _b), "RS3": ("sbuf", [128, 4, 52], _f), "raw": _t(W, _b), "Wx": _t(W, _b),
    "LH": _t(144, _b), "LW": _t(144, _b), "EX": _t(2048, _b), "SH": _t(2048, _b), "R16": ("sbuf", [128, 8, 32], _b),
    "i1": _t(128, _i), "i1b": _t(128, _i), "i2": _t(16, _i), "i2b": _t(16, _i), "i3": _t(16, _i), "i3b": _t(16, _i), "i4": _t(128, _i), "i5": _t(16, _i), "i6": _t(32, _i),
    "bi": _t(16, _i), "exb": _t(16, _u), "dg": _t(16, _f), "dgn": _t(16, _f), "ib": _t(8, _i), "a0": _t(16, _i), "a1": _t(16, _f), "a2": _t(16, _f), "a3": _t(16, _f), "a4": _t(16, _f), "a5": _t(16, _f),
    "blk": _t(128, _b), "diag": _t(128, _b), "I16": _t(128, _h), "IB": _t(128, _b), "IN": _t(128, _b), "INf": _t(128, _f), "If": _t(128, _f), "FF": _t(1024, _f),
    "half": _t(128, _f), "Kc": _l(8, _b), "ob": _t(136, _b), "T1": _t(128, _b), "CW": ("sbuf", [128, 4, 52], _b),
    "RST": _t(208, _f), "RN": _t(128, _f), "CJ": _t(16, _f), "CJ2": _t(256, _f), "col": _t(16, _f), "wti": _t(1, _i), "wtf": _t(1, _f),
    "ci": _t(256, _i), "mkb": _t(256, _b), "moi": _t(256, _i), "mk16": _t(256, _b), "mo16": _t(256, _h), "mi": _t(256, _i), "mj": _t(256, _i),
    "klb": ("sbuf", [128, 8, 32], _b),
    "lai": _t(16, _i), "LX": _t(32, _f), "LT": _t(32, _f), "prev0": _t(16, _f),
    "X": ("sbuf", [128, 16, 32], _h), "XT": ("sbuf", [128, 16, 32], _h), "Y": ("sbuf", [128, 8, 32], _b), "PF": _t(512, _f),
    "XF": ("sbuf", [128, 16, 32], _f), "XG": ("sbuf", [128, 16, 32], _f),
    "G": ("sbuf", [128, 8, 32], _h), "GT": ("sbuf", [128, 8, 32], _h), "PM": _t(512, _h), "PK": _t(512, _b), "S4": ("sbuf", [128, 4, 2, 16], _h),
    "M": ("sbuf", [128, 8, 32], _f), "Lp": _t(272, _f), "vI": _t(272, _i), "yy": _t(16, _i), "KG": _t(256, _b), "KT": ("sbuf", [128, 8, 32], _b), "AB": _t(256, _f), "es": _t(256, _i),
    "x2": _t(32, _i), "l2": _t(32, _i), "u2": _t(32, _u), "top": _t(256, _f), "cf": _t(256, _f),
    "na": _t(16, _f), "cov": _t(16, _f), "ncd": _t(16, _f), "xo": ("sbuf", [128, 8, 3], _h), "xx": ("sbuf", [128, 8, 3], _h), "wa": _t(416, _f), "wr": _t(416, _f),
    "s2u": _t(16, _u), "pn": _t(16, _f), "dn": _t(16, _f), "dn2": _t(16, _f),
    "cs": _t(1, _f), "csi": _t(1, _i), "csa": _t(1, _i), "limA": _t(1, _f),
    "inF": _t(256, _f), "ymo": _t(256, _f), "acc": _t(512, _f),
    "outC": _t(STEPS * CT, _u), "outD": ("sbuf", [128, STEPS, CT], _u), "inC": _t((STEPS + 1) * CT, _u), "outW": _t(STEPS * 256, _b), "inW": _t(STEPS * 256, _b),
    "pv0": ("psum", [128, 512], _f), "pv1": ("psum", [128, 512], _f), "pT": ("psum", [128, 9, 52], _f), "pL": ("psum", [128, 30, 17], _f),
    "pS": ("psum", [128, 16, 32], _f), "pX0": ("psum", [128, 512], _f), "pX1": ("psum", [128, 512], _f), "pX2": ("psum", [128, 512], _f),
}
DMAS = ["cand", "want", "wts", "last", "mkey", "mobj", "feat0", "feat", "ymu", "yd0", "yd1", "yd2", "yd3"] + ["k%d" % q for q in range(8)] + ["yn%d" % h for h in range(NP)]
SEMAPHORES = ["sv", "st", "ss", "sg", "ls"] + ["d_" + n for n in DMAS] + [x + "%d_%d" % (t, h) for x in "cw" for t in range(1, STEPS + 1) for h in range(NP)]
OWN = {"v": "sv", "t": "st", "s": "ss", "g": "sg"}


def make():
    ops, tags, lag, seen = [], {}, [0.0, -1], {}

    def tag(n):
        if n not in tags:
            tags[n] = {"w": [], "r": [], "base": [], "full": False, "mm": None}
        return tags[n]

    def add(q, call, ns, r=(), w=(), p=(), acc=False, sem=None, lat=0.0, after=(), nm=None):
        i, pre = len(ops), {}
        if nm is None:
            nm = (tuple(w) + tuple(p))[0]
            nm = nm[:-3] + nm[-1] if nm[:2] in ("in", "ou") else "Wx" + nm[-1] + "abcdefgh"[int(nm[2:-2]) // (2 if q == "g" else 4)] if nm[:2] == "Wx" else nm
            seen[lag[1], q, nm] = seen.get((lag[1], q, nm), -1) + 1
            nm += "'" * seen[lag[1], q, nm] if nm[:2] not in ("Wx", "wa") else ""
        for n in r:
            d = tag(n)
            pre.update({j: True for j in d["w"]})
            if n[0] == "p" and n[1] in "vLSXT":
                pre.update({j: True for j in d["r"] if ops[j]["q"] != q})
        for n in w:
            d = tag(n)
            pre.update({j: True for j in d["w"] + d["r"] + d["base"] if not (acc and ops[j]["q"] == q)})
        for n in p:
            d = tag(n)
            if d["full"] or d["r"]:
                d["base"], d["w"], d["r"], d["full"] = d["w"] + d["r"], [], [], False
            pre.update({j: True for j in d["base"]})
        for j in list(after) + [tag(n)["mm"] for n in tuple(w) + tuple(p) if q == "t" and tag(n)["mm"] is not None]:
            pre.setdefault(j, False)
        for n in r:
            tag(n)["r"].append(i)
        for n in w:
            d = tag(n)
            if acc:
                d["w"].append(i)
                d["r"] = []
            else:
                d["w"], d["r"], d["base"], d["full"] = [i], [], [], True
        for n in p:
            tag(n)["w"].append(i)
        if q == "t":
            for n in tuple(w) + tuple(p):
                tag(n)["mm"] = i
        ops.append({"nm": nm, "step": lag[1], "lag": lag[0], "q": q, "call": call, "ns": ns, "pre": pre, "sem": sem, "lat": lat})
        return i
    return ops, add, lag


def order(ops):
    n, ns = len(ops), [o["ns"] for o in ops]
    post = [[] for i in range(n)]
    for i, o in enumerate(ops):
        for j, sem in o["pre"].items():
            post[j].append((i, ops[j]["lat"] + HOP if sem else 0.0))
    when = {(q, w.split("@")[0]): float(w.split("@")[1]) for q in ROUND for w in ROUND[q].split()}
    due, way, row, row_end = [None] * n, [0.0] * n, set(), {}
    for i in range(n - 1, -1, -1):
        o = ops[i]
        way[i] = ns[i] + max([d + way[k] for k, d in post[i]] + [o["lat"]])
        edge = (o["q"], {-1: "-", 0: "<", STEPS - 1: ">", STEPS: "+"}.get(o["step"], "") + o["nm"])
        if edge in when or (0 <= o["step"] < STEPS and (o["q"], o["nm"]) in when):
            due[i] = PERIOD * min(max(o["step"], 0), STEPS - 1) + when.get(edge, when.get((o["q"], o["nm"])))
            if 0 < o["step"] < STEPS - 1:
                row.add(i)
        elif any(due[k] is not None for k, d in post[i]):
            due[i] = min(due[k] - d for k, d in post[i] if due[k] is not None) - ns[i]
    due = [PERIOD * STEPS + END - way[i] if due[i] is None else due[i] for i in range(n)]
    left, ready, start = [len(o["pre"]) for o in ops], [0.0] * n, [0.0] * n
    busy, cand = {o["q"]: [] for o in ops}, [(due[i], i) for i in range(n) if not left[i]]
    while cand:
        c = min(cand)
        cand.remove(c)
        i = c[1]
        at, b = ready[i], busy[ops[i]["q"]]
        if i in row:
            at = max(at, row_end.get(ops[i]["q"], 0.0))
        if ops[i]["q"] != "x":
            k = len(b)
            while k and b[k - 1][1] > at:
                k -= 1
            while k < len(b) and b[k][0] < at + ns[i] - 1e-6:
                at = max(at, b[k][1])
                k += 1
            b.insert(k, (at, at + ns[i]))
        start[i] = at
        if i in row:
            row_end[ops[i]["q"]] = at + ns[i]
        for k, d in post[i]:
            ready[k] = max(ready[k], at + ns[i] + d)
            left[k] -= 1
            if not left[k]:
                cand.append((due[k], k))
    return sorted(range(n), key=lambda i: (start[i], i))


def emit(g, T, ops, seq):
    Q = {"v": g.vector, "t": g.tensor, "s": g.scalar, "g": g, "y": g.sync}
    cnt, known, hist, at = {}, {q: {} for q in Q}, {}, {}
    for i in seq:
        o = ops[i]
        q = o["q"]
        if q == "x":
            at[i] = o["sem"]
            cnt[o["sem"][0]] = o["sem"][1]
            continue
        need = {}
        for j, sem in o["pre"].items():
            if sem:
                s, c = at[j]
                need[s] = max(need.get(s, 0), c)
        for s in sorted(need, key=lambda s: -len(hist.get((s, need[s]), {}))):
            if known[q].get(s, 0) < need[s]:
                Q[q].wait_ge(T.sem[s], need[s])
                for s2, c2 in list(hist.get((s, need[s]), {}).items()) + [(s, need[s])]:
                    known[q][s2] = max(known[q].get(s2, 0), c2)
        s, k = o["sem"] or (OWN[q], 1)
        cnt[s] = cnt.get(s, 0) + k
        at[i] = (s, cnt[s])
        hist[at[i]] = dict(known[q])
        ins = o["call"]()
        if s != "ls":
            ins.then_inc(T.sem[s], k)
    for s in sorted(cnt):
        if known["g"].get(s, 0) < cnt[s]:
            g.wait_ge(T.sem[s], cnt[s])


def rank_program(g, core, T, topo):
    rank, n = T.rank_of(core), len(T.cores)
    if rank is None:
        return
    ops, add, lag = make()
    v, te, sc = g.vector, g.tensor, g.scalar
    nxt, prv = T.cores[(rank + 1) % n], T.cores[(rank - 1) % n]
    nin = len(topo.engines(prv, core))
    cy = lambda k: max(64.0, k) * CY
    ga = lambda k: (60.0 + GA * k) * CY
    NP = len(PARTS)

    def ts(ns, out, in0, s1, s2, o0, o1, r, w=(), p=()):
        args = (out, in0, s1, s2, o0) if o1 is None else (out, in0, s1, s2, o0, o1)
        add("v", lambda: v.tensor_scalar(*args), ns, r, w, p)

    def tt(ns, out, a, b, o, r, w=(), p=()):
        add("v", lambda: v.tensor_tensor(out, a, b, o), ns, r, w, p)

    def cp(ns, out, a, r, w=(), p=()):
        add("v", lambda: v.tensor_copy(out, a), ns, r, w, p)

    def tr(ns, out, a, r, w):
        add("v", lambda: v.transpose(out, a), ns, r, w)

    def scan(ns, out, d0, d1, o0, o1, r, w):
        add("v", lambda: v.tensor_tensor_scan(out, d0, d1, 0.0, o0, o1), ns, r, w)

    def act(ns, out, a, f, r, w=(), p=(), **kw):
        add("s", lambda: sc.activation(out, a, f, **kw), ns, r, w, p)

    def copy(e, dims, out, a, r, w=(), p=(), fast=1.0):
        k = dims[0] * dims[1]
        if e == "v":
            cp(cy(k * fast), out, a, r, w, p)
        elif e == "s":
            act(cy(k), out, a, AF.Copy, r, w, p)
        else:
            add("g", lambda: g.affine_select(out, a, [[0, x] for x in dims if x > 1], ALU.is_equal, 0.0, 0, 0), 180 + 2 * k * CY, r, w, p)

    def mm(k, out, l, rh, st, sp, r, w, part=False, nm=None):
        if part:
            add("t", lambda: te.matmul(out, l, rh, st, sp), max(64, k) * PE, r, p=(w,), nm=nm)
        else:
            add("t", lambda: te.matmul(out, l, rh, st, sp), max(64, k) * PE, r, (w,), acc=not st, nm=nm)

    def fill(ns, ap, x, w=(), p=()):
        add("v", lambda: v.memset(ap, x), ns, (), w, p)

    def iota(k, out, pat, base, ch, w, **kw):
        last["g"] = [add("g", lambda: g.iota(out, pat, base, ch, **kw), 140 + 2 * k * CY, (), (w,), after=last["g"])]
    last = {"s": [], "y": [], "g": [], "bytes": [0.0]}

    def dma(q, out, in_, name, nbytes, r=(), w=()):
        last["bytes"][0] = nbytes + ROWS + (0.0 if r else last["bytes"][0])
        last[q] = [add(q, lambda: (sc if q == "s" else g.sync).dma_start(out, in_), 60.0, r, w, sem=("d_" + name, 16), lat=LOAD + last["bytes"][0] / RATE, after=() if r else last[q], nm=name)]

    def send(out, in_, sem, r, w, fly=FLY):
        rid, pid, _se = topo.addr(nxt)
        mask = topo.mask(core, nxt)
        if isinstance(in_, list):
            call = lambda: g.remote_dma_fused([RemoteDMATransfer(dst_ids=[DstId(rid=rid, pnc=pid)], dma_engine_mask=mask, remote_sem=T.sem[sem], srcs=in_, dsts=[out], alu_op=2)], local_sem=T.sem.ls)
        else:
            call = lambda: g.remote_dma(out, in_, T.sem[sem], T.sem.ls, pid, rid, mask)
        i = add("g", call, 400.0, r, sem=("ls", bin(mask).count("1")), nm="send" + sem[0] + sem[-1])
        add("x", None, fly, (), w, sem=(sem, nin), after=(i,))

    def bank(ps, k):
        return T[ps][:, 0:k] if ps[1] in "Xv" else T[ps][:, 0:k // 32, :] if ps == "pS" else T[ps][:, 0:k // 16, 0:16]
    C = lambda j: T.col[:, j:j + 1]
    M1, M0, SCT, BIT, DUMP, OFF, K0, K1, DU0 = range(9)
    S = cy(16)
    at = lambda t, h: CT * t + (0 if h else 144)
    own = lambda h, c: W + L - 16 * PARTS[h][1] + 16 * (c - PARTS[h][0])
    tag_all = lambda s: [s + "%d" % h for h in range(NP)]

    loads = {"wts": (T.wti[:], T.wts[:], 512, ("wti",)), "feat0": (T.featW[:, 0:W // 2], T.feat[:, 0:W // 2], 524288, ("feat0",)),
             "cand": (T.ci[:], T.cand[:], 131072, ("ci",)), "want": (T.inW[:, 0:256], T.want[:], 65536, tag_all("inW0_")),
             "feat": (T.featW[:, W // 2:W], T.feat[:, W // 2:W], 524288, ("feat",)), "mkey": (T.mkb[:], T.mkey[:], 65536, ("mkb",)),
             "mobj": (T.moi[:], T.mobj[:], 131072, ("moi",)), "last": (T.lai[:], T.last[:], 8192, ("lai",))}
    for nm in LOADS:
        dma("y", loads[nm][0], loads[nm][1], nm, loads[nm][2], w=loads[nm][3])
    for q, (a, e) in enumerate(zip(KQ, KQ[1:])):
        dma("y", T.kidi[:, a:e], T.kids[:, a:e], "k%d" % q, 512 * (e - a), w=("kidi%d" % q,))

    small = dict(allow_small_or_imprecise_dtypes=True)
    iota(16, T.i5[:], [[0, 16]], 0, 1, "i5")
    iota(16, T.i2[:], [[1, 16]], 128, -1, "i2")
    iota(128, T.i1[:], [[16, 8], [0, 16]], 15, -1, "i1")
    iota(16, T.i3[:], [[1, 16]], 0, 1, "i3")
    fill(cy(68), T.Kc[:], 0.0, w=("Kc",))
    fill(S, T.Kc[32:33, :, 0:16], -RC * RS, w=("Kc",))
    fill(S, T.Kc[32:33, :, 16], BIG, w=("Kc",))
    iota(136, T.Kc[0:1, :, :], [[0, 8], [8192, 17]], 6144, 0, "Kc", **small)
    for h, (c0, c1) in enumerate(PARTS):
        iota(16, T.i6[:, 2 * c0:2 * c1], [[0, 2], [16, c1 - c0]], own(h, c0), 0, "i6")
    iota(128, T.i4[:], [[0, 8], [1, 16]], 0, 0, "i4")
    fill(cy(128), T.LH[:], 0.0, w=("LH",))
    ts(S, T.i2b[:], T.i2[:], 15, None, ALU.bitwise_and, None, ("i2",), ("i2b",))
    ts(S, T.bi[:], T.i5[:], 15, None, ALU.bitwise_and, None, ("i5",), ("bi",))
    ts(cy(128), T.i1b[:], T.i1[:], 4, None, ALU.arith_shift_right, None, ("i1",), ("i1b",))
    ts(S, T.ib[:, 0:1], T.i5[:, 0:1], 4, 1, ALU.logical_shift_right, ALU.bitwise_and, ("i5",), ("ib0",))
    ts(S, T.ib[:, 1:2], T.i5[:, 0:1], 3, 1, ALU.logical_shift_right, ALU.bitwise_and, ("i5",), ("ib1",))
    ts(S, T.dg[:], T.i2b[:], 0.0, None, ALU.is_equal, None, ("i2b",), ("dg",))
    cp(S, T.exb[:], T.bi[:], ("bi",), ("exb",))
    ts(cy(128), T.blk[:], T.i1b[:], 0.0, None, ALU.is_equal, None, ("i1b",), ("blk",))
    act(ga(128), T.diag[:], T.dg[:].indirect(T.exb[:, 0:8]), AF.Copy, ("dg", "exb"), ("diag",))
    ts(S, T.LH[:, 15:143:16], T.blk[:, 0::16], RS, None, ALU.mult, None, ("blk",), ("LH",))
    cp(S, C(M1), T.ib[:, 0:1], ("ib0",), ("m1",))
    ts(S, C(M0), T.ib[:, 0:1], -1.0, 1.0, ALU.mult, ALU.add, ("ib0",), ("m0",))
    ts(S, C(SCT), T.ib[:, 1:2], -1.0, 1.0, ALU.mult, ALU.add, ("ib1",), p=("sct",))
    cp(S, C(SCT + 1), T.ib[:, 1:2], ("ib1",), p=("sct",))
    cp(S, C(DUMP), T.bi[:, 0:1], ("bi",), ("dump",))
    ts(S, T.yc[:], T.i6[:], C(DUMP), None, ALU.add, None, ("i6", "dump"), ("yc",))
    fill(S, T.kid[:, 0:D], 0.0, p=("kid",))
    tt(cy(256), T.IB[:], T.blk[:], T.diag[:], ALU.mult, ("blk", "diag"), ("IB",))
    cp(S, T.I16[:], T.IB[:], ("IB",), ("I16",))
    for nm, x in (("IN", -1.0), ("INf", -1.0), ("T1", 1.0 / DB)):
        ts(cy(128 if nm == "INf" else 64), T[nm][:], T.IB[:], x, None, ALU.mult, None, ("IB",), (nm,))

    for h, (c0, c1) in enumerate(PARTS):
        cp(cy(16 * (c1 - c0)), T.inC[:, at(0, h):at(0, h) + 16 * (c1 - c0)], T.ci[:, 16 * c0:16 * c1], ("ci",), ("inC0_%d" % h,))
    ts(S, T.wtf[:], T.wti[:], 1.0 / RS, None, ALU.mult, None, ("wti",), ("wtf",))
    fill(cy(128), T.RN[:], 0.0, w=("RN",))
    fill(S, T.RN[:, 0::16], float(NONE), w=("RN",))
    for e in range(2):
        ts(S, C(DU0 + e), T.bi[:, 0:1], 16.0 * e, 1.0 / DB, ALU.add, ALU.mult, ("bi",), p=("dmp",))
    fill(S, T.outD[:, :, 128:144], 0, w=("nought",))
    for i in range(8 - max(YP), 8):
        act(cy(128), T.FF[:, 128 * (7 - i):128 * (8 - i)], T.IB[:], AF.Copy, ("IB",), p=("F",), scale=float(i + 1))
    act(cy(128), T.If[:], T.IB[:], AF.Copy, ("IB",), ("If",))
    fill(S, T.limA[:], RS * (LIM - 1), w=("limA",))
    fill(S, T.ob[:], 1.0, w=("ob",))
    fill(cy(128), T.half[:], 0.5, w=("half",))
    ts(S, T.dgn[:], T.dg[:], -1.0, None, ALU.mult, None, ("dg",), ("dgd",))
    for b in range(16):
        act(cy(128), T.EX[:, 128 * b:128 * b + 128], T.blk[:], AF.Copy, ("blk", "dgd"), ("EX%d" % b,), scale=T.dgn[:, b:b + 1])
    fill(cy(104), T.CW[:], 0.0, w=("CW",))
    for a in (2, 36):
        ts(S, T.CW[:, :, a:a + 16], T.i4[:, 0:64], C(DUMP), BIG, ALU.is_ge, ALU.mult, ("i4", "dump"), p=("CW",))
    fill(S, T.CW[:, :, 1:36:34], (2048.0 + D) / DB, p=("CW",))
    for e, (a, x) in enumerate(((0, 18), (18, 52))):
        act(cy(4 * (x - a)), T.RS3[:, :, a:x], T.CW[:, :, a:x], AF.Identity, ("CW", "dmp"), p=("RS3",), scale=0.0, bias=C(DU0 + e))
    fill(S, T.RS3[:, :, 0:19:18], BIG, w=("RS3",))
    act(cy(208), T.RST[:], T.RS3[:], AF.Copy, ("RS3",), ("RST",))
    fill(cy(136), T.A[:, :, 16], 0.0, w=["A%d" % c for c in range(16)])
    fill(cy(68), T.limT[:], RS * (LIM - 1), w=("limT",))
    ts(S, T.i3b[:], T.i3[:], 15, None, ALU.bitwise_and, None, ("i3",), ("i3b",))
    ts(S, T.a0[:], T.i3[:], 14, None, ALU.bitwise_and, None, ("i3",), ("a0",))
    ts(S, T.a2[:], T.i3b[:], 4.0, -2.0, ALU.is_ge, ALU.mult, ("i3b",), ("a2",))
    ts(S, T.a3[:], T.i3b[:], 10.0, -2.0, ALU.is_ge, ALU.mult, ("i3b",), ("a3",))
    tt(S, T.a1[:], T.a0[:], T.i3b[:], ALU.add, ("a0", "i3b"), ("a1",))
    tt(S, T.a4[:], T.a2[:], T.a3[:], ALU.add, ("a2", "a3"), ("a4",))
    tt(S, T.a5[:], T.a1[:], T.a4[:], ALU.add, ("a1", "a4"), ("a5",))
    ts(S, T.CJ[:], T.a5[:], 4096.0, None, ALU.mult, None, ("a5",), ("CJ",))
    act(ga(256), T.CJ2[:], T.CJ[:].indirect(T.exb[:]), AF.Copy, ("CJ", "exb"), ("CJ2",), bias=2048.0)
    cp(S, T.R16[:, :, 0:16], T.IB[:], ("IB",), p=("R16",))
    cp(S, T.R16[:, :, 16:32], T.IB[:], ("IB",), p=("R16",))
    for b in range(16):
        copy(SHQ[b], (8, 16), T.SH[:, 128 * b:128 * b + 128], T.R16[:, :, b:b + 16], ("R16",), p=("SH",), fast=0.5)
    for s in range(2):
        cp(S, T.S4[:, :, s, :], T.R16[:, 1 - s::2, 0:16], ("R16",), p=("S4",))
    for e, m, nm in ((0, M0, "m0"), (1, M1, "m1")):
        ts(S, T.PM[:, 384 * e:384 * e + 128], T.I16[:], C(m), None, ALU.mult, None, ("I16", nm), p=("PM",))
        ts(S, T.PM[:, 128 + 128 * e:256 + 128 * e], T.S4[:], C(m), None, ALU.mult, None, ("S4", nm), p=("PM",))
    ts(cy(256), T.PK[:], T.PM[:], KS, None, ALU.mult, None, ("PM",), ("PK",))
    act(cy(512), T.PF[:], T.PK[:], AF.Copy, ("PK",), ("PF",), scale=-1.0 / KS)

    act(cy(256), T.mk16[:], T.mkb[:], AF.Copy, ("mkb",), ("mk16",), scale=KS)
    ts(cy(256), T.mo16[:], T.moi[:], -1.0, 2048.0, ALU.mult, ALU.add, ("moi",), ("mo16",))
    for b in range(16):
        for e, src in enumerate(("mk16", "mo16")):
            mm(16, T[MB][:, b:256:16], T.SH[:, 128 * b:128 * b + 128], T[src][:, b::16], e == 0, e == 1, ("SH", "mk16", "mo16"), MB, part=True, nm="rot")
    for e in range(2):
        act(cy(256), T.XF[:, :, 16 * e:16 * e + 16], T[MB][:, 0:256], AF.Copy, (MB, "m0", "m1"), p=("XF",), scale=C((M0, M1)[e]))
    tr(cy(512), T.XG[:], T.XF[:], ("XF",), ("XG",))
    mm(1024, T[MB][:, 0:256], T.INf[:], T.CJ2[:], True, False, ("INf", "CJ2"), MB, nm="code")
    for e in range(2):
        mm(1024, T[MB][:, 0:256], T.If[:], T.XG[:, :, 16 * e:16 * e + 16], False, e == 1, ("If", "XG"), MB, nm="join")
    act(cy(256), T.M[:], T[MB][:, 0:256], AF.Copy, (MB,), tag_all("M"))
    ts(S, T.LX[:, 0:16], T.lai[:], C(M0), None, ALU.mult, None, ("lai", "m0"), p=("LX",))
    ts(S, T.LX[:, 16:32], T.lai[:], C(M1), None, ALU.mult, None, ("lai", "m1"), p=("LX",))
    tr(S, T.LT[:], T.LX[:], ("LX",), ("LT",))
    tt(S, T.prev0[:], T.LT[:, 0:16], T.LT[:, 16:32], ALU.add, ("LT",), ("prev0",))
    ts(cy(128), T.LW[:], T.LH[:], T.wtf[:], None, ALU.mult, None, ("LH", "wtf"), ("LW",))

    def keys(x):
        for b in range(8 * x, 8 * x + 8):
            mm(256, T.pS[:, 0:8, :], T.LW[:, 15 - b:143 - b], T.featW[:, 256 * b:256 * b + 256], b % 8 == 0, b % 8 == 7, ("LW", "feat" if x else "feat0"), "pS", nm="ksum%d" % x)
        cp(cy(256), T.mi[:], T.pS[:, 0:8, :], ("pS",), ("mi",))
        ts(cy(256), T.mj[:], T.mi[:], 63, None, ALU.bitwise_and, None, ("mi",), ("mj",))
        ts(cy(256), T.klb[:], T.mj[:], -1.0, None, ALU.mult, None, ("mj",), ("klb",))
        for i in range(4 * x, 4 * x + 4):
            ps = KB[i]
            for e in range(2):
                b = 2 * i + e
                mm(256, T[ps][:, 256 * e:256 * e + 256] if ps != "pS" else T[ps][:, 8 * e:8 * e + 8, :], T.EX[:, 128 * b:128 * b + 128], T.klb[:], True, True, ("EX%d" % b, "klb"), ps, part=True, nm="rows%d" % i)
            copy(KEYQ[i], (512, 1), T.keyW[:, 512 * i:512 * i + 512], T[ps][:], (ps,), p=("keyW",))
    keys(0)
    for q, (a, e) in enumerate(zip(KQ, KQ[1:])):
        for x in range(a, e, 512):
            copy(KIDQ[x // 512], (512, 1), T.kid[:, D + x:D + x + 512], T.kidi[:, x:x + 512], ("kidi%d" % q,), p=("kid",))

    def mounts(t):
        N, q = lambda *s: [y for x in s for y in tag_all(x)], 5 * t % 16
        prev, prn = (T.inC[:, CT * t + 128:CT * t + 144], N("inC%d_" % t)) if t else (T.prev0[:], ["prev0"])
        ts(S, T.pn[:], prev, T.CJ[:, q:q + 1], None, ALU.add, None, prn + ["CJ"], ("pn",))
        ts(S, T.na[:], T.vI[:, 0::17], T.limA[:], (1 - RC) * RS, ALU.subtract, ALU.is_ge, N("vI") + ["limA"], ("na",))
        tt(S, T.dn[:], T.pS[:, 0:8, q::16], T.pn[:], ALU.subtract, ("pS", "pn"), ("dn",))
        tt(S, T.dn2[:], T.dn[:], T.na[:], ALU.mult, ("dn", "na"), ("dm",))
        tt(S, T.M[:, :, q::16], T.M[:, :, q::16], T.dn2[:], ALU.add, ["dm"] + N("M"), N("M"))

    def writers(c0, c1, hs, ps):
        N, lb, nc = lambda *s: [x + "%d" % h for x in s for h in hs], slice(c0, c1), c1 - c0
        k, pr, ws = nc // 2, slice(c0 // 2, c1 // 2), slice(26 * c0, 26 * c1)
        ts(S, T.xo[:, pr, 0:2], T.yy[:, lb], 2048.0, None, ALU.subtract, None, N("yy"), p=N("xo"))
        ts(S, T.xo[:, pr, 2], T.yy[:, c0 + 1:c1:2], 2048.0, None, ALU.subtract, None, N("yy"), p=N("xo"))
        ts(S, T.ncd[:, lb], T.es[:, 16 * c0 + 15:16 * c1:16], -1.0, NONE - 2048.0 - D, ALU.mult, ALU.add, N("es"), N("ncd"))
        tt(S, T.xx[:, pr, 1:3], T.xo[:, pr, 0:2], T.ncd[:, lb], ALU.min, N("xo", "ncd"), p=N("xx"))
        tt(S, T.xx[:, pr, 0], T.xo[:, pr, 0], T.ncd[:, c0:c1:2], ALU.min, N("xo", "ncd"), p=N("xx"))
        mm(52 * k, T[ps][:, 0:k, :], T.IB[:], T.CW[:, 0:k, :], True, False, ("IB", "CW"), ps, nm=N("cw")[0])
        for b in range(16):
            mm(3 * k, T[ps][:, 0:k, 2 + b:52:17], T.IB[:], T.xo[:, pr, :], False, False, N("xo"), ps, nm=N("own")[0])
        mm(nc, T[ps][:, 0:k, 1:36:34], T.T1[:], T.xx[:, pr, 1:3], False, False, ["T1"] + N("xx"), ps, nm=N("eq")[0])
        for b in range(16):
            mm(3 * k, T[ps][:, 0:k, 2 + b:52:17], T.EX[:, 128 * b:128 * b + 128], T.xx[:, pr, :], False, b == 15, N("xx"), ps, nm=N("eq")[0])
        act(cy(52 * k), T.wa[:, ws], T[ps][:, 0:k, :], AF.Abs, (ps,), N("wa"))
        scan(cy(52 * k), T.wr[:, ws], T.wa[:, ws], T.RST[:, 0:52 * k], ALU.min, ALU.max, ["RST"] + N("wa"), N("wr"))
        for e in range(2):
            ts(S, T.s2u[:, c0 + e:c1:2], T.wr[:, 26 * c0 + 17 + 34 * e:26 * c1:52], DB, None, ALU.mult, None, N("wr"), p=N("s2u"))

    for t in range(STEPS):
        final = t == STEPS - 1
        lag[1] = t
        for h, (c0, c1) in enumerate(PARTS):
            N = lambda s: s + "%d" % h
            lag[0] = LAG * h
            NC, o = c1 - c0, at(t, h)
            l0, l1, nl, ob = 16 * c0, 16 * c1, 16 * NC, CT * t + 128 + c0
            ls, lb, pr = slice(l0, l1), slice(c0, c1), slice(c0 // 2, c1 // 2)
            iw, ic, pv = "inW%d_%d" % (t, h), "inC%d_%d" % (t, h), "pv%d" % h
            nf = 16 * sum(m for e, m in CH[h] if e == "f")
            wx = lambda a, k: [N("Wx%d_" % y) for y in range(a, a + k)]
            Wk = lambda e, a, m: T.Wx[:, 16 * a + e:16 * (a + m):16]
            for e, qu in enumerate(WXQ[h] if t else WX0[h]):
                m = nf if e else nl
                if qu == "s":
                    act(cy(m), Wk(e, l0, m), T.inW[:, 256 * t + l0:256 * t + l0 + m], AF.Abs, (iw,), wx(e, 1))
                elif t:
                    copy(qu, (m, 1), Wk(e, l0, m), Wk(0, l0, m), wx(0, 1), wx(e, 1), fast=0.5)
                else:
                    copy(qu, (m, 1), Wk(e, l0, m), T.inW[:, l0:l0 + m], (iw,), wx(e, 1), fast=0.5)
            c = c0
            for u, (e, k) in enumerate(CH[h]):
                a, raw, rn, an = o + 16 * (c - c0), T.raw[:, 256 * c:256 * (c + k)], ["raw%d" % y for y in range(c, c + k)], ["A%d" % y for y in range(c, c + k)]
                src = T.featW[:].indirect(T.inC[:, a:a + 16 * k])
                if e == "f":
                    tt(ga(256 * k), raw, src, T.Wx[:, 256 * c:256 * (c + k)], ALU.subtract, ["feat", "feat0", ic] + wx(0, 16), rn)
                    act(cy(256 * k), T.A[:, 16 * c:16 * (c + k), 0:16], raw, AF.Abs, rn, an)
                else:
                    px = "pX%d" % ([(x, y) for x in range(NP) for y, z in enumerate(CH[x]) if z[0] != "f"].index((h, CH[h].index((e, k), u))) % 3)
                    for y in range(16):
                        mm(16 * k, T[px][:, y:256 * k:16], T.IN[:], Wk(0, 16 * c, 16 * k), y == 0, False, ["IN"] + wx(0, 1), px, nm="sub%d" % c)
                    if e == "p":
                        cp(ga(256 * k), raw, src, ("feat", "feat0", ic), rn)
                    else:
                        act(ga(256 * k), raw, src, AF.Copy, ("feat", "feat0", ic), rn)
                    mm(256 * k, T[px][:, 0:256 * k], T.IB[:], raw, False, True, ["IB"] + rn, px, nm="add%d" % c)
                    act(cy(256 * k), T.A[:, 16 * c:16 * (c + k), 0:16], T[px][:, 0:256 * k], AF.Abs, (px,), an)
                c += k
            if t == h == 0:
                keys(1)
            ts(cy(nl / 2), T.G[:, pr, :], T.inC[:, o:o + nl], 2048.0, None, ALU.subtract, None, (ic,), (N("G"),))
            tr(cy(nl / 2), T.GT[:, pr, :], T.G[:, pr, :], (N("G"),), (N("GT"),))

            def turned(ps, PM, nm, XT, nxt_, stop):
                for e in range(2):
                    for s in range(2):
                        out = T.pS[:, pr, 16 * e:16 * e + 16] if ps == "pS" else T[ps][:, e:NC:2, 0:16]
                        mm(8 * NC, out, PM[:, 256 * e + 128 * s:256 * e + 128 * s + 128], XT[:, pr, 16 * s:16 * s + 16], False, stop and e + s == 2, (nm, nxt_), ps, nm=N("t" + ps[1]))
            mm(17 * NC, T.pL[:, 0:NC, :], T.ob[0:33, 0:128], T.Kc[0:33, 0:NC, :], True, False, ("ob", "Kc"), "pL", nm=N("kL"))
            turned("pL", T.PM, "PM", T.GT, N("GT"), True)
            l17, back = slice(17 * c0, 17 * c1), lambda a, e: slice(17 * e - 1, 17 * a - 1 if a else None, -1)
            if LPQ[h] == "v":
                ts(cy(17 * NC), T.Lp[:, l17], T.pL[:, 0:NC, :], T.limA[:], None, ALU.add, None, ("pL", "limA"), (N("Lp"),))
            else:
                act(cy(17 * NC), T.Lp[:, l17], T.pL[:, 0:NC, :], AF.Identity, ("pL", "limA"), (N("Lp"),), bias=T.limA[:])
            mm(17 * NC, T[pv][:, 0:17 * NC], T.IN[:], T.limT[:, 0:17 * NC], True, False, ("IN", "limT"), pv, nm=N("kv"))
            for a, e in BATCH[h]:
                if (a, e) == BATCH[h][TV[h]]:
                    mm(68 * NC, T[pv][:, 0:17 * NC], T.If[:], T.Lp[:, l17], False, False, ("If", N("Lp")), pv, nm=N("tv"))
                for b in range(16):
                    mm(17 * (e - a), T[pv][:, 17 * a:17 * e], T.LH[:, 15 - b:143 - b], T.A[:, 16 * (c0 + a) + b:16 * (c0 + e):16, :], False, b == 15 and (a, e) == BATCH[h][-1],
                       ["LH"] + ["A%d" % y for y in range(c0 + a, c0 + e)], pv, nm="sum%d" % (c0 + a))
            scan(cy(17 * NC), T.vI[:, back(c0, c1)], T[pv][:, back(0, NC)], T.Lp[:, back(c0, c1)], ALU.min, ALU.max, (pv, N("Lp")), (N("vI"),))
            ts(S, T.yy[:, lb], T.vI[:, 17 * c0:17 * c1:17], 4095, None, ALU.bitwise_and, None, (N("vI"),), (N("yy"),))
            ou, oo = T.outC[:, ob:ob + NC], "outO%d_%d" % (t, h)
            cp(S, ou, T.yy[:, lb], (N("yy"),), (oo,))
            if KGQ[h] == "v":
                cp(ga(nl), T.KG[:, ls], T.keyW[:].indirect(ou), ("keyW", oo), (N("KG"),))
            else:
                act(ga(nl), T.KG[:, ls], T.keyW[:].indirect(ou), AF.Copy, ("keyW", oo), (N("KG"),))
            if not final:
                ow = T.outW[:, 256 * t + l0:256 * t + l1]
                tt(ga(nl), ow, T.featW[:].indirect(ou), Wk(0, l0, nl), ALU.subtract, ["feat", "feat0", oo] + wx(0, 1), ("outW%d_%d" % (t, h),))
                send(T.inW[:, 256 * (t + 1) + l0:256 * (t + 1) + l1], ow, "w%d_%d" % (t + 1, h), ("outW%d_%d" % (t, h),), ("inW%d_%d" % (t + 1, h),), FLYW)
            tr(cy(nl / 2), T.KT[:, pr, :], T.KG[:, ls], (N("KG"),), (N("KT"),))
            mm(4 * nl, T.pS[:, pr, :], T.INf[:], T.M[:, pr, :], True, False, ("INf", N("M")), "pS", nm=N("kS"))
            turned("pS", T.PK, "PK", T.KT, N("KT"), True)
            act(cy(nl), T.AB[:, ls], T.pS[:, pr, :], AF.Abs, ("pS",), (N("AB"),))
            scan(cy(nl), T.es[:, ls], T.RN[:, 0:nl], T.AB[:, ls], ALU.max, ALU.min, ("RN", N("AB")), (N("es"),))
            two = lambda b, e: b[:, 2 * c0 + NC * e:2 * c0 + NC * e + NC]
            both = lambda b: b[:, 2 * c0:2 * c1]
            for e, bit in enumerate((16, 2)):
                ts(S, two(T.x2, e), T.es[:, l0 + 15:l1:16], 4095 + 4096 * bit + NONE, None, ALU.bitwise_and, None, (N("es"),), p=(N("x2"),))
            tt(S, both(T.l2), both(T.x2), both(T.yc), ALU.min, (N("x2"), "yc"), (N("l2"),))
            stg, win, wn = T.kid[:, D + own(h, c0):D + own(h, c1)], T.kid[:, D:D + own(h, c1)], ["kid"] + tag_all("stg")[:h + 1]
            act(ga(nl), stg, T.kid[:, D:D + W].indirect(ou), AF.Copy, ("kid", oo), (N("stg"),))
            cp(S, both(T.u2), both(T.l2), (N("l2"),), (N("u2"),))
            oc, od = "outC%d_%d" % (t, h), "outD%d_%d" % (t, h)
            if True:
                for e, (out, nm) in enumerate(((T.outC[:, o:o + nl], oc), (T.outD[:, t, o % CT:o % CT + nl], od))):
                    ts(ga(nl), out, win.indirect(two(T.u2, e)), C(SCT + e), None, ALU.mult, None, wn + [N("u2"), "sct"], (nm,))
                a = min(o, ob)
                send(T.inC[:, a + CT:a + CT + CT // 2], [T.outC[:, a:a + CT // 2], T.outD[:, t, a % CT:a % CT + CT // 2]], "c%d_%d" % (t + 1, h), (oc, od, oo, "nought"), ("inC%d_%d" % (t + 1, h),))
            for e, nm in enumerate(("top", "cf")):
                act(ga(nl), T[nm][:, ls], win.indirect(two(T.u2, e)), AF.Copy, wn + [N("u2"), "sct"], (N(nm),), scale=C(SCT + e))
            if final:
                cp(cy(nl), T.inF[:, ls], T.inC[:, o + CT:o + CT + nl], ("inC%d_%d" % (t + 1, h),), (N("yf"),))
                dma("y", T.yn[:, ls], T.inF[:, ls], N("yn"), 512 * nl, r=(N("yf"),))
            lag[0] = LAGW * h
            if not JW:
                writers(c0, c1, [h], "pT")
        lag[0] = LAGJ
        if JW:
            writers(0, 16, range(NP), "pT")
        mounts(t)
        lag[0] = 0.0
        if not final:
            act(S, T.cov[:], T.ncd[:], AF.Sign, tag_all("ncd"), ("cov", "cs"), accum_out=T.cs[:])
            mm(256, T.pL[:, 0, 0:1], T.half[:], T.cs[:], True, True, ("half", "cs"), "pL", nm="cnt")
            cp(S, T.csi[:], T.pL[:, 0, 0:1], ("pL",), ("csi",))
            ts(S, T.csa[:], T.csi[:], 15, None, ALU.bitwise_and, None, ("csi",), ("csa",))
            ts(S, T.limA[:], T.csa[:], RS, RS * (LIM - 1), ALU.mult, ALU.add, ("csa",), ("limA",))
            ts(cy(68), T.limT[:], T.ob[:], T.limA[:], None, ALU.mult, None, ("ob", "limA"), ("limT",))
        for h, (c0, c1) in enumerate(PARTS):
            for c in range(c1 - 2, c0 - 2, -2):
                ns, off, r = (60 + 32 * SCAT) * CY, T.s2u[:, c:c + 2], ["s2u%d" % h, "top%d" % h, "cf%d" % h]
                tt(ns, T.kid[:, 0:D + W].indirect(off), T.top[:, 16 * c:16 * c + 32], T.cf[:, 16 * c:16 * c + 32], ALU.add, r, ("kid",))
    lag[1] = STEPS
    act(cy(256), T.mk16[:], T.M[:], AF.Copy, tag_all("M"), ("mk16",), scale=1.0 / KS, bias=192.0)
    ts(cy(128), T.klb[:], T.mk16[:], 192.0, None, ALU.subtract, None, ("mk16",), ("klb",))
    ts(cy(128), T.Y[:], T.mk16[:], 192.0, 1.0 / 64, ALU.subtract, ALU.mult, ("mk16",), ("Y",))
    mm(1024, T.pS[:, 0:8, :], T.INf[:], T.CJ2[:], True, False, ("INf", "CJ2"), "pS", nm="code")
    for x, (k, PM, src, r) in enumerate(((512, T.PF, T.M, ["PF"] + tag_all("M")), (128, T.PK, T.klb, ["PK", "klb"]), (128, T.PM, T.Y, ["PM", "Y"]))):
        for e in range(2):
            for s in range(2):
                out = T.pS[:, 8 * (x // 2):8 * (x // 2) + 8, 16 * s:16 * s + 16]
                mm(k, out, PM[:, 256 * s + 128 * e:256 * s + 128 * e + 128], src[:, :, 16 * e:16 * e + 16], False, x == 2 and e + s == 2, r, "pS", nm="turn%d" % x)
    for e in range(2):
        cp(cy(256), T.X[:, 8 * e:8 * e + 8, :], T.pS[:, 8 * e:8 * e + 8, :], ("pS",), ("X%d" % e,))
        tr(cy(128), T.XT[:, 8 * e:8 * e + 8, :], T.X[:, 8 * e:8 * e + 8, :], ("X%d" % e,), ("XT%d" % e,))
    for b in range(16):
        for e in range(2):
            mm(16, T.pS[:, 0:8, b::16], T.SH[:, 128 * (-b % 16):128 * (-b % 16) + 128], T.XT[:, 8 * e:8 * e + 8, b::16], e == 0, e == 1, ("SH", "XT0", "XT1"), "pS", part=True, nm="back")
    act(cy(256), T.ymo[:], T.pS[:, 0:8, :], AF.Copy, ("pS",), ("ymo",), scale=64.0, bias=131072.0)
    dma("s", T.ymu[:], T.ymo[:], "ymu", 131072, r=("ymo",))
    yb, n = ["pX0", "pX1", "pL", "pv0", "pv1", "pX2"], 0
    col = lambda i, x: T.kid[:, D + 512 * i + YQ[x]:D + 512 * i + YQ[x + 1]]
    acc = lambda x: T.acc[:, YQ[x]:YQ[x + 1]]
    for two in range(0, len(YQ) - 1, 2):
        for x in (two, two + 1):
            k = YQ[x + 1] - YQ[x]
            for i in range(8 - YP[x], 8):
                mm(4 * k, bank(yb[x % 2], k), T.FF[:, 128 * (7 - i):128 * (8 - i)], col(i, x), i == 8 - YP[x], i == 7, ("F", "kid"), yb[x % 2], nm="yd%d" % x)
        for i in range(1, 9):
            for x in [x for x in (two + 1, two) if i <= 8 - YP[x]]:
                k, ps = YQ[x + 1] - YQ[x], yb[2 + n % 4] if i < 8 - YP[x] else yb[x % 2]
                if i < 8 - YP[x]:
                    n += 1
                    act(cy(k), bank(ps, k), col(i, x), AF.Copy, ("kid",), (ps,), scale=float(i + 1))
                tt(cy(k), acc(x), col(0, x) if i == 1 else acc(x), bank(ps, k), ALU.add, ("kid" if i == 1 else "acc%d" % x, ps), ("acc%d" % x,))
        for x in (two, two + 1):
            dma("ys"[x % 2], T.yd[:, YQ[x]:YQ[x + 1]], acc(x), "yd%d" % x, 512 * (YQ[x + 1] - YQ[x]), r=("acc%d" % x,))
    emit(g, T, ops, order(ops))
